import numpy as np, ml_dtypes
CORES = [48,51,52,55]
N = 4
BF = ml_dtypes.bfloat16
def gentries(a):
    return np.ascontiguousarray(a.reshape(8, 16, -1).transpose(0, 2, 1)).reshape(8, -1)
def gtable(e):
    e = np.asarray(e); return np.ascontiguousarray(e.reshape(8, -1, 16).transpose(0, 2, 1)).reshape(128, -1).astype(np.int32)
W, H, L, CAP, RO = 2560, 1024, 256, 256, 4
def pick(t, e):
    return np.take_along_axis(t, e[:, None, :], 2)
def at(x, c):
    return pick(x, c.reshape(8, -1)).reshape(8, 16, 16, -1)
def moved(v, dl):
    return np.clip(v + dl[:, :, None, :], 0, 63)
def spot(u):
    return (((u * u) >> 5) + 37 * u) & (H - 1)
def parts(rng):
    x = rng.integers(0, 64, (N, 8, 16, W)); su = rng.integers(0, W, (N, 8, 16, W)); co = np.argsort(rng.random((N, 8, 16, W)), axis=-1)
    dl = rng.integers(-20, 21, (N, 8, 16, L)); la = rng.integers(0, W, (N, 8, L)); lb = rng.integers(0, W, (N, 8, L))
    wt = rng.integers(0, 256, (N, 8, 16)); th = 110 + 20 * np.argsort(rng.random((N, 8)), axis=-1) + rng.integers(0, 20, (N, 8))
    return x, su, co, dl, la, lb, wt, th
def pack(x, su, co, dl, la, lb, wt, th):
    fl = lambda a, n: np.ascontiguousarray(np.asarray(a).reshape(N, 128, n)).astype(np.float32).astype(BF)
    it = lambda a: np.ascontiguousarray(np.asarray(a).reshape(N, 128, W)).astype(np.int32)
    return {"x0": fl(x, W), "su": it(su), "co": it(co), "dl": fl(dl, L), "la": np.stack([gtable(a) for a in la]), "lb": np.stack([gtable(a) for a in lb]),
            "wt": fl(wt, 1), "th": np.asarray(th).reshape(N, 8, 1).astype(np.int32)}
def put(p, c, v):
    w = np.argmax(p == v[..., None], axis=-1); old = p[..., c].copy()
    np.put_along_axis(p, w[..., None], old[..., None], -1); p[..., c] = v
def two(rng, n):
    c = rng.integers(0, 3, (N, 8, 1, n)); return np.where(c < 2, c, rng.integers(0, 2, (N, 8, 16, n)))
def spots(dl, wt):
    return spot(np.sum(63 * wt[:, :, None] * (dl > 0), axis=1) & 4095)
def setup_inputs(rng):
    return pack(*parts(rng))
def setup_inputs_spread(rng):
    x, su, co, dl, la, lb, wt, th = parts(rng)
    p = np.exp2(rng.integers(-2, 3, (N, 8, 1, W))); x = np.minimum((64 * rng.random((N, 8, 16, W)) ** p).astype(np.int64), 63)
    p = np.exp2(rng.integers(-2, 3, (N, 8, 1, W))); su = np.minimum((W * rng.random((N, 8, 16, W)) ** p).astype(np.int64), W - 1)
    dl = np.rint((2 * rng.random((N, 8, 16, L)) - 1) * rng.choice(np.array([0, 1, 3, 9, 27, 63]), (N, 8, 1, L))).astype(np.int64)
    la = np.minimum((W * rng.random((N, 8, L)) ** 2).astype(np.int64), W - 1); lb = W - 1 - np.minimum((W * rng.random((N, 8, L)) ** 2).astype(np.int64), W - 1)
    wt = np.minimum(np.exp2(8 * rng.random((N, 8, 16))).astype(np.int64), 256) - 1
    th = np.where(rng.random((N, 8)) < 0.5, np.minimum(np.exp2(10 * rng.random((N, 8))).astype(np.int64), 1024) - 1, rng.integers(100, 300, (N, 8)))
    return pack(x, su, co, dl, la, lb, wt, th)
def setup_inputs_ends(rng):
    x, su, co, dl, la, lb, wt, th = parts(rng)
    x = 63 * two(rng, W); su = (W - 1) * two(rng, W); dl = 126 * two(rng, L) - 63
    la = (W - 1) * rng.integers(0, 2, (N, 8, L)); lb = (W - 1) * rng.integers(0, 2, (N, 8, L)); la[:, :, L - 1] = W - 1; lb[:, :, 0] = 0
    wt = 255 * rng.integers(0, 2, (N, 8, 16)); wt[:, 0] = 255 * (np.arange(16) & 1); wt[:, 7] = 255
    th = 1023 * rng.integers(0, 2, (N, 8)); th[:, 0] = 1023; th[:, 1] = 0; th[:, 7] = 0; th[0, 6] = 1023
    z = rng.integers(0, 2, (N, 8, 16)); z[:, :, 0] = 1; z[:, :, 15] = 0
    put(co, 0, (W - 1) * z); put(co, W - 1, (W - 1) * (1 - z))
    dl[:, 7] = np.where(rng.random((N, 1, L)) < 0.5, 63, -63); dl[:, 7, :, 0] = 63; dl[:, 7, :, 1] = -63; dl[:, 7, :, L - 1] = 63
    x[:, 7, :, 0] = 0; x[:, 7, :, W - 1] = 0; x[:, 7, :, spot((16 * 63 * 255) & 4095)] = 0
    x[:, 6, :, 0] = 63; x[:, 6, :, W - 1] = 63; dl[:, 6, :, 0] = -63; dl[:, 6, :, L - 1] = -63
    return pack(x, su, co, dl, la, lb, wt, th)
def setup_inputs_corners(rng):
    x, su, co, dl, la, lb, wt, th = parts(rng); th[:] = 0; dl = 126 * rng.integers(0, 2, (N, 8, 16, L)) - 63
    for r in range(N):
        own = spots(dl[r], wt[r]); come = spots(dl[r - 1], wt[r])
        for i in range(8):
            p = np.unique(own[i]); z = p[:0]
            if i % 2: z = p; p = np.setdiff1d(come[i], z)
            n = int(rng.choice(np.array([0, 1, CAP - 1, CAP, CAP + 1, W - H])))
            if r in (0, N - 1): n = (CAP, CAP, CAP + 1, CAP + 1, CAP - 1, CAP - 1, 0, 1)[i]
            if r == 1 and i in (2, 6): n = W - H
            n = min(n, 16 * len(p), W - H)
            a = np.concatenate([z, p]); s = np.stack([rng.permutation(H)[:len(a)] for k in range(16)])
            c = s[:, len(z):].copy().reshape(-1); c[rng.permutation(len(c))[:n]] = H + rng.permutation(W - H)[:n]
            s[:, len(z):] = c.reshape(16, -1)
            rest = np.ones(W, bool); rest[a] = False
            for k in range(16):
                free = np.ones(W, bool); free[s[k]] = False
                co[r, i, k, a] = s[k]; co[r, i, k, rest] = rng.permutation(np.flatnonzero(free))
    return pack(x, su, co, dl, la, lb, wt, th)
def setup_inputs_crowd(rng):
    x, su, co, dl, la, lb, wt, th = parts(rng)
    dl[:, :2] = 126 * rng.integers(0, 2, (N, 2, 16, L)) - 63
    for i in range(8):
        m = (1, 1, 2, 1, 4, 1, 2, 1)[i]; s = rng.integers(0, m, L); z = int(rng.integers(1, L - 1))
        if i % 2: s[z] = m
        la[:, i] = la[:, i][:, s]; lb[:, i] = lb[:, i][:, s]; dl[:, i] = dl[:, i][:, :, s]
    for r in range(N):
        n = spots(dl[r], wt[r])
        put(co[r, 0], int(n[0, 0]), np.full(16, W - 1)); put(co[r, 1], int(n[1, 0]), np.full(16, H))
        if r % 3 < 2: th[r] = 0
        if r % 3 == 0: dl[r, 5, :, L - 1] = 0; lb[r, 5, L - 1] = la[r, 5, L - 1]
        if r % 3 == 1: th[r, 3] = 1; dl[r, 3, :, L - 1] = 0; lb[r, 3, L - 1] = la[r, 3, L - 1]
    return pack(x, su, co, dl, la, lb, wt, th)
def setup_inputs_ties(rng):
    x, su, co, dl, la, lb, wt, th = parts(rng)
    x = 8 * (x >> 4); x[:, 1::2] = 63 - x[:, 1::2]; dl = 8 * rng.integers(-1, 2, (N, 8, 16, L))
    x[:, 3] = 63; x[:, 3, :7] = 62 + np.minimum(rng.integers(0, 4, (N, 7, W)), 1); dl[:, 3] = -63; dl[2, 3, :, 48:] = 0
    put(co[2, 3], 0, H + np.arange(16)); su[2, 3, :, H:H + 16] = H + ((np.arange(16) + 1) & 15)
    su[:, ::2, :, :W // 2] = su[:, ::2, :1, :W // 2].copy()
    la[:, :, 16:32] = la[:, :, :16].copy(); lb[:, :, 16:32] = lb[:, :, :16].copy(); dl[:, :, :, 16:32] = dl[:, :, :, :16].copy()
    lb[:, :, 32:48] = la[:, :, 32:48].copy(); dl[:, :, :, 32:48] = 0
    for r in range(N):
        dd = np.sum(np.abs(at(x[r], pick(co[r], lb[r])) - moved(at(x[r], pick(co[r], la[r])), dl[r])), axis=1)
        th[r] = np.sort(np.min(dd, axis=1), axis=1)[:, L // 2]; th[r, 4:] += rng.integers(0, 2, 4)
        if r == 2: th[r] = 1023; th[r, 3] = np.min(dd[3, :, :32])
    return pack(x, su, co, dl, la, lb, wt, th)
def check_inputs(d):
    bad = []
    for k, lo, hi in (("x0", 0, 63), ("su", 0, W - 1), ("co", 0, W - 1), ("dl", -63, 63), ("la", 0, W - 1), ("lb", 0, W - 1), ("wt", 0, 255), ("th", 0, 1023)):
        a = np.asarray(d[k]).astype(np.float64)
        if not (np.min(a) >= lo and np.max(a) <= hi): bad.append("range of " + k)
        if np.any(a != np.floor(a)): bad.append("whole numbers of " + k)
    if np.any(np.sort(np.asarray(d["co"]), axis=-1) != np.arange(W)): bad.append("a row of co holds every node once")
    return bad
def reference(x0, su, co, dl, la, lb, wt, th):
    x = x0.astype(np.float32).astype(np.int32).reshape(N, 8, 16, W); s = su.astype(np.int64).reshape(N, 8, 16, W); c = co.astype(np.int64).reshape(N, 8, 16, W)
    sh = dl.astype(np.float32).astype(np.int32).reshape(N, 8, 16, L); w = wt.astype(np.float32).astype(np.int32).reshape(N, 8, 16, 1, 1); lim = th.astype(np.int64).reshape(N, 8, 1)
    a = np.stack([gentries(v) for v in la]).astype(np.int64); b = np.stack([gentries(v) for v in lb]).astype(np.int64)
    flag = np.zeros((N, 8, W), bool); last = np.zeros(N, np.int64)
    for t in range(RO):
        for r in range(N):
            q = (r - t) % N
            d = pick(c[r], a[q]); f = pick(c[r], b[q])
            dist = np.sum(np.abs(at(x[r], f) - moved(at(x[r], d), sh[q])), axis=1)
            k = np.argmin(dist, axis=1)[:, None, :]
            dk = np.take_along_axis(d, k, 1)[:, 0]; fk = np.take_along_axis(f, k, 1)[:, 0]
            same = np.take_along_axis(dist, k, 1)[:, 0] < lim[r] + (last[r] & 63)
            e = moved(at(x[r], pick(s[r], dk)), sh[q])
            n = spot(np.sum(w[r] * e, axis=1).astype(np.int64) & 4095)
            j = np.argmax(np.sum(np.abs(at(x[r], n) - e), axis=1), axis=1)[:, None, :]
            nj = np.take_along_axis(n, j, 1)[:, 0]; ej = np.take_along_axis(e, j[:, None], 2)[:, :, 0]
            for i in range(8):
                lane = np.flatnonzero(~same[i]); place, first = np.unique(nj[i, lane], return_index=True)
                x[r, i][:, place] = ej[i][:, lane[first]]
                flag[r, i, c[r, i][:, place].reshape(-1)] = True; flag[r, i, :H] = False
                v = np.flatnonzero(flag[r, i])[:CAP]
                z = x[r, i][:, s[r, i][:, v]]
                x[r, i][:, v] = (np.max(z, axis=1) + np.min(z, axis=1)) >> 1
                flag[r, i, v] = False
            last[r] = np.sum(~same)
            a[q] = np.where(same, dk, a[q]); b[q] = np.where(same, fk, b[q])
    return {"yx": x.reshape(N, 128, W).astype(np.float32).astype(BF), "ya": np.stack([gtable(a[(r - RO + 1) % N]) for r in range(N)]).astype(np.float32),
            "yb": np.stack([gtable(b[(r - RO + 1) % N]) for r in range(N)]).astype(np.float32)}

@@ -1,0 +1,467 @@
+from concourse.mybir import AluOpType as OP, AxisListType, ActivationFunctionType as AF
+
+R = 4
+SCRATCH = {}
+for _n, _w, _t in [
+        ("Xw", 2816, "bfloat16"), ("coI", 2560, "int32"), ("coH", 2560, "bfloat16"), ("coF", 2688, "float32"),
+        ("suI", 2816, "int32"), ("sh0", 4096, "bfloat16"), ("sh1", 4096, "bfloat16"), ("dls", 1024, "bfloat16"),
+        ("M", 4096, "bfloat16"), ("E", 4096, "bfloat16"), ("z", 4096, "bfloat16"), ("az", 4096, "bfloat16"), ("gF", 4096, "bfloat16"),
+        ("Fv", 2688, "bfloat16"), ("Fs0", 2688, "float32"), ("Fs1", 2688, "float32"), ("FsB0", 1536, "bfloat16"), ("FsB1", 1536, "bfloat16"),
+        ("Vw0", 3072, "float32"), ("Vw1", 3072, "float32"), ("iotaV", 1536, "float32"),
+        ("ident", 128, "bfloat16"), ("nident", 128, "bfloat16"), ("nid32", 128, "bfloat16"), ("nid4k", 128, "bfloat16"), ("idBig", 128, "bfloat16"),
+        ("c4k", 96, "bfloat16"), ("dmI", 128, "float32"), ("ta", 32, "float32"), ("identF", 128, "float32"), ("grp", 128, "bfloat16"), ("grpF", 128, "float32"),
+        ("onesF", 128, "float32"), ("onesB", 128, "bfloat16"), ("ntri", 128, "bfloat16"), ("selX", 2048, "bfloat16"), ("WT", 2048, "bfloat16"),
+        ("g8", 8, "float32"), ("g8s", 24, "float32"), ("g8p", 48, "bfloat16"), ("cK", 640, "bfloat16"),
+        ("jm", 1024, "float32"), ("segN", 512, "float32"), ("segX", 128, "float32"), ("seg1", 256, "float32"), ("rN", 512, "bfloat16"), ("rX", 512, "bfloat16"),
+        ("dm", 640, "float32"), ("ltm", 128, "bfloat16"), ("pI", 8, "int32"), ("pT", 32, "int32"), ("pF", 8, "float32"),
+        ("eI", 64, "int32"), ("LE", 40, "uint16"), ("LX", 8, "uint16"), ("LP", 8, "uint16"), ("Ld1", 96, "float32"),
+        ("idx", 8, "float32"), ("EB", 8, "float32"), ("one96", 96, "bfloat16"),
+        ("stv", 512, "bfloat16"), ("sts", 512, "float32"), ("wt_", 8, "bfloat16"), ("wtF", 8, "float32"), ("thI", 8, "int32"), ("thF", 8, "float32"),
+        ("thr", 8, "float32"), ("th16", 8, "float32"), ("gT", 128, "float32"), ("laI", 16, "int32"), ("lbI", 16, "int32"),
+        ("abI", 32, "float32"), ("land", 128, "float32"), ("abo", 128, "float32"), ("abU", 32, "uint16"),
+        ("al", 16, "float32"), ("acc", 8, "float32"), ("acJ", 16, "int32"),
+        ("df", 512, "uint16"), ("dfH", 512, "bfloat16"), ("dfF", 512, "float32"),
+        ("Fp", 96, "bfloat16"), ("Fc", 96, "bfloat16"), ("Fi", 96, "bfloat16"), ("t96", 96, "float32"), ("s96", 96, "float32"), ("Lv", 96, "uint16"),
+        ("vX", 256, "float32"), ("vS", 256, "float32"), ("vL", 16, "uint16"), ("sR", 256, "uint16"), ("rs", 256, "float32"), ("rI", 256, "int32")]:
+    SCRATCH[_n] = ("sbuf", [128, _w], _t)
+HALF = {}
+for _n, _w, _t in [("S", 640, "float32"), ("B", 640, "float32"), ("dL", 8, "uint16"), ("sT", 128, "uint16"),
+                   ("uI", 128, "int32"), ("uA", 128, "int32"), ("uB", 128, "int32"), ("nO", 128, "uint16"), ("nP", 128, "float32"),
+                   ("vI", 8, "int32"), ("nI", 8, "int32"), ("jI", 8, "int32"), ("eO", 8, "uint16"), ("nS", 8, "float32"), ("nt", 8, "float32"), ("nl", 8, "float32"),
+                   ("nBs", 128, "float32"), ("EQ", 1024, "bfloat16"), ("oU", 8, "uint16"), ("oD", 16, "uint16"), ("T1", 256, "float32"),
+                   ("T2", 256, "float32"), ("fL", 128, "uint16"), ("eS", 128, "bfloat16")]:
+    SCRATCH[_n] = ("sbuf", [128, 2 * _w], _t)
+    HALF[_n] = _w
+for _b in range(8):
+    SCRATCH["P%d" % _b] = ("psum", [128, 512], "float32")
+
+LOADS = ["la", "lb", "dl", "co0", "co1", "x0", "x1", "su0", "su1", "wt", "th"]
+SEMAPHORES = ["sv", "ss", "sp", "sg", "ls", "so"] + ["ld_" + n for n in LOADS] + ["rdl%d" % t for t in (1, 2, 3)] + ["rab%d" % t for t in (1, 2, 3)]
+
+CY, WAKE, LAM, GA, SC = 0.83e-3, 0.1, 0.0, 1.5, 3.5
+SPATH = {1: ((1, 3), (1, 2, 3)), 2: ((1, 3), (1, 3))}
+MPATH = {1: ((1, 3), (3,)), 2: ((), (3,))}
+FLAG_S = (tuple(range(10)), tuple(range(5)))
+REN_S = (1, 2, 3, 4, 5, 6, 7)
+ORDER = {}
+
+
+def schedule(ops):
+    n = len(ops)
+    succ = [[] for _ in ops]
+    for i, o in enumerate(ops):
+        for d in o["deps"]:
+            succ[d].append(i)
+    pri = [0.0] * n
+    for i in range(n - 1, -1, -1):
+        pri[i] = ops[i]["c"] + max([pri[s] + WAKE for s in succ[i]], default=0.0)
+    need = [len(o["deps"]) for o in ops]
+    early, start, free, out = [0.0] * n, [0.0] * n, {}, []
+    ready = {i for i in range(n) if need[i] == 0}
+    while ready:
+        best = {}
+        for i in ready:
+            e = ops[i]["e"]
+            best[e] = min(best.get(e, 1e18), max(early[i], free.get(e, 0.0)))
+        e = min(best, key=lambda q: (best[q], q))
+        i = max((j for j in ready if ops[j]["e"] == e and max(early[j], free.get(e, 0.0)) <= best[e] + 0.02), key=lambda j: (pri[j] - LAM * j, -j))
+        s = start[i] = max(early[i], free.get(e, 0.0))
+        free[e] = s + (0.05 if ops[i]["async"] else ops[i]["c"])
+        ready.discard(i)
+        out.append(i)
+        for j in succ[i]:
+            early[j] = max(early[j], s + ops[i]["c"] + WAKE)
+            need[j] -= 1
+            if need[j] == 0:
+                ready.add(j)
+    return out, start, max(start[i] + ops[i]["c"] for i in range(n))
+
+
+def rank_program(g, core, T, topo):
+    rank = T.rank_of(core)
+    if rank is None:
+        return
+    N = len(T.cores)
+    V, S, PE = g.vector, g.scalar, g.tensor
+    ops, lastw, readers = [], {}, {}
+
+    def op(e, c, r, w, fs, sem=None, val=None, isasync=False, order=()):
+        i = len(ops)
+        deps, soft = {lastw[t] for t in r if t in lastw}, set(order)
+        for t in w:
+            if t in lastw:
+                (soft if t[0] == "P" and ops[lastw[t]]["e"] == e else deps).add(lastw[t])
+            deps.update(readers.get(t, ()))
+        for t in r:
+            readers.setdefault(t, []).append(i)
+        for t in w:
+            lastw[t] = i
+            readers[t] = []
+        deps.discard(i)
+        ops.append({"e": e, "c": c, "hard": sorted(deps), "deps": sorted(deps | soft), "f": fs, "sem": sem, "val": val, "async": isasync})
+        return i
+
+    esem = {"V": "sv", "S": "ss", "PE": "sp", "G": "sg"}
+    vop = lambda n, r, w, f, cy=1.0: op("V", 0.055 + max(n * cy, 64) * CY, r, w, [f])
+    sop = lambda n, r, w, f, cy=1.0: op("S", 0.07 + max(n * cy, 64) * CY, r, w, [f])
+    vg = lambda n, r, w, f: vop(n, r, w, f, GA)
+    sg = lambda n, r, w, f: sop(n, r, w, f, GA)
+    pop = lambda cyc, r, w, fs: op("PE", cyc * CY, r, w, fs)
+    gop = lambda n, r, w, f: op("G", 0.17 + 2 * n * CY, r, w, [f])
+    load = lambda q, name, c, w, out, in_: op(q, c, [], w, [lambda: (g.sync if q == "Y" else S).dma_start(out, in_)], "ld_" + name, 16, True)
+
+    def ts(out, a, s1, s2, o0, o1=None):
+        return (lambda: V.tensor_scalar(out, a, s1, s2, o0)) if o1 is None else (lambda: V.tensor_scalar(out, a, s1, s2, o0, o1))
+
+    tt = lambda out, a, b, o: (lambda: V.tensor_tensor(out, a, b, o))
+    cp = lambda out, a: (lambda: V.tensor_copy(out, a))
+    fill = lambda out, c: (lambda: V.memset(out, c))
+    act = lambda out, a, f, **k: (lambda: S.activation(out, a, f, **k))
+    mm = lambda out, l, r, a, b: (lambda: PE.matmul(out, l, r, a, b))
+    scan = lambda out, a, b, i, o0, o1: (lambda: V.tensor_tensor_scan(out, a, b, i, o0, o1))
+    iof = lambda out, pat, base: (lambda: g.iota(out, pat, base, 0, allow_small_or_imprecise_dtypes=True))
+    ioi = lambda out, pat, base, cm: (lambda: g.iota(out, pat, base, cm))
+    sel = lambda out, a, pat, o, base, cm: (lambda: g.affine_select(out, a, pat, o, 0.0, base, cm))
+    turn = [0]
+
+    def bank():
+        turn[0] += 1
+        return 5 + turn[0] % 3
+
+    load("Y", "la", 2, ["laI"], T.laI[:], T.la[:])
+    load("Y", "lb", 2, ["lbI"], T.lbI[:], T.lb[:])
+    load("S", "dl", 2.5, ["dl0"], T.dls[:, 0:256], T.dl[:])
+    load("Y", "co0", 6, ["co0"], T.coI[:, 0:1280], T.co[:, 0:1280])
+    load("S", "co1", 6, ["co1"], T.coI[:, 1280:2560], T.co[:, 1280:2560])
+    load("Y", "x0", 8, ["X", "Xa"], T.Xw[:, 0:1280], T.x0[:, 0:1280])
+    load("S", "x1", 8, ["Xb"], T.Xw[:, 1280:2560], T.x0[:, 1280:2560])
+    load("Y", "wt", 3, ["wt"], T.wt_[:, 0:1], T.wt[:])
+    load("Y", "th", 3, ["thI"], T.thI[0:8, 0:1], T.th[:])
+    load("Y", "su0", 12, ["su0"], T.suI[:, 0:1280], T.su[:, 0:1280])
+    load("Y", "su1", 12, ["su1"], T.suI[:, 1280:2560], T.su[:, 1280:2560])
+    co_t, su_t, x_t = ["co0", "co1"], ["su0", "su1", "su2"], ["X", "Xa", "Xb"]
+
+    gop(1, [], ["pI"], ioi(T.pI[:, 0:1], [[0, 1]], 0, 1))
+    gop(256, [], ["jm"], iof(T.jm[:], [[0, 64], [1, 16]], 0))
+    vop(1, ["pI"], ["pT"], ts(T.pT[:, 0:1], T.pI[:, 0:1], 15, None, OP.bitwise_and))
+    vop(1, ["pT"], ["pF"], cp(T.pF[:, 0:1], T.pT[:, 0:1]))
+    vop(640, ["jm", "pF"], ["dm"], ts(T.dm[:], T.jm[:, 0:640], T.pF[:, 0:1], None, OP.is_equal))
+    vop(512, ["jm"], ["segN"], ts(T.segN[:], T.jm[:, 0:512], 0.0, 1e9, OP.is_equal, OP.mult))
+    gop(40, [], ["eI"], ioi(T.eI[:, 0:40], [[16, 40]], 15, 0))
+    vop(40, ["eI"], ["LE"], cp(T.LE[:], T.eI[:, 0:40]))
+    vop(128, [], ["onesB"], fill(T.onesB[:], 1.0))
+    vop(128, [], ["onesF"], fill(T.onesF[:], 1.0))
+    gop(128, ["onesB"], ["ident"], sel(T.ident[:], T.onesB[:], [[-1, 128]], OP.is_equal, 0, 1))
+    for nm, c in (("nident", -1.0), ("nid32", -32.0), ("nid4k", -4096.0), ("idBig", 1048576.0)):
+        vop(128, ["ident"], [nm], ts(T[nm][:], T.ident[:], c, None, OP.mult))
+    vop(96, [], ["c4k"], fill(T.c4k[:], 4096.0))
+    gop(128, [], ["dmI"], iof(T.dmI[:], [[1, 128]], 2560))
+    vop(128, ["dmI", "dm"], ["dmI"], tt(T.dmI[:], T.dmI[:], T.dm[:, 0:128], OP.mult), 2)
+    gop(8, ["onesF"], ["g8"], sel(T.g8[:], T.onesF[:, 0:8], [[-16, 8]], OP.is_ge, 0, 1))
+    gop(8, ["g8"], ["g8"], sel(T.g8[:], T.g8[:], [[16, 8]], OP.is_ge, 15, -1))
+    for i, s in enumerate((2048.0, 512.0, 16.0, 2048.0, 512.0, 16384.0)):
+        vop(8, ["g8"], ["g8p"], ts(T.g8p[:, 8 * i:8 * i + 8], T.g8[:], s, None, OP.mult))
+    for i, s in enumerate((32.0, -4128.0, 1.0)):
+        vop(8, ["g8"], ["g8s"], ts(T.g8s[:, 8 * i:8 * i + 8], T.g8[:], s, None, OP.mult))
+    for i, (s, v) in enumerate(((128, -160), (32, 5120), (1, 0), (128, -160), (32, 5120))):
+        gop(128, [], ["cK"], iof(T.cK[:, 128 * i:128 * i + 128], [[0, 8], [s, 16]], v))
+    gop(128, ["onesF"], ["grpF"], sel(T.grpF[:], T.onesF[:], [[-16, 8], [0, 16]], OP.is_ge, 0, 1))
+    gop(128, ["grpF"], ["grpF"], sel(T.grpF[:], T.grpF[:], [[16, 8], [0, 16]], OP.is_ge, 15, -1))
+    vop(128, ["grpF"], ["grp"], cp(T.grp[:], T.grpF[:]))
+    gop(128, ["onesF"], ["gT"], sel(T.gT[:], T.onesF[:], [[1, 8], [0, 16]], OP.is_equal, 0, -1))
+    gop(128, ["onesF"], ["identF"], sel(T.identF[:], T.onesF[:], [[-1, 128]], OP.is_equal, 0, 1))
+    vop(1, ["thI"], ["thF"], cp(T.thF[0:8, 0:1], T.thI[0:8, 0:1]))
+    pop(256, ["gT", "thF"], ["P7"], [mm(T.P7[:, 0:1], T.gT[0:8, :], T.thF[0:8, 0:1], True, True)])
+    vop(1, [], ["th16", "P7"], ts(T.th16[:, 0:1], T.P7[:, 0:1], 16.0, None, OP.mult))
+    vop(1, ["th16"], ["thr"], cp(T.thr[:, 0:1], T.th16[:, 0:1]))
+    for j in range(16):
+        gop(128, ["grp"], ["selX"], sel(T.selX[:, 128 * j:128 * j + 128], T.grp[:], [[0, 8], [1, 16]], OP.is_equal, -j, 0))
+    vop(1, ["wt"], ["wtF"], cp(T.wtF[:, 0:1], T.wt_[:, 0:1]))
+    vop(2048, ["selX", "wtF"], ["WT"], ts(T.WT[:], T.selX[:], T.wtF[:, 0:1], None, OP.mult), 0.5)
+    vop(128, ["jm"], ["segX"], ts(T.segX[:], T.jm[:, 0:128], 0.0, 1e9, OP.is_gt, OP.mult))
+    vop(256, ["jm"], ["seg1"], ts(T.seg1[:], T.jm[:, 0:256], 0.0, None, OP.is_gt))
+    vop(512, ["jm"], ["rN"], ts(T.rN[:], T.jm[:, 0:512], 0.0, 64.0, OP.is_equal, OP.mult))
+    vop(512, ["jm"], ["rX"], ts(T.rX[:], T.jm[:, 0:512], 0.0, 64.0, OP.is_gt, OP.mult))
+    vop(128, ["jm", "pF"], ["ltm"], ts(T.ltm[:], T.jm[:, 0:128], T.pF[:, 0:1], None, OP.is_gt))
+    vop(96, [], ["one96"], fill(T.one96[:], 1.0))
+    vop(96, [], ["Fc"], fill(T.Fc[:], 0.0))
+    vop(2688, [], ["Fv"], fill(T.Fv[:], 0.0), 0.5)
+    for h in (0, 1):
+        gop(2688, [], ["Fs%d" % h], iof(T["Fs%d" % h][:], [[0, 2688]], 0))
+    vop(256, [], ["su2"], fill(T.suI[:, 2560:2816], 0))
+    gop(128, [], ["coF2"], iof(T.coF[:, 2560:2688], [[1, 128]], 2560))
+    gop(1536, [], ["iotaV"], iof(T.iotaV[:], [[1, 1536]], 1024))
+    sop(1536, ["iotaV"], ["iotaV"], act(T.iotaV[:], T.iotaV[:], AF.Identity, bias=0.25))
+    gop(8, [], ["eI2"], ioi(T.eI[:, 48:56], [[1, 8]], 0, 0))
+    vop(8, ["eI2"], ["LX"], cp(T.LX[:], T.eI[:, 48:56]))
+    gop(8, [], ["idx"], iof(T.idx[:], [[16, 8]], 2560))
+    vop(8, ["pF", "idx"], ["idx"], ts(T.idx[:], T.idx[:], T.pF[:, 0:1], None, OP.add))
+    gop(96, [], ["Ld1"], iof(T.Ld1[:], [[16, 96]], 1537))
+    vop(96, ["pF", "Ld1"], ["Ld1"], ts(T.Ld1[:], T.Ld1[:], T.pF[:, 0:1], None, OP.add))
+    vop(1, ["pF"], ["pF2"], ts(T.pF[:, 1:2], T.pF[:, 0:1], 16.0, None, OP.mult))
+    vop(1, ["pF"], ["pFn"], ts(T.pF[:, 6:7], T.pF[:, 0:1], -1024.0, 15360.0, OP.mult, OP.add))
+    gop(8, [], ["EB"], iof(T.EB[:], [[256, 8]], 15))
+    vop(8, ["pF2", "EB"], ["EB"], ts(T.EB[:], T.EB[:], T.pF[:, 1:2], None, OP.add))
+    vop(1, ["pI"], ["pT1"], ts(T.pT[:, 8:9], T.pI[:, 0:1], 7, None, OP.bitwise_and))
+    vop(1, ["pI"], ["pT2"], ts(T.pT[:, 16:17], T.pI[:, 0:1], 16, None, OP.bitwise_and))
+    vop(1, ["pI"], ["pT3"], ts(T.pT[:, 24:25], T.pI[:, 0:1], 3, 1, OP.logical_shift_right, OP.bitwise_and))
+    vop(1, ["pT2"], ["pF3"], cp(T.pF[:, 3:4], T.pT[:, 16:17]))
+    vop(1, ["pT1", "pF3"], ["pF4"], ts(T.pF[:, 4:5], T.pT[:, 8:9], 32.0, T.pF[:, 3:4], OP.mult, OP.add))
+    vop(1, ["pT3", "pF4"], ["pF5"], tt(T.pF[:, 5:6], T.pT[:, 24:25], T.pF[:, 4:5], OP.add))
+    gop(8, [], ["eI3"], ioi(T.eI[:, 56:64], [[2, 8]], 0, 0))
+    vop(8, ["eI3", "pF5"], ["LP"], ts(T.LP[:], T.eI[:, 56:64], T.pF[:, 5:6], None, OP.add))
+    gop(128, ["onesB"], ["ntri"], sel(T.ntri[:], T.onesB[:], [[-1, 128]], OP.is_gt, 0, 1))
+    vop(128, ["ntri", "grp"], ["ntri"], tt(T.ntri[:], T.ntri[:], T.grp[:], OP.mult))
+    vop(128, ["ntri"], ["ntri"], ts(T.ntri[:], T.ntri[:], -1.0, None, OP.mult))
+    for t in range(R):
+        vop(128, [], ["stv%d" % t], fill(T.stv[:, 128 * t:128 * t + 128], float(32 * 8 ** t)))
+        vop(128, [], ["sts%d" % t], fill(T.sts[:, 128 * t:128 * t + 128], float(32 * 8 ** t)))
+    for x in (0, 1):
+        vop(1280, ["co%d" % x], ["coF%d" % x], cp(T.coF[:, 1280 * x:1280 * x + 1280], T.coI[:, 1280 * x:1280 * x + 1280]))
+        sop(1280, ["coF%d" % x], ["coH%d" % x], act(T.coH[:, 1280 * x:1280 * x + 1280], T.coF[:, 1280 * x:1280 * x + 1280], AF.Identity, scale=0.03125, bias=159.515625))
+
+    def send(dst_rank, out, in_, sem, r):
+        dst = T.cores[dst_rank]
+        rid, pid, _ = topo.addr(dst)
+        m = sum(1 << e for e in topo.engines(core, dst)[:4])
+        return op("G", 0.6, r, [], [lambda: g.remote_dma(out, in_, T.sem[sem], T.sem.ls, pid, rid, m)], "none", 0)
+
+    for t in (1, 2, 3):
+        i = send((rank + t) % N, T.dls[:, 256 * t:256 * t + 256], T.dls[:, 0:256], "rdl%d" % t, ["dl0"])
+        op("R", 4.0, [], ["dl%d" % t], [], "rdl%d" % t, 4, True, order=[i])
+    for k in range(16):
+        if k % 2:
+            vop(256, ["dl0"], ["sh0_%d" % k], cp(T.sh0[:, k::16], T.dls[:, 0:256]), 0.5)
+        else:
+            sop(256, ["dl0"], ["sh0_%d" % k], act(T.sh0[:, k::16], T.dls[:, 0:256], AF.Copy))
+    hs = (0, 1)
+    for q, nm in enumerate(("laI", "lbI")):
+        vop(16, [nm], ["abI%d" % q], cp(T.abI[:, 16 * q:16 * q + 16], T[nm][:]))
+    cur, co_, cur_t = T.abI, 0, ["abI0", "abI1"]
+
+    for t in range(R):
+        sh = T.sh0 if t % 2 == 0 else T.sh1
+        sht = ["sh%d_%d" % (t % 2, k) for k in range(16)]
+        if t:
+            for k in range(16):
+                gop(256, ["dl%d" % t], [sht[k]], sel(sh[:, k::16], T.dls[:, 256 * t:256 * t + 256], [[0, 256]], OP.is_ge, 1, 0))
+        no = 32 * t
+        vop(32, cur_t, ["abU"], cp(T.abU[:], cur[:, co_:co_ + 32]))
+        vg(512, ["abU"] + co_t, ["df"], cp(T.df[:], T.coI[:].indirect(T.abU[:])))
+        for nm in ("H", "F"):
+            sg(512, ["abU", "co%s0" % nm, "co%s1" % nm], ["df" + nm], act(T["df" + nm][:], T["co" + nm][:, 0:2560].indirect(T.abU[:]), AF.Copy))
+
+        def second(step, h, q, lists, lo, Mb, mt, lt):
+            a, zt = 2048 * h + 512 * q, "z%d%d" % (h, q)
+            win = T.Xw[:, 0:2560].indirect(lists[:, lo + 32 * q:lo + 32 * q + 32])
+            if q in SPATH[step][h]:
+                gt, P = "gF%d%d" % (h, q), "P%d" % bank()
+                sg(512, x_t + [lt], [gt], act(T.gF[:, a:a + 512], win, AF.Copy))
+                pop(1024, ["ident", "nident", gt, mt], [P], [mm(T[P][:], T.nident[:], Mb[:, a:a + 512], True, False), mm(T[P][:], T.ident[:], T.gF[:, a:a + 512], False, True)])
+                sop(512, [], [P, "a" + zt], act(T.az[:, a:a + 512], T[P][:], AF.Abs))
+            else:
+                vg(512, x_t + [lt, mt], [zt], tt(T.z[:, a:a + 512], win, Mb[:, a:a + 512], OP.subtract))
+                sop(512, [zt], ["a" + zt], act(T.az[:, a:a + 512], T.z[:, a:a + 512], AF.Abs))
+
+        def moved(step, h, q, lists, lo, lt, Mb, mt):
+            a = 2048 * h + 512 * q
+            win = T.Xw[:, 0:2560].indirect(lists[:, lo + 32 * q:lo + 32 * q + 32])
+            if q in MPATH[step][h]:
+                gt, P = "gF%d%d" % (h, q), "P%d" % bank()
+                sg(512, x_t + [lt], [gt], act(T.gF[:, a:a + 512], win, AF.Copy))
+                pop(1024, ["ident", gt] + sht, [P], [mm(T[P][:], T.ident[:], sh[:, a:a + 512], True, False), mm(T[P][:], T.ident[:], T.gF[:, a:a + 512], False, True)])
+                vop(512, [], [P, mt], ts(Mb[:, a:a + 512], T[P][:], 0.0, 63.0, OP.max, OP.min))
+                return
+            vg(512, x_t + [lt] + sht, [mt], tt(Mb[:, a:a + 512], win, sh[:, a:a + 512], OP.add))
+            vop(512, [mt], [mt], ts(Mb[:, a:a + 512], Mb[:, a:a + 512], 0.0, 63.0, OP.max, OP.min), 0.5)
+
+        for h in hs:
+            X = lambda n, a=0, b=None, s=1, h=h: T[n][:, h * HALF[n] + a:h * HALF[n] + (HALF[n] if b is None else b):s]
+            K = lambda n, h=h: "%s_%d" % (n, h)
+            b, a0 = 128 * h, 2048 * h
+            for q in range(4):
+                moved(1, h, q, T.df, b, "df", T.M, "M%d%d" % (h, q))
+            for q in range(4):
+                second(1, h, q, T.df, b + 256, T.M, "M%d%d" % (h, q), "df")
+            azt = ["az%d%d" % (h, q) for q in range(4)]
+            for P, w, c0, d in (("P0", 384, 0, b), ("P1", 256, 384, b + 256)):
+                lh, lf = T.dfH[:, d:d + 128], T.dfF[:, d:d + 128]
+                pop(w + 768, ["ident", "identF", "nid32", "cK", "dfH", "dfF"], [P], [
+                    mm(T[P][:, 0:w], T.ident[:], T.cK[:, c0:c0 + w], True, False), mm(T[P][:, 0:128], lh, T.ident[:], False, False),
+                    mm(T[P][:, 128:256], lf, T.identF[:], False, False), mm(T[P][:, 128:256], lh, T.nid32[:], False, False)])
+            l = [T.az[:, a0 + k:a0 + 2048:16] for k in range(16)]
+            pop(1024, azt + ["g8p"], ["P0"], [mm(T.P0[:, k:384:16], l[k], T.g8p[:, 0:24], False, k == 15) for k in range(16)])
+            pop(1024, azt + ["g8p"], ["P1"], [mm(T.P1[:, k:256:16], l[k], T.g8p[:, 24:40], False, k == 15) for k in range(16)])
+            vop(384, ["segN"], [K("S") + "a", "P0"], scan(X("S", 0, 384), T.segN[:, 0:384], T.P0[:, 0:384], 1e9, OP.max, OP.min))
+            vg(384, [K("S") + "a", "LE", "dm"], [K("B")], tt(X("B", 0, 384), X("S", 0, 384).indirect(T.LE[:, 0:24]), T.dm[:, 0:384], OP.mult))
+            vop(256, ["segN"], [K("S") + "b", "P1"], scan(X("S", 384), T.segN[:, 0:256], T.P1[:, 0:256], 1e9, OP.max, OP.min))
+            vg(256, [K("S") + "b", "LE", "dm"], [K("B") + "b"], tt(X("B", 384), X("S", 384).indirect(T.LE[:, 0:16]), T.dm[:, 0:256], OP.mult))
+            c32, c41, c1 = T.g8s[:, 0:8], T.g8s[:, 8:16], T.g8s[:, 16:24]
+            blk = [X("B", 128 * i, 128 * i + 128) for i in range(5)]
+            pd, pf, pk = T.P2[:, 8 * h:8 * h + 8], T.P3[:, 8 * h:8 * h + 8], T.P3[:, 16 + 8 * h:24 + 8 * h]
+            pop(768, [K("B"), "g8s"], ["P2"], [mm(pd, blk[0], c32, True, False), mm(pd, blk[2], c41, False, False), mm(pd, blk[1], c1, False, True)])
+            pop(1024, [K("B"), K("B") + "b", "g8s"], ["P3"], [mm(pf, blk[3], c32, True, False), mm(pf, blk[2], c41, False, False), mm(pf, blk[4], c1, False, True), mm(pk, blk[2], c1, True, True)])
+            vop(8, [], [K("dL"), "P2"], cp(X("dL"), pd))
+        vop(16, ["thr"], ["al", "P3"], ts(T.al[:], T.P3[:, 16:32], T.thr[:, 0:1], None, OP.is_lt))
+        for q, P in ((0, "P2"), (1, "P3")):
+            tq = T.ta[:, 16 * q:16 * q + 16]
+            vop(16, cur_t, ["ta%d" % q, P], tt(tq, T[P][:, 0:16], cur[:, co_ + 16 * q:co_ + 16 * q + 16], OP.subtract))
+            vop(16, ["ta%d" % q, "al"], ["ta%d" % q], tt(tq, tq, T.al[:], OP.mult))
+        vop(32, ["ta0", "ta1"] + cur_t, ["abo%d" % t], tt(T.abo[:, no:no + 32], T.ta[:], cur[:, co_:co_ + 32], OP.add))
+        if t < R - 1:
+            i = send((rank + 1) % N, T.land[:, no:no + 32], T.abo[:, no:no + 32], "rab%d" % (t + 1), ["abo%d" % t])
+            op("R", 4.0, [], ["land%d" % (t + 1)], [], "rab%d" % (t + 1), 4, True, order=[i])
+            vop(16, ["al"], ["acc"], lambda: V.tensor_reduce(T.acc[:, 0:1], T.al[:], AxisListType.X, OP.add))
+            pop(256, ["acc", "onesF"], ["P3"], [mm(T.P3[:, 32:33], T.onesF[:], T.acc[:, 0:1], True, True)])
+            vop(1, [], ["acI", "P3"], ts(T.acJ[:, 0:1], T.P3[:, 32:33], -1.0, 2048.0, OP.mult, OP.add))
+            vop(1, ["acI"], ["acJ"], ts(T.acJ[:, 8:9], T.acJ[:, 0:1], 63, None, OP.bitwise_and))
+            vop(1, ["acJ", "th16"], ["thr"], ts(T.thr[:, 0:1], T.acJ[:, 8:9], 16.0, T.th16[:, 0:1], OP.mult, OP.add))
+        else:
+            for q, y in enumerate((T.ya, T.yb)):
+                u = no + 16 * q
+                op("Y", 2.0, ["abo%d" % t], [], [lambda y=y, u=u: g.sync.dma_start(y[:], T.abo[:, u:u + 16])], "so", 16, True)
+
+        for h in hs:
+            X = lambda n, a=0, b=None, s=1, h=h: T[n][:, h * HALF[n] + a:h * HALF[n] + (HALF[n] if b is None else b):s]
+            K = lambda n, h=h: "%s_%d" % (n, h)
+            a0 = 2048 * h
+            vg(128, [K("dL")] + su_t[:2], [K("sT")], cp(X("sT"), T.suI[:, 0:2560].indirect(X("dL"))))
+            for q in range(4):
+                moved(2, h, q, T.sT, 128 * h, K("sT"), T.E, "E%d%d" % (h, q))
+            et, azt = ["E%d%d" % (h, q) for q in range(4)], ["az%d%d" % (h, q) for q in range(4)]
+            for x in (0, 1):
+                pop(1024, et[2 * x:2 * x + 2] + ["WT"], ["P4"], [mm(T.P4[:, 64 * x:64 * x + 64], T.WT[:, 128 * j:128 * j + 128], T.E[:, a0 + 1024 * x + j:a0 + 1024 * x + 1024:16], j == 0, j == 15) for j in range(16)])
+            vop(128, [], [K("uI"), "P4"], cp(X("uI"), T.P4[:, 0:128]))
+            vop(128, [K("uI")], [K("uI")], ts(X("uI"), X("uI"), 4095, None, OP.bitwise_and))
+            vop(128, [K("uI")], [K("uA")], ts(X("uA"), X("uI"), -2048.0, None, OP.add))
+            vop(128, [K("uI")], [K("uB")], ts(X("uB"), X("uI"), 3232.0, None, OP.add))
+            vop(128, [K("uA"), K("uB")], [K("uA")], tt(X("uA"), X("uA"), X("uB"), OP.mult), 2)
+            vop(128, [K("uA")], [K("uI")], ts(X("uI"), X("uA"), 5, 1023, OP.arith_shift_right, OP.bitwise_and))
+            vop(128, [K("uI")], [K("nO")], cp(X("nO"), X("uI")))
+            vop(128, [K("uI"), "pFn"], [K("nP")], ts(X("nP"), X("uI"), T.pF[:, 6:7], None, OP.add))
+            for q in range(4):
+                second(2, h, q, T.nO, 128 * h, T.E, "E%d%d" % (h, q), K("nO"))
+            pop(512, [K("nP"), "identF"], ["P1"], [mm(T.P1[:, 256:384], X("nP"), T.identF[:], True, False)])
+            pop(1024, azt + ["g8p"], ["P1"], [mm(T.P1[:, 256 + j:384:16], T.az[:, a0 + j:a0 + 2048:16], T.g8p[:, 40:48], False, j == 15) for j in range(16)])
+            vop(128, ["segX"], [K("S") + "a", "P1"], scan(X("S", 0, 128), T.segX[:], T.P1[:, 256:384], 0.0, OP.min, OP.max))
+            vg(128, [K("S") + "a", "LE", "dm"], [K("B")], tt(X("B", 0, 128), X("S", 0, 128).indirect(T.LE[:, 0:8]), T.dm[:, 0:128], OP.mult))
+            pop(256, [K("B"), "g8"], ["P2"], [mm(T.P2[:, 16:24], X("B", 0, 128), T.g8[:], True, True)])
+            vop(8, [], [K("vI"), "P2"], cp(X("vI"), T.P2[:, 16:24]))
+            vop(8, [K("vI")], [K("nI")], ts(X("nI"), X("vI"), 1023, None, OP.bitwise_and))
+            vop(8, [K("vI")], [K("jI")], ts(X("jI"), X("vI"), 10, 15, OP.logical_shift_right, OP.bitwise_and))
+            vop(8, [K("jI"), "EB"], [K("jI")], tt(X("jI"), T.EB[:], X("jI"), OP.subtract))
+            vop(8, [K("jI")], [K("eO")], cp(X("eO"), X("jI")))
+            sg(128, et + [K("eO")], [K("eS")], act(X("eS"), T.E[:, a0:a0 + 2048].indirect(X("eO")), AF.Copy))
+            vop(8, [K("nI"), "idx"], [K("nt")], tt(X("nt"), T.idx[:], X("nI"), OP.subtract))
+            vop(8, [K("nt"), "al"], [K("nt")], tt(X("nt"), X("nt"), T.al[:, 8 * h:8 * h + 8], OP.mult))
+            vop(8, [K("nt"), K("nI")], [K("nS")], tt(X("nS"), X("nI"), X("nt"), OP.add))
+            sg(128, [K("S") + "a", "LE"], [K("nBs")], act(X("nBs"), X("S", 0, 128).indirect(T.LE[:, 0:8]), AF.Copy))
+            pop(512, [K("nBs"), "identF"], ["P2"], [mm(T.P2[:, 128:256], X("nBs"), T.identF[:], True, True)])
+            vop(128, [], [K("uA"), "P2"], cp(X("uA"), T.P2[:, 128:256]))
+            vop(128, [K("uA")], [K("uA")], ts(X("uA"), X("uA"), 1023, None, OP.bitwise_and))
+            eqt = ["EQ%d%d" % (h, i) for i in range(8)]
+            vg(128, [K("nS"), "LX", K("uA")], [eqt[7]], tt(X("EQ", 896), X("nS").indirect(T.LX[:]), X("uA"), OP.is_equal))
+            vop(128, [eqt[7], "ltm"], [eqt[7]], tt(X("EQ", 896), X("EQ", 896), T.ltm[:], OP.mult), 2)
+            fs = [mm(T.P3[:, 128:256], T.grp[:], X("EQ", 896), True, False)]
+            for c in range(7):
+                s = 16 * (c + 1)
+                e = X("EQ", 128 * c + s, 128 * c + 128)
+                vop(128 - s, [K("nS"), K("uA")], [eqt[c]], ts(e, X("uA", s), X("nS", c, c + 1), None, OP.is_equal))
+                fs.append(mm(T.P3[:, 128 + s:256], T.grp[:], e, False, c == 6))
+            pop(640, eqt + ["grp"], ["P3"], fs)
+            vop(128, ["dmI"], [K("B"), "P3"], tt(X("B", 0, 128), T.P3[:, 128:256], T.dmI[:], OP.mult))
+            vop(128, [K("B"), "seg1"], [K("S") + "b"], scan(X("S", 512), T.seg1[:, 0:128], X("B", 0, 128), 0.0, OP.mult, OP.add))
+            vop(8, [K("S") + "b", K("nS")], [K("nl")], tt(X("nl"), X("S", 527, 640, 16), X("nS"), OP.max))
+            vop(8, [K("nl"), "idx"], [K("nl")], tt(X("nl"), X("nl"), T.idx[:], OP.min))
+            for x in (0, 1):
+                vop(8, [K("nl")], [K("oD%d" % x)], cp(X("oD", x, 16, 2), X("nl")))
+            vop(8, [K("nl")], [K("oU")], cp(X("oU"), X("nl")))
+            sg(256, [K("oD0"), K("oD1"), "coF0", "coF1", "coF2"], [K("T1")], act(X("T1"), T.coF[:].indirect(X("oD")), AF.Copy))
+            vop(256, [K("T1")], [K("T2")], lambda X=X: V.transpose(X("T2"), X("T1")))
+            vg(128, [K("T2"), "LP"], [K("fL")], cp(X("fL"), X("T2").indirect(T.LP[:])))
+            for k in range(16):
+                off = X("fL", 8 * k, 8 * k + 8)
+                if k in FLAG_S[h]:
+                    sop(128, [K("fL"), "sts%d" % t], ["Fs%d" % h], act(T["Fs%d" % h][:].indirect(off), T.sts[:, 128 * t:128 * t + 128], AF.Silu), SC)
+                else:
+                    vop(128, [K("fL"), "stv%d" % t], ["Fv"], cp(T.Fv[:].indirect(off), T.stv[:, 128 * t:128 * t + 128]), SC)
+            sop(1536, ["Fs%d" % h], ["FsB%d" % h], act(T["FsB%d" % h][:], T["Fs%d" % h][:, 1024:2560], AF.Copy))
+        for h in (1, 0):
+            vop(128, ["eS_%d" % h, "oU_%d" % h], x_t, cp(T.Xw[:].indirect(T.oU[:, 8 * h:8 * h + 8]), T.eS[:, 128 * h:128 * h + 128]), SC)
+
+        F = lambda src, o, first, last: [mm(T.P4[:, 256:352], T.selX[:, 128 * r:128 * r + 128], src[:, o + r:o + 1536:16], first and r == 0, last and r == 15) for r in range(16)]
+        pop(1632, ["FsB0", "selX", "Fc", "idBig"], ["P4"], F(T.FsB0, 0, True, False) + [mm(T.P4[:, 256:352], T.idBig[:], T.Fc[:], False, False)])
+        for x in (0, 1):
+            gop(256, [], ["Vw%d" % x], iof(T["Vw%d" % x][:, 0:256], [[1, 256]], 2560))
+        pop(1536, ["FsB1", "selX"], ["P4"], F(T.FsB1, 0, False, False))
+        pop(1536, ["Fv", "selX"], ["P4"], F(T.Fv, 1024, False, True))
+        vop(96, [], ["Fp", "P4"], ts(T.Fp[:], T.P4[:, 256:352], 384.0 * 8 ** t, None, OP.is_ge))
+        vop(96, ["Fp", "one96"], ["Fi"], scan(T.Fi[:], T.one96[:], T.Fp[:], 0.0, OP.mult, OP.add), 0.5)
+        p7 = T.P7[:, 0:96]
+        pop(288, ["Fp", "ident", "c4k", "nid4k", "ntri"], ["P7"], [mm(p7, T.ident[:], T.c4k[:], True, False), mm(p7, T.nid4k[:], T.Fp[:], False, False), mm(p7, T.ntri[:], T.Fp[:], False, False)])
+        pop(96, ["Fi", "grp"], ["P7"], [mm(p7, T.grp[:], T.Fi[:], False, True)])
+        vop(96, ["Ld1"], ["s96", "P7"], tt(T.s96[:], p7, T.Ld1[:], OP.min))
+        vop(96, ["s96"], ["Lv"], ts(T.Lv[:], T.s96[:], -1.0, None, OP.add))
+        vop(96, [], ["t96", "P7"], ts(T.t96[:], p7, 256.0, None, OP.is_le))
+        vop(768, ["Lv", "iotaV"], ["Vw0"], cp(T.Vw0[:].indirect(T.Lv[:, 0:48]), T.iotaV[:, 0:768]), SC)
+        sop(768, ["Lv", "iotaV"], ["Vw1"], act(T.Vw1[:].indirect(T.Lv[:, 48:96]), T.iotaV[:, 768:1536], AF.Silu), SC)
+        vop(96, ["t96", "Fp"], ["Fc"], tt(T.Fc[:], T.Fp[:], T.t96[:], OP.subtract), 2)
+        vop(256, ["Vw0", "Vw1"], ["vS"], tt(T.vS[:], T.Vw0[:, 0:256], T.Vw1[:, 0:256], OP.min), 2)
+        vop(256, ["vS", "dm"], ["vX"], tt(T.vX[:], T.vS[:], T.dm[:, 0:256], OP.mult), 2)
+        vop(256, ["vX", "seg1"], ["vS"], scan(T.vS[:], T.seg1[:], T.vX[:], 0.0, OP.mult, OP.add))
+        vop(16, ["vS"], ["vL"], cp(T.vL[:], T.vS[:, 15::16]))
+        vg(256, ["vL"] + su_t, ["sR"], cp(T.sR[:], T.suI[:].indirect(T.vL[:])))
+        for q in range(8):
+            a, h = 512 * q, q // 4
+            gt, zt, at = "gF%d%d" % (h, q % 4), "z%d%d" % (h, q % 4), "az%d%d" % (h, q % 4)
+            win = T.Xw[:, 0:2560].indirect(T.sR[:, 32 * q:32 * q + 32])
+            if q in REN_S:
+                sg(512, x_t + ["sR"], [gt], act(T.gF[:, a:a + 512], win, AF.Copy))
+            else:
+                vg(512, x_t + ["sR"], [gt], cp(T.gF[:, a:a + 512], win))
+            vop(512, [gt, "rX"], [zt], scan(T.z[:, a:a + 512], T.rX[:], T.gF[:, a:a + 512], 0.0, OP.min, OP.max), 0.5)
+            vop(512, [gt, "rN"], [at], scan(T.az[:, a:a + 512], T.rN[:], T.gF[:, a:a + 512], 64.0, OP.max, OP.min), 0.5)
+            if q % 4 == 3:
+                b = 2048 * h
+                vop(128, [x + "%d%d" % (h, i) for i in range(4) for x in ("z", "az")], ["rs%d" % h],
+                    tt(T.rs[:, 128 * h:128 * h + 128], T.z[:, b + 15:b + 2048:16], T.az[:, b + 15:b + 2048:16], OP.add), 2)
+        vop(256, ["rs0", "rs1"], ["rI"], ts(T.rI[:], T.rs[:], 0.5, -0.25, OP.mult, OP.add))
+        vop(256, ["rI", "vL"], x_t, cp(T.Xw[:].indirect(T.vL[:]), T.rI[:]), SC)
+        cur, co_, cur_t = T.land, no, ["land%d" % (t + 1)]
+    for a in (0, 1280):
+        op("Y", 4.0, x_t, [], [lambda a=a: g.sync.dma_start(T.yx[:, a:a + 1280], T.Xw[:, a:a + 1280])], "so", 16, True)
+
+    if "o" not in ORDER:
+        ORDER["o"], ORDER["start"], ORDER["end"] = schedule(ops)
+        ORDER["ops"] = [(o["e"], o["c"]) for o in ops]
+    queue = {"V": V, "S": S, "PE": PE, "G": g, "Y": g.sync}
+    count, known = {}, {q: {} for q in queue}
+    for i in ORDER["o"]:
+        o = ops[i]
+        e, clk = o["e"], {}
+        if e != "R":
+            kn = known[e]
+            for d in reversed(o["hard"]):
+                x = ops[d]
+                if x["sem"] != "none" and kn.get(x["s"], 0) < x["n"]:
+                    queue[e].wait_ge(T.sem[x["s"]], x["n"])
+                    for s, v in x["clk"].items():
+                        kn[s] = max(kn.get(s, 0), v)
+            clk = dict(kn)
+        s = o["sem"] or esem[e]
+        inc = 16 if o["sem"] else 1
+        for f in o["f"]:
+            ins = f()
+            if s != "none":
+                ins.then_inc(T.sem[s], inc)
+                count[s] = count.get(s, 0) + inc
+        if e == "R":
+            count[s] = o["val"]
+        if s != "none":
+            o["s"], o["n"] = s, count[s]
+            clk[s] = count[s]
+        o["clk"] = clk
+    for s in SEMAPHORES:
+        if count.get(s, 0) > known["Y"].get(s, 0):
+            g.sync.wait_ge(T.sem[s], count[s])
+    g.wait_ge(T.sem.ls, 4 * 6)

@@ -1,80 +1,102 @@
-from concourse.mybir import AluOpType as OP, AxisListType, ActivationFunctionType as AF
+from concourse.mybir import AluOpType as OP, ActivationFunctionType as AF
 
 R = 4
+MID = 8096
 SCRATCH = {}
 for _n, _w, _t in [
-        ("Xw", 2816, "bfloat16"), ("coI", 2560, "int32"), ("coH", 2560, "bfloat16"), ("coF", 2688, "float32"),
-        ("suI", 2816, "int32"), ("sh0", 4096, "bfloat16"), ("sh1", 4096, "bfloat16"), ("dls", 1024, "bfloat16"),
-        ("M", 4096, "bfloat16"), ("E", 4096, "bfloat16"), ("z", 4096, "bfloat16"), ("az", 4096, "bfloat16"), ("gF", 4096, "bfloat16"),
-        ("Fv", 2688, "bfloat16"), ("Fs0", 2688, "float32"), ("Fs1", 2688, "float32"), ("FsB0", 1536, "bfloat16"), ("FsB1", 1536, "bfloat16"),
-        ("Vw0", 3072, "float32"), ("Vw1", 3072, "float32"), ("iotaV", 1536, "float32"),
-        ("ident", 128, "bfloat16"), ("nident", 128, "bfloat16"), ("nid32", 128, "bfloat16"), ("nid4k", 128, "bfloat16"), ("idBig", 128, "bfloat16"),
-        ("c4k", 96, "bfloat16"), ("dmI", 128, "float32"), ("ta", 32, "float32"), ("identF", 128, "float32"), ("grp", 128, "bfloat16"), ("grpF", 128, "float32"),
-        ("onesF", 128, "float32"), ("onesB", 128, "bfloat16"), ("ntri", 128, "bfloat16"), ("selX", 2048, "bfloat16"), ("WT", 2048, "bfloat16"),
-        ("g8", 8, "float32"), ("g8s", 24, "float32"), ("g8p", 48, "bfloat16"), ("cK", 640, "bfloat16"),
-        ("jm", 1024, "float32"), ("segN", 512, "float32"), ("segX", 128, "float32"), ("seg1", 256, "float32"), ("rN", 512, "bfloat16"), ("rX", 512, "bfloat16"),
-        ("dm", 640, "float32"), ("ltm", 128, "bfloat16"), ("pI", 8, "int32"), ("pT", 32, "int32"), ("pF", 8, "float32"),
-        ("eI", 64, "int32"), ("LE", 40, "uint16"), ("LX", 8, "uint16"), ("LP", 8, "uint16"), ("Ld1", 96, "float32"),
-        ("idx", 8, "float32"), ("EB", 8, "float32"), ("one96", 96, "bfloat16"),
-        ("stv", 512, "bfloat16"), ("sts", 512, "float32"), ("wt_", 8, "bfloat16"), ("wtF", 8, "float32"), ("thI", 8, "int32"), ("thF", 8, "float32"),
-        ("thr", 8, "float32"), ("th16", 8, "float32"), ("gT", 128, "float32"), ("laI", 16, "int32"), ("lbI", 16, "int32"),
-        ("abI", 32, "float32"), ("land", 128, "float32"), ("abo", 128, "float32"), ("abU", 32, "uint16"),
-        ("al", 16, "float32"), ("acc", 8, "float32"), ("acJ", 16, "int32"),
-        ("df", 512, "uint16"), ("dfH", 512, "bfloat16"), ("dfF", 512, "float32"),
-        ("Fp", 96, "bfloat16"), ("Fc", 96, "bfloat16"), ("Fi", 96, "bfloat16"), ("t96", 96, "float32"), ("s96", 96, "float32"), ("Lv", 96, "uint16"),
-        ("vX", 256, "float32"), ("vS", 256, "float32"), ("vL", 16, "uint16"), ("sR", 256, "uint16"), ("rs", 256, "float32"), ("rI", 256, "int32")]:
+        ("sh0", 4096, "bfloat16"), ("sh1", 4096, "bfloat16"), ("dls", 1024, "bfloat16"),
+        ("ident", 128, "bfloat16"), ("nident", 128, "bfloat16"), ("idC", 512, "bfloat16"), ("idBig", 128, "bfloat16"), ("id4k", 128, "bfloat16"),
+        ("identF", 128, "float32"), ("id64F", 128, "float32"), ("antiF", 256, "float32"), ("grp", 128, "bfloat16"), ("onesF", 128, "float32"), ("onesB", 128, "bfloat16"),
+        ("c32", 128, "bfloat16"), ("cK", 768, "bfloat16"), ("selX", 2048, "bfloat16"),
+        ("dupB", 256, "bfloat16"), ("dupF", 256, "float32"), ("triI", 128, "bfloat16"), ("triS", 128, "bfloat16"),
+        ("g8", 8, "float32"), ("g8p", 48, "bfloat16"), ("gK", 48, "float32"), ("gB", 64, "float32"), ("gN", 24, "float32"), ("g4B", 8, "bfloat16"), ("g4F", 8, "float32"),
+        ("jm", 512, "float32"), ("dm", 512, "float32"), ("dmr", 128, "float32"), ("segN", 512, "float32"), ("segX", 256, "float32"), ("seg1", 128, "bfloat16"),
+        ("rN", 1024, "bfloat16"), ("rX", 1024, "bfloat16"), ("mE", 576, "bfloat16"), ("iotaB", 256, "bfloat16"), ("w12", 16, "bfloat16"), ("c1k", 8, "bfloat16"),
+        ("rk", 128, "float32"), ("idx", 16, "float32"), ("idxR", 128, "float32"), ("EB", 8, "float32"), ("pI", 8, "int32"), ("pT", 64, "int32"), ("pF", 16, "float32"),
+        ("eI", 64, "int32"), ("LE", 32, "uint16"), ("LX", 8, "uint16"), ("LP", 8, "uint16"), ("LD", 8, "uint16"),
+        ("stv", 512, "bfloat16"), ("sts", 512, "float32"), ("thI", 8, "int32"), ("thF", 8, "float32"), ("gT", 256, "float32"),
+        ("thr", 8, "float32"), ("th16", 8, "float32"), ("acc", 8, "float32"), ("acJ", 16, "int32"), ("junk", 8, "float32"),
+        ("abI", 32, "int32"), ("land", 96, "float32"), ("abo", 128, "float32")]:
     SCRATCH[_n] = ("sbuf", [128, _w], _t)
-HALF = {}
-for _n, _w, _t in [("S", 640, "float32"), ("B", 640, "float32"), ("dL", 8, "uint16"), ("sT", 128, "uint16"),
-                   ("uI", 128, "int32"), ("uA", 128, "int32"), ("uB", 128, "int32"), ("nO", 128, "uint16"), ("nP", 128, "float32"),
-                   ("vI", 8, "int32"), ("nI", 8, "int32"), ("jI", 8, "int32"), ("eO", 8, "uint16"), ("nS", 8, "float32"), ("nt", 8, "float32"), ("nl", 8, "float32"),
-                   ("nBs", 128, "float32"), ("EQ", 1024, "bfloat16"), ("oU", 8, "uint16"), ("oD", 16, "uint16"), ("T1", 256, "float32"),
-                   ("T2", 256, "float32"), ("fL", 128, "uint16"), ("eS", 128, "bfloat16")]:
-    SCRATCH[_n] = ("sbuf", [128, 2 * _w], _t)
-    HALF[_n] = _w
+OWN = {}
+for _n, _w, _t in [
+        ("Xw", 2816, "bfloat16"), ("coF", 2688, "float32"), ("suI", 2816, "int32"), ("Fv0", 2688, "bfloat16"), ("Fv1", 2688, "bfloat16"), ("Fs", 2688, "float32"),
+        ("M", 2048, "bfloat16"), ("E", 2048, "bfloat16"), ("z", 1024, "bfloat16"), ("az", 2048, "bfloat16"), ("gF", 2048, "bfloat16"),
+        ("WT", 2048, "bfloat16"), ("wt_", 8, "bfloat16"),
+        ("abU", 16, "uint16"), ("df", 256, "uint16"), ("dfF", 256, "float32"), ("dfH", 256, "bfloat16"), ("S", 512, "float32"), ("B", 512, "float32"),
+        ("dL", 8, "uint16"), ("dF", 16, "float32"), ("d64", 8, "float32"), ("al", 16, "float32"), ("alI", 16, "float32"), ("ta", 16, "float32"),
+        ("sT", 128, "uint16"), ("uI", 128, "int32"), ("uA", 128, "int32"), ("uB", 128, "int32"), ("nO", 128, "uint16"), ("nP", 128, "float32"),
+        ("jI", 8, "int32"), ("eO", 8, "uint16"), ("nS", 16, "float32"), ("nt", 128, "float32"), ("fm", 128, "float32"), ("nl", 8, "float32"),
+        ("sp", 128, "bfloat16"), ("EQ", 576, "bfloat16"), ("EK", 576, "bfloat16"),
+        ("oD", 16, "uint16"), ("oU", 16, "uint16"), ("T1", 256, "float32"), ("T2", 256, "float32"), ("fL", 128, "uint16"),
+        ("eS", 128, "bfloat16"), ("eD", 256, "bfloat16"), ("Fp", 128, "bfloat16"), ("Fc", 128, "bfloat16"), ("Fi", 128, "bfloat16"), ("tot", 128, "bfloat16"),
+        ("cum", 8, "bfloat16"), ("Th", 1024, "bfloat16"), ("cL", 8, "uint16"), ("Rw", 136, "float32"), ("D", 128, "bfloat16"),
+        ("vL", 8, "uint16"), ("vF", 8, "float32"), ("vD", 16, "uint16"), ("sR", 128, "uint16"), ("rI", 256, "int32")]:
+    _b = _n if _w > 256 or _n == "wt_" else "small_" + _t
+    _at, _w16 = SCRATCH.get(_b, (0, [0, 0]))[1][1], -(-_w // 16) * 16
+    SCRATCH[_b] = ("sbuf", [128, _at + 2 * _w16], _t)
+    OWN[_n] = (_b, _at, _w16, _w)
 for _b in range(8):
     SCRATCH["P%d" % _b] = ("psum", [128, 512], "float32")
 
-LOADS = ["la", "lb", "dl", "co0", "co1", "x0", "x1", "su0", "su1", "wt", "th"]
-SEMAPHORES = ["sv", "ss", "sp", "sg", "ls", "so"] + ["ld_" + n for n in LOADS] + ["rdl%d" % t for t in (1, 2, 3)] + ["rab%d" % t for t in (1, 2, 3)]
+LOADS = ["ab", "dl", "co0", "co1", "x0", "x1", "su0", "su1", "wt", "th"]
+SEMAPHORES = (["sv", "ss", "sp", "sg", "ls", "so", "sb0", "sb1"] + ["ld_" + n for n in LOADS] + ["rdl%d" % t for t in (1, 2, 3)]
+              + ["rab%d%d" % (t, s) for t in (1, 2, 3) for s in (0, 1)])
 
-CY, WAKE, LAM, GA, SC = 0.83e-3, 0.1, 0.0, 1.5, 3.5
-SPATH = {1: ((1, 3), (1, 2, 3)), 2: ((1, 3), (1, 3))}
-MPATH = {1: ((1, 3), (3,)), 2: ((), (3,))}
-FLAG_S = (tuple(range(10)), tuple(range(5)))
-REN_S = (1, 2, 3, 4, 5, 6, 7)
+CFG = {"first": {1: "VVVV", 2: "VVVV"}, "second": {1: "SSSS", 2: "SSSV"}, "renew": "SSSS", "flagS": 7, "conv": "S", "merge": 2, "scans": ((0, 2), (2, 1), (3, 1)),
+       "cum": True, "passes": 3, "lead": 8.0, "wake": 0.14, "pe": 0.8}
+CY, GA, SC = 0.83e-3, 1.45, 3.3
 ORDER = {}
 
 
 def schedule(ops):
     n = len(ops)
+    cost = [o["c"] for o in ops]
+    hold = [0.06 * max(len(o["f"]), 1) if o["async"] else o["c"] for o in ops]
+    pred = [[(d, cost[d] + CFG["wake"] if d in o["hard"] else cost[d] if o["e"] == "R" else hold[d]) for d in o["deps"]] for o in ops]
     succ = [[] for _ in ops]
-    for i, o in enumerate(ops):
-        for d in o["deps"]:
-            succ[d].append(i)
+    for i in range(n):
+        for d, lag in pred[i]:
+            succ[d].append((i, lag))
+
+    def place(order, back):
+        at, used = [0.0] * n, {}
+        for i in order:
+            t = max([at[j] + hold[j] + lag - hold[i] for j, lag in succ[i]] + [cost[i] - hold[i]]) if back else max([at[d] + lag for d, lag in pred[i]] + [0.0])
+            u = used.setdefault(ops[i]["e"], [])
+            lo, hi = 0, len(u)
+            while lo < hi:
+                mid = (lo + hi) // 2
+                lo, hi = (mid + 1, hi) if u[mid][1] <= t else (lo, mid)
+            while lo < len(u) and u[lo][0] < t + hold[i] - 1e-9:
+                t, lo = max(t, u[lo][1]), lo + 1
+            u.insert(lo, (t, t + hold[i]))
+            at[i] = t
+        return at
+
     pri = [0.0] * n
     for i in range(n - 1, -1, -1):
-        pri[i] = ops[i]["c"] + max([pri[s] + WAKE for s in succ[i]], default=0.0)
-    need = [len(o["deps"]) for o in ops]
-    early, start, free, out = [0.0] * n, [0.0] * n, {}, []
-    ready = {i for i in range(n) if need[i] == 0}
-    while ready:
-        best = {}
-        for i in ready:
-            e = ops[i]["e"]
-            best[e] = min(best.get(e, 1e18), max(early[i], free.get(e, 0.0)))
-        e = min(best, key=lambda q: (best[q], q))
-        i = max((j for j in ready if ops[j]["e"] == e and max(early[j], free.get(e, 0.0)) <= best[e] + 0.02), key=lambda j: (pri[j] - LAM * j, -j))
-        s = start[i] = max(early[i], free.get(e, 0.0))
-        free[e] = s + (0.05 if ops[i]["async"] else ops[i]["c"])
-        ready.discard(i)
-        out.append(i)
-        for j in succ[i]:
-            early[j] = max(early[j], s + ops[i]["c"] + WAKE)
-            need[j] -= 1
-            if need[j] == 0:
-                ready.add(j)
-    return out, start, max(start[i] + ops[i]["c"] for i in range(n))
+        pri[i] = max([pri[j] + lag for j, lag in succ[i]] + [cost[i] + (CFG["lead"] if ops[i]["w"][:1] == ["X_0"] else 0.0)])
+    order, best = sorted(range(n), key=lambda i: (-pri[i], i)), None
+    for _ in range(CFG["passes"]):
+        at = place(order, False)
+        end = max(at[i] + cost[i] for i in range(n))
+        if best is None or end < best[2]:
+            best = (sorted(range(n), key=lambda i: (at[i], i)), at, end)
+        bk = place(sorted(range(n), key=lambda i: (-at[i], -i)), True)
+        order = sorted(range(n), key=lambda i: (-bk[i] - hold[i], i))
+    return best
+
+
+def runs(path, letter, most):
+    out = []
+    for q, c in enumerate(path):
+        if c == letter:
+            if out and out[-1][0] + out[-1][1] == q and out[-1][1] < most:
+                out[-1][1] += 1
+            else:
+                out.append([q, 1])
+    return out
 
 
 def rank_program(g, core, T, topo):
@@ -98,17 +120,19 @@ def rank_program(g, core, T, topo):
             lastw[t] = i
             readers[t] = []
         deps.discard(i)
-        ops.append({"e": e, "c": c, "hard": sorted(deps), "deps": sorted(deps | soft), "f": fs, "sem": sem, "val": val, "async": isasync})
+        ops.append({"e": e, "c": c, "hard": sorted(deps), "deps": sorted(deps | soft), "f": fs, "sem": sem, "val": val, "async": isasync, "w": w})
         return i
 
     esem = {"V": "sv", "S": "ss", "PE": "sp", "G": "sg"}
-    vop = lambda n, r, w, f, cy=1.0: op("V", 0.055 + max(n * cy, 64) * CY, r, w, [f])
-    sop = lambda n, r, w, f, cy=1.0: op("S", 0.07 + max(n * cy, 64) * CY, r, w, [f])
+    vop = lambda n, r, w, f, cy=1.0: op("V", 0.04 + max(n * cy, 64) * CY, r, w, [f])
+    sop = lambda n, r, w, f, cy=1.0: op("S", 0.055 + max(n * cy, 64) * CY, r, w, [f])
     vg = lambda n, r, w, f: vop(n, r, w, f, GA)
     sg = lambda n, r, w, f: sop(n, r, w, f, GA)
-    pop = lambda cyc, r, w, fs: op("PE", cyc * CY, r, w, fs)
-    gop = lambda n, r, w, f: op("G", 0.17 + 2 * n * CY, r, w, [f])
-    load = lambda q, name, c, w, out, in_: op(q, c, [], w, [lambda: (g.sync if q == "Y" else S).dma_start(out, in_)], "ld_" + name, 16, True)
+    pop = lambda cyc, r, w, fs: op("PE", cyc * CY * CFG["pe"], r, w, fs)
+    gop = lambda n, r, w, f: op("G", 0.15 + 2 * n * CY, r, w, [f])
+
+    def load(q, name, c, w, pairs, r=(), order=()):
+        return op(q, c, r, w, [(lambda a=a, b=b: (g.sync if q == "Y" else S).dma_start(a, b)) for a, b in pairs], "ld_" + name, 16, True, order)
 
     def ts(out, a, s1, s2, o0, o1=None):
         return (lambda: V.tensor_scalar(out, a, s1, s2, o0)) if o1 is None else (lambda: V.tensor_scalar(out, a, s1, s2, o0, o1))
@@ -122,103 +146,145 @@ def rank_program(g, core, T, topo):
     iof = lambda out, pat, base: (lambda: g.iota(out, pat, base, 0, allow_small_or_imprecise_dtypes=True))
     ioi = lambda out, pat, base, cm: (lambda: g.iota(out, pat, base, cm))
     sel = lambda out, a, pat, o, base, cm: (lambda: g.affine_select(out, a, pat, o, 0.0, base, cm))
-    turn = [0]
+    sets = (0, 1)
 
-    def bank():
-        turn[0] += 1
-        return 5 + turn[0] % 3
+    def own(s):
+        def col(n, a, b, st):
+            _, at, step, w = OWN[n]
+            return slice(at + s * step + a, at + s * step + (w if b is None else b), st)
+        return (lambda n, a=0, b=None, st=1: T[OWN[n][0]][:, col(n, a, b, st)],
+                lambda p, n, a=0, b=None, st=1: T[OWN[n][0]][p:p + 64, col(n, a, b, st)],
+                lambda n: "%s_%d" % (n, s))
 
-    load("Y", "la", 2, ["laI"], T.laI[:], T.la[:])
-    load("Y", "lb", 2, ["lbI"], T.lbI[:], T.lb[:])
-    load("S", "dl", 2.5, ["dl0"], T.dls[:, 0:256], T.dl[:])
-    load("Y", "co0", 6, ["co0"], T.coI[:, 0:1280], T.co[:, 0:1280])
-    load("S", "co1", 6, ["co1"], T.coI[:, 1280:2560], T.co[:, 1280:2560])
-    load("Y", "x0", 8, ["X", "Xa"], T.Xw[:, 0:1280], T.x0[:, 0:1280])
-    load("S", "x1", 8, ["Xb"], T.Xw[:, 1280:2560], T.x0[:, 1280:2560])
-    load("Y", "wt", 3, ["wt"], T.wt_[:, 0:1], T.wt[:])
-    load("Y", "th", 3, ["thI"], T.thI[0:8, 0:1], T.th[:])
-    load("Y", "su0", 12, ["su0"], T.suI[:, 0:1280], T.su[:, 0:1280])
-    load("Y", "su1", 12, ["su1"], T.suI[:, 1280:2560], T.su[:, 1280:2560])
-    co_t, su_t, x_t = ["co0", "co1"], ["su0", "su1", "su2"], ["X", "Xa", "Xb"]
+    half = lambda u: slice(64 * u, 64 * u + 64)
+    X0, XP0, _ = own(0)
+    X1, XP1, _ = own(1)
+    i = load("Y", "co0", 4.5, ["col0"], [(X1("suI", 0, 1280), T.co[:, 0:1280])])
+    i = load("Y", "co1", 7.0, ["col1"], [(X1("suI", 1280, 2560), T.co[:, 1280:2560])], order=[i])
+    i = load("Y", "x0", 8.0, ["Xa_0"], [(XP0(0, "Xw", 0, 2560), T.x0[0:64, :])], order=[i])
+    i = load("Y", "x1", 9.5, ["Xa_1"], [(XP1(64, "Xw", 0, 2560), T.x0[64:128, :])], order=[i])
+    su0 = load("Y", "su0", 14.0, ["su_0"], [(XP0(64 * u, "suI", 0, 2560), T.su[0:64, :]) for u in (0, 1)], order=[i])
+    i = load("S", "ab", 2.5, ["ab0_0", "ab0_1"], [(T.abI[half(u), 16 * s + 8 * q:16 * s + 8 * q + 8], x[half(s), 8 * u:8 * u + 8]) for s in sets for q, x in enumerate((T.la, T.lb)) for u in (0, 1)])
+    i = load("S", "dl", 2.5, ["dl0"], [(T.dls[half(u), 128 * s:128 * s + 128], T.dl[half(s), 128 * u:128 * u + 128]) for s in sets for u in (0, 1)], order=[i])
+    i = load("S", "th", 3, ["thI"], [(T.thI[0:8, 0:1], T.th[:])], order=[i])
+    load("S", "wt", 3, ["wt"], [(own(s)[1](64 * u, "wt_", 0, 1), T.wt[half(s)]) for s in sets for u in (0, 1)], order=[i])
+    for s in sets:
+        X, XP, K = own(s)
+        for h in (0, 1):
+            a, b = 1280 * h, 1280 * h + 1280
+            vop(1280, ["col%d" % h], [K("coa%d" % h)], cp(XP(64 * s, "coF", a, b), XP1(64 * s, "suI", a, b)))
+            sop(1280, [K("coa%d" % h)], [K("cob%d" % h)], act(XP(64 - 64 * s, "coF", a, b), XP(64 * s, "coF", a, b), AF.Copy))
+        vop(2560, [K("Xa")], [K("X")], cp(XP(64 - 64 * s, "Xw", 0, 2560), XP(64 * s, "Xw", 0, 2560)), 0.5)
+    load("Y", "su1", 9.0, ["su_1", "col0", "col1"], [(XP1(64 * u, "suI", 0, 2560), T.su[64:128, :]) for u in (0, 1)], order=[su0])
 
+    pF = lambda c: T.pF[:, c:c + 1]
+    pT = lambda c: T.pT[:, 4 * c:4 * c + 1]
     gop(1, [], ["pI"], ioi(T.pI[:, 0:1], [[0, 1]], 0, 1))
-    gop(256, [], ["jm"], iof(T.jm[:], [[0, 64], [1, 16]], 0))
-    vop(1, ["pI"], ["pT"], ts(T.pT[:, 0:1], T.pI[:, 0:1], 15, None, OP.bitwise_and))
-    vop(1, ["pT"], ["pF"], cp(T.pF[:, 0:1], T.pT[:, 0:1]))
-    vop(640, ["jm", "pF"], ["dm"], ts(T.dm[:], T.jm[:, 0:640], T.pF[:, 0:1], None, OP.is_equal))
-    vop(512, ["jm"], ["segN"], ts(T.segN[:], T.jm[:, 0:512], 0.0, 1e9, OP.is_equal, OP.mult))
-    gop(40, [], ["eI"], ioi(T.eI[:, 0:40], [[16, 40]], 15, 0))
-    vop(40, ["eI"], ["LE"], cp(T.LE[:], T.eI[:, 0:40]))
+    gop(512, [], ["jm"], iof(T.jm[:], [[0, 32], [1, 16]], 0))
+    for c, (a, b) in enumerate(((0, 15), (0, 112), (0, 64), (0, 7), (0, 16), (3, 1))):
+        vop(1, ["pI"], ["pT%d" % c], ts(pT(c), T.pI[:, 0:1], a, b, OP.logical_shift_right, OP.bitwise_and))
+    vop(1, ["pT0"], ["p16"], cp(pF(0), pT(0)))
+    vop(1, ["pT0"], ["p15"], ts(pF(1), pT(0), -1.0, 15.0, OP.mult, OP.add))
+    vop(1, ["pT0"], ["p256"], ts(pF(3), pT(0), 16.0, None, OP.mult))
+    vop(1, ["pT1"], ["p32"], ts(pF(4), pT(1), 2.0, None, OP.mult))
+    vop(1, ["pT2"], ["p128"], ts(pF(5), pT(2), 2.0, None, OP.mult))
+    vop(512, ["jm", "p16"], ["dm"], ts(T.dm[:], T.jm[:], pF(0), None, OP.is_equal))
+    vop(128, ["jm", "p15"], ["dmr"], ts(T.dmr[:], T.jm[:, 0:128], pF(1), None, OP.is_equal))
+    sop(512, ["jm"], ["segN"], act(T.segN[:], T.jm[:], AF.Identity, scale=-1e9, bias=5e8))
+    sop(256, ["jm"], ["segX"], act(T.segX[:], T.jm[:, 0:256], AF.Identity, scale=1e9))
+    sop(128, ["jm"], ["seg1"], act(T.seg1[:], T.jm[:, 0:128], AF.Sign))
+    for h in (0, 1):
+        sop(512, ["jm"], ["rN%d" % h], act(T.rN[:, 512 * h:512 * h + 512], T.jm[:], AF.Relu, scale=-64.0, bias=64.0))
+        sop(512, ["jm"], ["rX%d" % h], act(T.rX[:, 512 * h:512 * h + 512], T.jm[:], AF.Identity, scale=64.0))
+    gop(32, [], ["eI"], ioi(T.eI[:, 0:32], [[16, 32]], 15, 0))
+    vop(32, ["eI"], ["LE"], cp(T.LE[:], T.eI[:, 0:32]))
     vop(128, [], ["onesB"], fill(T.onesB[:], 1.0))
     vop(128, [], ["onesF"], fill(T.onesF[:], 1.0))
-    gop(128, ["onesB"], ["ident"], sel(T.ident[:], T.onesB[:], [[-1, 128]], OP.is_equal, 0, 1))
-    for nm, c in (("nident", -1.0), ("nid32", -32.0), ("nid4k", -4096.0), ("idBig", 1048576.0)):
-        vop(128, ["ident"], [nm], ts(T[nm][:], T.ident[:], c, None, OP.mult))
-    vop(96, [], ["c4k"], fill(T.c4k[:], 4096.0))
-    gop(128, [], ["dmI"], iof(T.dmI[:], [[1, 128]], 2560))
-    vop(128, ["dmI", "dm"], ["dmI"], tt(T.dmI[:], T.dmI[:], T.dm[:, 0:128], OP.mult), 2)
+    gop(128, ["onesF"], ["identF"], sel(T.identF[:], T.onesF[:], [[-1, 128]], OP.is_equal, 0, 1))
+    for nm, a, c in (("ident", 0, 1.0), ("nident", 0, -1.0), ("idC", 0, 1.0), ("idC", 128, -2048.0), ("idC", 256, -32.0), ("idC", 384, 1.0),
+                     ("idBig", 0, 1048576.0), ("id4k", 0, 4096.0), ("id64F", 0, 64.0)):
+        sop(128, ["identF"], ["%s%d" % (nm, a) if nm == "idC" else nm], act(T[nm][:, a:a + 128], T.identF[:], AF.Identity, scale=c))
+    gop(128, ["onesF"], ["anti0"], sel(T.antiF[:, 0:128], T.onesF[:], [[1, 128]], OP.is_equal, -127, 1))
+    sop(128, ["anti0"], ["anti1"], act(T.antiF[:, 128:256], T.antiF[:, 0:128], AF.Identity, scale=-1.0))
     gop(8, ["onesF"], ["g8"], sel(T.g8[:], T.onesF[:, 0:8], [[-16, 8]], OP.is_ge, 0, 1))
     gop(8, ["g8"], ["g8"], sel(T.g8[:], T.g8[:], [[16, 8]], OP.is_ge, 15, -1))
-    for i, s in enumerate((2048.0, 512.0, 16.0, 2048.0, 512.0, 16384.0)):
-        vop(8, ["g8"], ["g8p"], ts(T.g8p[:, 8 * i:8 * i + 8], T.g8[:], s, None, OP.mult))
-    for i, s in enumerate((32.0, -4128.0, 1.0)):
-        vop(8, ["g8"], ["g8s"], ts(T.g8s[:, 8 * i:8 * i + 8], T.g8[:], s, None, OP.mult))
-    for i, (s, v) in enumerate(((128, -160), (32, 5120), (1, 0), (128, -160), (32, 5120))):
-        gop(128, [], ["cK"], iof(T.cK[:, 128 * i:128 * i + 128], [[0, 8], [s, 16]], v))
-    gop(128, ["onesF"], ["grpF"], sel(T.grpF[:], T.onesF[:], [[-16, 8], [0, 16]], OP.is_ge, 0, 1))
-    gop(128, ["grpF"], ["grpF"], sel(T.grpF[:], T.grpF[:], [[16, 8], [0, 16]], OP.is_ge, 15, -1))
-    vop(128, ["grpF"], ["grp"], cp(T.grp[:], T.grpF[:]))
-    gop(128, ["onesF"], ["gT"], sel(T.gT[:], T.onesF[:], [[1, 8], [0, 16]], OP.is_equal, 0, -1))
-    gop(128, ["onesF"], ["identF"], sel(T.identF[:], T.onesF[:], [[-1, 128]], OP.is_equal, 0, 1))
-    vop(1, ["thI"], ["thF"], cp(T.thF[0:8, 0:1], T.thI[0:8, 0:1]))
-    pop(256, ["gT", "thF"], ["P7"], [mm(T.P7[:, 0:1], T.gT[0:8, :], T.thF[0:8, 0:1], True, True)])
-    vop(1, [], ["th16", "P7"], ts(T.th16[:, 0:1], T.P7[:, 0:1], 16.0, None, OP.mult))
-    vop(1, ["th16"], ["thr"], cp(T.thr[:, 0:1], T.th16[:, 0:1]))
-    for j in range(16):
-        gop(128, ["grp"], ["selX"], sel(T.selX[:, 128 * j:128 * j + 128], T.grp[:], [[0, 8], [1, 16]], OP.is_equal, -j, 0))
-    vop(1, ["wt"], ["wtF"], cp(T.wtF[:, 0:1], T.wt_[:, 0:1]))
-    vop(2048, ["selX", "wtF"], ["WT"], ts(T.WT[:], T.selX[:], T.wtF[:, 0:1], None, OP.mult), 0.5)
-    vop(128, ["jm"], ["segX"], ts(T.segX[:], T.jm[:, 0:128], 0.0, 1e9, OP.is_gt, OP.mult))
-    vop(256, ["jm"], ["seg1"], ts(T.seg1[:], T.jm[:, 0:256], 0.0, None, OP.is_gt))
-    vop(512, ["jm"], ["rN"], ts(T.rN[:], T.jm[:, 0:512], 0.0, 64.0, OP.is_equal, OP.mult))
-    vop(512, ["jm"], ["rX"], ts(T.rX[:], T.jm[:, 0:512], 0.0, 64.0, OP.is_gt, OP.mult))
-    vop(128, ["jm", "pF"], ["ltm"], ts(T.ltm[:], T.jm[:, 0:128], T.pF[:, 0:1], None, OP.is_gt))
-    vop(96, [], ["one96"], fill(T.one96[:], 1.0))
-    vop(96, [], ["Fc"], fill(T.Fc[:], 0.0))
-    vop(2688, [], ["Fv"], fill(T.Fv[:], 0.0), 0.5)
-    for h in (0, 1):
-        gop(2688, [], ["Fs%d" % h], iof(T["Fs%d" % h][:], [[0, 2688]], 0))
-    vop(256, [], ["su2"], fill(T.suI[:, 2560:2816], 0))
-    gop(128, [], ["coF2"], iof(T.coF[:, 2560:2688], [[1, 128]], 2560))
-    gop(1536, [], ["iotaV"], iof(T.iotaV[:], [[1, 1536]], 1024))
-    sop(1536, ["iotaV"], ["iotaV"], act(T.iotaV[:], T.iotaV[:], AF.Identity, bias=0.25))
-    gop(8, [], ["eI2"], ioi(T.eI[:, 48:56], [[1, 8]], 0, 0))
-    vop(8, ["eI2"], ["LX"], cp(T.LX[:], T.eI[:, 48:56]))
-    gop(8, [], ["idx"], iof(T.idx[:], [[16, 8]], 2560))
-    vop(8, ["pF", "idx"], ["idx"], ts(T.idx[:], T.idx[:], T.pF[:, 0:1], None, OP.add))
-    gop(96, [], ["Ld1"], iof(T.Ld1[:], [[16, 96]], 1537))
-    vop(96, ["pF", "Ld1"], ["Ld1"], ts(T.Ld1[:], T.Ld1[:], T.pF[:, 0:1], None, OP.add))
-    vop(1, ["pF"], ["pF2"], ts(T.pF[:, 1:2], T.pF[:, 0:1], 16.0, None, OP.mult))
-    vop(1, ["pF"], ["pFn"], ts(T.pF[:, 6:7], T.pF[:, 0:1], -1024.0, 15360.0, OP.mult, OP.add))
-    gop(8, [], ["EB"], iof(T.EB[:], [[256, 8]], 15))
-    vop(8, ["pF2", "EB"], ["EB"], ts(T.EB[:], T.EB[:], T.pF[:, 1:2], None, OP.add))
-    vop(1, ["pI"], ["pT1"], ts(T.pT[:, 8:9], T.pI[:, 0:1], 7, None, OP.bitwise_and))
-    vop(1, ["pI"], ["pT2"], ts(T.pT[:, 16:17], T.pI[:, 0:1], 16, None, OP.bitwise_and))
-    vop(1, ["pI"], ["pT3"], ts(T.pT[:, 24:25], T.pI[:, 0:1], 3, 1, OP.logical_shift_right, OP.bitwise_and))
-    vop(1, ["pT2"], ["pF3"], cp(T.pF[:, 3:4], T.pT[:, 16:17]))
-    vop(1, ["pT1", "pF3"], ["pF4"], ts(T.pF[:, 4:5], T.pT[:, 8:9], 32.0, T.pF[:, 3:4], OP.mult, OP.add))
-    vop(1, ["pT3", "pF4"], ["pF5"], tt(T.pF[:, 5:6], T.pT[:, 24:25], T.pF[:, 4:5], OP.add))
-    gop(8, [], ["eI3"], ioi(T.eI[:, 56:64], [[2, 8]], 0, 0))
-    vop(8, ["eI3", "pF5"], ["LP"], ts(T.LP[:], T.eI[:, 56:64], T.pF[:, 5:6], None, OP.add))
-    gop(128, ["onesB"], ["ntri"], sel(T.ntri[:], T.onesB[:], [[-1, 128]], OP.is_gt, 0, 1))
-    vop(128, ["ntri", "grp"], ["ntri"], tt(T.ntri[:], T.ntri[:], T.grp[:], OP.mult))
-    vop(128, ["ntri"], ["ntri"], ts(T.ntri[:], T.ntri[:], -1.0, None, OP.mult))
-    for t in range(R):
-        vop(128, [], ["stv%d" % t], fill(T.stv[:, 128 * t:128 * t + 128], float(32 * 8 ** t)))
-        vop(128, [], ["sts%d" % t], fill(T.sts[:, 128 * t:128 * t + 128], float(32 * 8 ** t)))
+    for nm, cs in (("g8p", (2048.0, 32768.0, 2048.0, 16.0, 16384.0, 16384.0)), ("gK", (-4096.0, -266240.0, 1.0, 1.0)),
+                   ("gB", (32.0, 2048.0, 0.0, 32.0, 0.015625, 1.0, -32.0, -2048.0))):
+        for i, c in enumerate(cs):
+            sop(8, ["g8"], ["%s%d" % (nm, i)], act(T[nm][:, 8 * i:8 * i + 8], T.g8[:], AF.Identity, scale=c))
     for x in (0, 1):
-        vop(1280, ["co%d" % x], ["coF%d" % x], cp(T.coF[:, 1280 * x:1280 * x + 1280], T.coI[:, 1280 * x:1280 * x + 1280]))
-        sop(1280, ["coF%d" % x], ["coH%d" % x], act(T.coH[:, 1280 * x:1280 * x + 1280], T.coF[:, 1280 * x:1280 * x + 1280], AF.Identity, scale=0.03125, bias=159.515625))
+        sop(8, ["g8"], ["gK%d" % (4 + x)], act(T.gK[:, 32 + x:48:2], T.g8[:], AF.Copy))
+        sop(8, ["g8"], ["gN%d" % x], act(T.gN[:, x:16:2], T.g8[:], AF.Identity, scale=-1.0))
+        vop(4, ["g8"], ["g4F%d" % x], tt(T.g4F[:, 4 * x:4 * x + 4], T.g8[:, 0:4], T.g8[:, 4:8], OP.add))
+    sop(8, ["g8"], ["gN2"], act(T.gN[:, 16:24], T.g8[:], AF.Copy))
+    sop(8, ["g4F0", "g4F1"], ["g4B"], act(T.g4B[:], T.g4F[:], AF.Copy))
+    g8p_t, gK_t, gB_t = ["g8p%d" % i for i in range(6)], ["gK%d" % i for i in range(6)], ["gB%d" % i for i in range(8)]
+    vop(128, [], ["c32"], fill(T.c32[0:64, :], 0.03125))
+    for i, (a, v) in enumerate(((128, -160), (2048, 5120), (128, -160), (1, 0))):
+        gop(128, [], ["cK%d" % i], iof(T.cK[0:32, 128 * i:128 * i + 128], [[0, 8], [a, 16]], v))
+    for i, v in enumerate((-128.0 * MID, 327680.0 - 2048.0 * MID, -128.0 * MID, -1.0 * MID)):
+        vop(128, [], ["cK%d" % (4 + i)], fill(T.cK[32:64, 128 * i:128 * i + 128], v), 0.5)
+    gop(256, [], ["cK8"], iof(T.cK[0:32, 512:768], [[0, 16], [-1024, 16]], 15360))
+    cK_t = ["c32"] + ["cK%d" % i for i in range(8)] + ["idC%d" % a for a in (0, 128, 256, 384)] + ["identF", "id64F"]
+    th_t = ["Th%d_%d" % (G, s) for s in sets for G in range(8)]
+    gop(2048, [], th_t, iof(T.Th[:], [[-1, 16], [32, 8], [1, 16]], 0))
+    vop(2048, th_t + ["p32"], ["selX"], ts(T.selX[:], T.Th[:], pF(4), None, OP.is_equal), 0.5)
+    gop(128, ["onesB"], ["grp"], sel(T.grp[:], T.onesB[:], [[-16, 8], [0, 16]], OP.is_ge, 0, 1))
+    gop(128, ["grp"], ["grp"], sel(T.grp[:], T.grp[:], [[16, 8], [0, 16]], OP.is_ge, 15, -1))
+    sop(128, ["grp"], ["grp"], act(T.grp[:], T.grp[:], AF.Identity, scale=4096.0))
+    for u in (0, 1):
+        gop(128, ["onesF"], ["dupF%d" % u], sel(T.dupF[:, 128 * u:128 * u + 128], T.onesF[:], [[0, 2], [-1, 64]], OP.is_equal, 64 * u - 64, 1))
+    sop(256, ["dupF0", "dupF1"], ["dupB"], act(T.dupB[:], T.dupF[:], AF.Copy))
+    gop(128, ["onesB"], ["triI"], sel(T.triI[:], T.onesB[:], [[1, 128]], OP.is_ge, 0, -1))
+    gop(128, ["onesB"], ["triS"], sel(T.triS[:], T.onesB[:], [[1, 128]], OP.is_gt, 0, -1))
+    gop(256, [], ["iotaB"], iof(T.iotaB[:], [[1, 256]], 0))
+    gop(16, [], ["w12"], iof(T.w12[:], [[16, 16]], 0))
+    gop(16, ["w12"], ["w12"], sel(T.w12[:], T.w12[:], [[0, 16]], OP.is_equal, -127, 1))
+    sop(16, ["w12"], ["w12"], act(T.w12[:], T.w12[:], AF.Identity, bias=12.0))
+    sop(8, ["onesF"], ["c1k"], act(T.c1k[:], T.onesF[:, 0:8], AF.Identity, scale=1024.0))
+    gop(128, [], ["rk"], iof(T.rk[:], [[1, 8], [8, 16]], 0))
+    sop(128, ["rk", "p128"], ["rk"], act(T.rk[:], T.rk[:], AF.Identity, bias=pF(5)))
+    gop(16, [], ["idx"], iof(T.idx[:], [[16, 8], [0, 2]], 2560))
+    sop(16, ["p16", "idx"], ["idx"], act(T.idx[:], T.idx[:], AF.Identity, bias=pF(0)))
+    gop(128, [], ["idxR"], iof(T.idxR[:], [[0, 16], [16, 8]], 2560))
+    sop(128, ["p16", "idxR"], ["idxR"], act(T.idxR[:], T.idxR[:], AF.Identity, bias=pF(0)))
+    gop(8, [], ["EB"], iof(T.EB[:], [[256, 8]], 15))
+    sop(8, ["p256", "EB"], ["EB"], act(T.EB[:], T.EB[:], AF.Identity, bias=pF(3)))
+    gop(8, [], ["eI2"], ioi(T.eI[:, 32:40], [[-1, 8]], 7, 0))
+    vop(8, ["eI2"], ["LX"], cp(T.LX[:], T.eI[:, 32:40]))
+    vop(1, ["pT4"], ["pF6"], cp(pF(6), pT(4)))
+    vop(1, ["pT3", "pF6"], ["pF7"], ts(pF(7), pT(3), 32.0, pF(6), OP.mult, OP.add))
+    vop(1, ["pT5", "pF7"], ["pF8"], tt(pF(8), pT(5), pF(7), OP.add))
+    gop(8, [], ["eI3"], ioi(T.eI[:, 40:48], [[2, 8]], 0, 0))
+    vop(8, ["eI3", "pF8"], ["LP"], ts(T.LP[:], T.eI[:, 40:48], pF(8), None, OP.add))
+    vop(576, [], ["mE"], fill(T.mE[:], 1.0), 0.5)
+    vop(16, ["jm", "p15", "mE"], ["mE0"], ts(T.mE[:, 0:16], T.jm[:, 0:16], pF(1), None, OP.is_gt))
+    for c in range(1, 8):
+        sop(16, ["mE0", "mE"], ["mE%d" % c], act(T.mE[:, 8 * c * (c + 1):8 * c * (c + 1) + 16], T.mE[:, 0:16], AF.Copy))
+    mE_t = ["mE%d" % c for c in range(8)]
+    vop(1, ["pT3"], ["pF9"], ts(pF(9), pT(3), 8.0, 24.0, OP.mult, OP.add))
+    vop(1, ["pT3", "pF9"], ["pF2"], ts(pF(2), pT(3), pF(9), 15.0, OP.mult, OP.add))
+    vop(8, ["pF2", "onesF"], ["LD"], ts(T.LD[:], T.onesF[:, 0:8], pF(2), None, OP.mult))
+    vop(1, ["thI"], ["thF"], cp(T.thF[0:8, 0:1], T.thI[0:8, 0:1]))
+    for s in sets:
+        X, XP, K = own(s)
+        gop(128, ["onesF"], [K("gT")], sel(T.gT[0:8, 128 * s:128 * s + 128], T.onesF[0:8, :], [[0, 2], [1, 4], [0, 16]], OP.is_equal, 4 * s, -1))
+        vop(1, ["wt"], [K("wtF")], cp(pF(10 + s), X("wt_", 0, 1)))
+        vop(2048, th_t + ["p32", K("wtF")], [K("WT")], ts(X("WT"), T.Th[:], pF(4), pF(10 + s), OP.is_equal, OP.mult), 0.5)
+        gop(128, [], [K("co2")], iof(X("coF", 2560), [[1, 128]], 2560))
+        gop(256, [], [K("su2")], ioi(X("suI", 2560), [[0, 256]], 0, 0))
+        gop(128, [], [K("Fc")], iof(X("Fc"), [[0, 128]], 0))
+        gop(1536, [], [K("Fs")], iof(X("Fs", 1024, 2560), [[0, 1536]], 0))
+        vop(1536, [], [K("Fv0")], fill(X("Fv0", 1024, 2560), 0.0), 0.5)
+        gop(1536, [], [K("Fv1")], iof(X("Fv1", 1024, 2560), [[0, 1536]], 0))
+        vop(8, ["p16", "p128", "onesF"], [K("Rw2")], ts(X("Rw", 128), T.onesF[:, 0:8], pF(0), 8.0, OP.add, OP.mult))
+        sop(8, [K("Rw2"), "p128"], [K("Rw2")], act(X("Rw", 128), X("Rw", 128), AF.Identity, bias=pF(5)))
+    pop(512, ["gT_0", "gT_1", "thF"], ["P3"], [mm(T.P3[:, s:s + 1], T.gT[0:8, 128 * s:128 * s + 128], T.thF[0:8, 0:1], True, True) for s in sets])
+    vop(2, [], ["th16", "P3"], ts(T.th16[:, 0:2], T.P3[:, 0:2], 16.0, -1.0 * MID, OP.mult, OP.add))
+    vop(2, ["th16"], ["thr"], cp(T.thr[:, 0:2], T.th16[:, 0:2]))
+    for t in range(R):
+        gop(128, [], ["stv%d" % t], iof(T.stv[:, 128 * t:128 * t + 128], [[0, 128]], 32 * 8 ** t))
+        gop(128, [], ["sts%d" % t], iof(T.sts[:, 128 * t:128 * t + 128], [[0, 128]], 32 * 8 ** t))
 
     def send(dst_rank, out, in_, sem, r):
         dst = T.cores[dst_rank]
@@ -230,210 +296,222 @@ def rank_program(g, core, T, topo):
         i = send((rank + t) % N, T.dls[:, 256 * t:256 * t + 256], T.dls[:, 0:256], "rdl%d" % t, ["dl0"])
         op("R", 4.0, [], ["dl%d" % t], [], "rdl%d" % t, 4, True, order=[i])
     for k in range(16):
-        if k % 2:
+        if k % 3:
             vop(256, ["dl0"], ["sh0_%d" % k], cp(T.sh0[:, k::16], T.dls[:, 0:256]), 0.5)
         else:
             sop(256, ["dl0"], ["sh0_%d" % k], act(T.sh0[:, k::16], T.dls[:, 0:256], AF.Copy))
-    hs = (0, 1)
-    for q, nm in enumerate(("laI", "lbI")):
-        vop(16, [nm], ["abI%d" % q], cp(T.abI[:, 16 * q:16 * q + 16], T[nm][:]))
-    cur, co_, cur_t = T.abI, 0, ["abI0", "abI1"]
+
+    def lanes(t, s):
+        X, XP, K = own(s)
+        PK, PA, PB, PD = ("P%d" % (4 * s + i) for i in range(4))
+        sht = ["sh%d_%d" % (t % 2, k) for k in range(16)]
+        sh = lambda a, n: (T.sh0 if t % 2 == 0 else T.sh1)[:, 2048 * s + a:2048 * s + a + n]
+        cur = T.abI[:, 16 * s:16 * s + 16] if t == 0 else T.land[:, 32 * t - 32 + 16 * s:32 * t - 16 + 16 * s]
+        nxt = lambda a=0, b=16, p=slice(0, 128): T.abo[p, 32 * t + 16 * s + a:32 * t + 16 * s + b]
+        win = lambda lst, lo, q, n: X("Xw", 0, 2560).indirect(X(lst, lo + 32 * q, lo + 32 * (q + n)))
+        blk = lambda nm, q, n=1: [K("%s%d" % (nm, i)) for i in range(q, q + n)]
+        xt, turn = K("X"), [0]
+        co_t = blk("coa", 0, 2) + blk("cob", 0, 2)
+
+        def bank():
+            turn[0] += 1
+            return PD if turn[0] % 2 else PA
+
+        def first(step, lst, Mb):
+            path = CFG["first"][step]
+            for q, n in runs(path, "V", CFG["merge"]):
+                a, m = 512 * q, X(Mb, 512 * q, 512 * (q + n))
+                vg(512 * n, [xt, K(lst)] + sht, blk(Mb, q, n), tt(m, win(lst, 0, q, n), sh(a, 512 * n), OP.add))
+                vop(512 * n, blk(Mb, q, n), blk(Mb, q, n), ts(m, m, 0.0, 63.0, OP.max, OP.min), 0.5)
+            for q, n in runs(path, "S", 1):
+                a, P = 512 * q, bank()
+                sg(512, [xt, K(lst)], blk("gF", q), act(X("gF", a, a + 512), win(lst, 0, q, 1), AF.Copy))
+                pop(1024, ["ident"] + blk("gF", q) + sht, [P], [mm(T[P][:], T.ident[:], sh(a, 512), True, False), mm(T[P][:], T.ident[:], X("gF", a, a + 512), False, True)])
+                vop(512, [], [P] + blk(Mb, q), ts(X(Mb, a, a + 512), T[P][:], 0.0, 63.0, OP.max, OP.min))
+
+        def second(step, lst, lo, Mb):
+            path = CFG["second"][step]
+            for q, n in runs(path, "S", 1):
+                a, P = 512 * q, bank()
+                sg(512, [xt, K(lst)], blk("gF", q), act(X("gF", a, a + 512), win(lst, lo, q, 1), AF.Copy))
+                one = (mm(T[P][:], T.ident[:], X("gF", a, a + 512), step == 1, step == 2), ["ident"] + blk("gF", q))
+                two = (mm(T[P][:], T.nident[:], X(Mb, a, a + 512), step == 2, step == 1), ["nident"] + blk(Mb, q))
+                for f, r in (one, two) if step == 1 else (two, one):
+                    pop(512, r, [P], [f])
+                sop(512, [], [P] + blk("az", q), act(X("az", a, a + 512), T[P][:], AF.Abs))
+            for x, (q, n) in enumerate(runs(path, "V", 1)):
+                a, z = 512 * q, X("z", 512 * (x % 2), 512 * (x % 2) + 512)
+                vg(512, [xt, K(lst)] + blk(Mb, q), blk("z", x % 2), tt(z, win(lst, lo, q, 1), X(Mb, a, a + 512), OP.subtract))
+                sop(512, blk("z", x % 2), blk("az", q), act(X("az", a, a + 512), z, AF.Abs))
+
+        vop(16, [K("ab%d" % t)], [K("abU")], cp(X("abU"), cur))
+        vg(256, [K("abU")] + co_t, [K("df")], cp(X("df"), X("coF", 0, 2560).indirect(X("abU"))))
+        sg(256, [K("abU")] + co_t, [K("dfF")], act(X("dfF"), X("coF", 0, 2560).indirect(X("abU")), AF.Copy))
+        sop(256, [K("dfF")], [K("dfH")], act(X("dfH"), X("dfF"), AF.Identity, scale=0.03125, bias=159.515625))
+        P = T[PK]
+        pop(2048, cK_t + [K("dfH"), K("dfF")], [PK], [
+            mm(P[:], T.c32[0:64, :], T.cK[0:64, 0:512], True, False), mm(P[:, 128:256], X("dfF", 0, 128), T.id64F[:], False, False),
+            mm(P[:, 0:256], X("dfH", 0, 128), T.idC[:, 0:256], False, False), mm(P[:, 128:256], X("dfF", 128), T.identF[:], False, False),
+            mm(P[:, 128:384], X("dfH", 128), T.idC[:, 256:512], False, False)])
+        first(1, "df", "M")
+        second(1, "df", 128, "M")
+        pop(1024, blk("az", 0, 4) + g8p_t, [PK], [mm(P[:, k::16], X("az", k, None, 16), T.g8p[:, 0:32], False, k == 15) for k in range(16)])
+        vop(512, ["segN"], [K("S"), PK], scan(X("S"), T.segN[:], P[:], 1e9, OP.max, OP.min))
+        vg(512, [K("S"), "LE", "dm"], [K("B"), K("Bn")], tt(X("B"), X("S").indirect(T.LE[:]), T.dm[:], OP.mult))
+        P = T[PB]
+        pop(1280, [K("B"), K("Bn")] + gK_t + gB_t, [PB], [mm(P[:, 0:48], X("B", 384), T.gK[:], True, False)]
+            + [mm(P[:, 0:16], X("B", a, a + 128), T.gB[:, 16 * i:16 * i + 16], False, i == 3) for i, a in enumerate((0, 256, 128, 384))])
+        vop(8, [], [K("dL"), PB], cp(X("dL"), P[:, 0:8]))
+        vop(16, ["thr"], [K("al"), PB], ts(X("al"), P[:, 16:32], T.thr[:, s:s + 1], None, OP.is_lt))
+        vop(16, ["thr"], [K("alI"), PB], ts(X("alI"), P[:, 32:48], T.thr[:, s:s + 1], None, OP.is_lt))
+        vop(16, [K("alI"), "idx"], [K("alI")], tt(X("alI"), X("alI"), T.idx[:], OP.mult))
+        vop(8, [K("dL")], [K("dF")], cp(X("dF", 0, 8), X("dL")))
+        sop(8, [K("dF")], [K("d64")], act(X("d64"), X("dF", 0, 8), AF.Identity, scale=-64.0))
+        vop(8, [K("d64")], [K("fF"), PB], tt(X("dF", 8), P[:, 8:16], X("d64"), OP.add))
+        vop(16, [K("dF"), K("fF"), K("ab%d" % t)], [K("ta")], tt(X("ta"), X("dF"), cur, OP.subtract))
+        vop(16, [K("ta"), K("al")], [K("ta")], tt(X("ta"), X("ta"), X("al"), OP.mult))
+        vop(16, [K("ta"), K("ab%d" % t)], [K("abo%d" % t)], tt(nxt(), X("ta"), cur, OP.add))
+        if t < R - 1:
+            i = send((rank + 1) % N, T.land[:, 32 * t + 16 * s:32 * t + 16 * s + 16], nxt(), "rab%d%d" % (t + 1, s), [K("abo%d" % t)])
+            op("R", 4.0, [], [K("ab%d" % (t + 1))], [], "rab%d%d" % (t + 1, s), 4, True, order=[i])
+            sop(8, [K("al")], [K("acc"), "junk"], act(T.junk[:], X("al", 0, 8), AF.Copy, accum_out=T.acc[:, s:s + 1]))
+        else:
+            op("Y", 2.0, [K("abo%d" % t)], [], [(lambda y=y, q=q, u=u: g.sync.dma_start(y[half(s), 8 * u:8 * u + 8], nxt(8 * q, 8 * q + 8, half(u))))
+                                                for q, y in enumerate((T.ya, T.yb)) for u in (0, 1)], "so", 16, True)
+        if t < R - 1 and s == 1:
+            Q = T[PD]
+            pop(512, ["acc_0", "acc_1", "onesF"], [PD], [mm(Q[:, 0:1], T.onesF[:], T.acc[:, x:x + 1], x == 0, x == 1) for x in sets])
+            vop(1, [], ["acI", PD], ts(T.acJ[:, 0:1], Q[:, 0:1], -16.0, 32768.0, OP.mult, OP.add))
+            vop(1, ["acI"], ["acJ"], ts(T.acJ[:, 8:9], T.acJ[:, 0:1], 1008, None, OP.bitwise_and))
+            vop(1, ["acJ"], ["acF"], cp(T.acc[:, 4:5], T.acJ[:, 8:9]))
+            sop(2, ["acF", "th16"], ["thr"], act(T.thr[:, 0:2], T.th16[:, 0:2], AF.Identity, bias=T.acc[:, 4:5]))
+        Pk = T[PK]
+        vg(128, [K("al"), "LX", "dmr"], [K("sp")], tt(X("sp"), X("al").indirect(T.LX[:]), T.dmr[:], OP.mult))
+        pop(128, [K("sp"), "grp"], [PK], [mm(Pk[:, 0:128], T.grp[:], X("sp"), True, False)])
+
+        vg(128, [K("dL"), K("su")], [K("sT")], cp(X("sT"), X("suI", 0, 2560).indirect(X("dL"))))
+        first(2, "sT", "E")
+        P = T[PB]
+        for x in (0, 1):
+            pop(1024, blk("E", 2 * x, 2) + [K("WT")], [PB], [mm(P[:, 64 + 64 * x:128 + 64 * x], X("WT", 128 * j, 128 * j + 128), X("E", 1024 * x + j, 1024 * x + 1024, 16), j == 0, j == 15) for j in range(16)])
+        vop(128, [], [K("uI"), PB], cp(X("uI"), P[:, 64:192]))
+        vop(128, [K("uI")], [K("uI")], ts(X("uI"), X("uI"), 4095, None, OP.bitwise_and))
+        vop(128, [K("uI")], [K("uB")], ts(X("uB"), X("uI"), 1184.0, None, OP.add))
+        vop(128, [K("uI"), K("uB")], [K("uA")], tt(X("uA"), X("uI"), X("uB"), OP.mult), 2)
+        vop(128, [K("uA")], [K("uI")], ts(X("uI"), X("uA"), 5, 1023, OP.arith_shift_right, OP.bitwise_and))
+        vop(128, [K("uI")], [K("nO")], cp(X("nO"), X("uI")))
+        vop(128, [K("uI")], [K("nP")], cp(X("nP"), X("uI")))
+        pop(768, [K("nP"), "identF", "c32", "cK8"], [PB], [mm(P[:, 256:512], T.c32[0:32, :], T.cK[0:32, 512:768], True, False), mm(P[:, 256:384], X("nP"), T.identF[:], False, False)])
+        second(2, "nO", 0, "E")
+        pop(1024, blk("az", 0, 4) + g8p_t, [PB], [mm(P[:, 256 + j:512:16], X("az", j, None, 16), T.g8p[:, 32:48], False, j == 15) for j in range(16)])
+        vop(256, ["segX"], [K("S"), PB], scan(X("S", 0, 256), T.segX[:], P[:, 256:512], 0.0, OP.min, OP.max))
+        vg(256, [K("S"), "LE", "dm"], [K("B")], tt(X("B", 0, 256), X("S", 0, 256).indirect(T.LE[:, 0:16]), T.dm[:, 0:256], OP.mult))
+        sg(256, [K("S"), "LE"], [K("Bn")], act(X("B", 256), X("S", 0, 256).indirect(T.LE[:, 0:16]), AF.Copy))
+        Q = T[PA]
+        pop(512, [K("B"), "gN0", "gN1", "gN2"] + gK_t, [PA], [mm(Q[:, 0:24], X("B", 128, 256), T.gN[:], True, False), mm(Q[:, 0:16], X("B", 0, 128), T.gK[:, 32:48], False, True)])
+        pop(1024, [K("Bn"), "anti0", "anti1"], [PK], [mm(Pk[:, 0:128], X("B", 384), T.antiF[:, 128:256], False, False), mm(Pk[:, 0:128], X("B", 256, 384), T.antiF[:, 0:128], False, True)])
+        vop(16, [K("alI")], [K("nS"), PA], tt(X("nS"), Q[:, 0:16], X("alI"), OP.max))
+        vop(8, [], [K("jI"), PA], cp(X("jI"), Q[:, 16:24]))
+        vop(8, [K("jI")], [K("jI")], ts(X("jI"), X("jI"), 10, 15, OP.logical_shift_right, OP.bitwise_and))
+        vop(8, [K("jI"), "EB"], [K("jI")], tt(X("jI"), T.EB[:], X("jI"), OP.subtract))
+        vop(8, [K("jI")], [K("eO")], cp(X("eO"), X("jI")))
+        sg(128, blk("E", 0, 4) + [K("eO")], [K("eS")], act(X("eS"), X("E").indirect(X("eO")), AF.Copy))
+        vop(16, [K("nS")], [K("oD")], cp(X("oD"), X("nS")))
+        sg(256, [K("oD"), K("co2")] + co_t, [K("T1")], act(X("T1"), X("coF").indirect(X("oD")), AF.Copy))
+        vop(256, [K("T1")], [K("T2")], lambda: V.transpose(X("T2"), X("T1")))
+        for c in range(8):
+            a, n = 8 * c * (c + 1), 16 * (c + 1)
+            vop(n, [K("nS")], [PK, K("EQ%d" % c)], ts(X("EQ", a, a + n), Pk[:, 128 - n:128], X("nS", 2 * c, 2 * c + 1), None, OP.is_equal))
+        vop(576, blk("EQ", 0, 8) + mE_t, [K("EK")], scan(X("EK"), X("EQ"), T.mE[:], 0.0, OP.max, OP.min), 0.5)
+        vg(128, [K("EK"), "LD", "idxR"], [K("nt")], tt(X("nt"), X("EK").indirect(T.LD[:]), T.idxR[:], OP.mult))
+        vg(128, [K("T2"), "LP", K("nt")], [K("fm")], tt(X("fm"), X("T2").indirect(T.LP[:]), X("nt"), OP.max))
+        vop(128, [K("fm")], [K("fL")], cp(X("fL"), X("fm")))
+        vop(8, [K("nt"), K("nS")], [K("nl")], tt(X("nl"), X("nt", 0, 8), X("nS", 0, None, 2), OP.max))
+        for k in range(16):
+            off = X("fL", 8 * k, 8 * k + 8)
+            if k < CFG["flagS"]:
+                sop(128, [K("fL"), "sts%d" % t], [K("Fs")], act(X("Fs").indirect(off), T.sts[:, 128 * t:128 * t + 128], AF.Silu), SC)
+            else:
+                nm = "Fv%d" % (k % 2)
+                vop(128, [K("fL"), "stv%d" % t], [K(nm)], cp(X(nm).indirect(off), T.stv[:, 128 * t:128 * t + 128]), SC)
+
+        pop(768, [K("eS"), K("nl"), "dupB", "dupF0", "dupF1"], [PA],
+            [mm(Q[:, 128 * u:128 * u + 128], T.dupB[:, 128 * u:128 * u + 128], X("eS"), True, True) for u in (0, 1)]
+            + [mm(Q[:, 256 + 8 * u:264 + 8 * u], T.dupF[:, 128 * u:128 * u + 128], X("nl"), True, True) for u in (0, 1)])
+        sop(256, [], [PA, K("eD")], act(X("eD"), Q[:, 0:256], AF.Copy))
+        vop(16, [], [PA, K("oU")], cp(X("oU"), Q[:, 256:272]))
+        for u in (0, 1):
+            vop(128, [K("eD"), K("oU")], [xt], cp(X("Xw").indirect(X("oU", 8 * u, 8 * u + 8)), X("eD", 128 * u, 128 * u + 128)), SC)
+        if t == R - 1:
+            op("Y", 3.0, [xt], [], [(lambda u=u: g.sync.dma_start(T.yx[half(s), 512 * u:512 * u + 512], XP(64 * u, "Xw", 512 * u, 512 * u + 512))) for u in (0, 1)], "sb%d" % s, 16, True)
+
+        F = lambda nm, o, w, last: [mm(P[:, 128 + m:256:16], X(nm, o + m, o + 1536, 12), w, False, last and m == 11) for m in range(12)]
+        pop(128, [K("Fc"), "idBig"], [PB], [mm(P[:, 128:256], T.idBig[:], X("Fc"), True, False)])
+        pop(768, [K("Fv0"), "g4B"], [PB], F("Fv0", 1024, T.g4B[:], False))
+        if CFG["conv"] == "PE":
+            pop(3072, [K("Fs"), "g4F0", "g4F1"], [PB], F("Fs", 1024, T.g4F[:], False))
+        pop(768, [K("Fv1"), "g4B"], [PB], F("Fv1", 1024, T.g4B[:], CFG["conv"] == "PE"))
+        if CFG["conv"] != "PE":
+            if CFG["conv"] == "G":
+                gop(1536, [K("Fs")], blk("gF", 0, 3), sel(X("gF", 0, 1536), X("Fs", 1024, 2560), [[0, 1536]], OP.is_ge, 1, 0))
+            else:
+                sop(1536, [K("Fs")], blk("gF", 0, 3), act(X("gF", 0, 1536), X("Fs", 1024, 2560), AF.Copy))
+            pop(768, blk("gF", 0, 3) + ["g4B"], [PB], F("gF", 0, T.g4B[:], True))
+        vop(128, [], [K("Fp"), PB], ts(X("Fp"), P[:, 128:256], 448.0 * 8 ** t, None, OP.is_ge))
+        vop(128, [K("Fp"), "seg1"], [K("Fi")], scan(X("Fi"), T.seg1[:], X("Fp"), 0.0, OP.mult, OP.add), 0.5)
+        pop(64, [K("Fi"), "triI"], [PA], [mm(Q[:, 0:8], T.triI[:], X("Fi", 15, None, 16), True, True)])
+        if CFG["cum"]:
+            vop(8, [], [K("cum"), PA], cp(X("cum"), Q[:, 0:8]))
+        for G in range(8):
+            c = X("cum", G, G + 1) if CFG["cum"] else Q[:, G:G + 1]
+            vop(128, [K("cum"), "iotaB"], [K("Th%d" % G)] + [PA] * (not CFG["cum"]), ts(X("Th", 128 * G, 128 * G + 128), T.iotaB[:, 128 * (G // 4):128 * (G // 4) + 128], c, None, OP.is_ge), 0.5)
+        pop(512, blk("Th", 0, 8) + ["onesB"], [PA], [mm(Q[:, 8 + q:9 + q], X("Th", q, None, 8), T.onesB[:, 0:1], True, True) for q in range(8)])
+        vop(8, [], [K("cL"), PA], cp(X("cL"), Q[:, 8:16]))
+        pop(1088, blk("Th", 0, 8) + ["w12", "c1k", "ident"], [PB], [mm(P[:, 0:8], T.ident[:], T.c1k[:], True, False)]
+            + [mm(P[half(u), q:q + 1], X("Th", 512 * u + q, 512 * u + 512, 8), T.w12[:, 8 * u + q:8 * u + q + 1], False, False) for u in (0, 1) for q in range(8)])
+        sg(128, [K("Fi"), "LE"], [K("tot")], act(X("tot"), X("Fi").indirect(T.LE[:, 0:8]), AF.Copy))
+        D = T[PD]
+        pop(256, [K("Fi"), K("tot"), "ident", "triS"], [PD], [mm(D[:, 0:128], X("Fi"), T.ident[:], True, False), mm(D[:, 0:128], X("tot"), T.triS[:], False, True)])
+        sop(128, [], [PD, K("Rw")], act(X("Rw", 0, 128), D[:, 0:128], AF.Copy))
+        vg(128, [K("Rw"), K("Rw2"), K("cL"), "rk"], [K("D")], tt(X("D"), X("Rw").indirect(X("cL")), T.rk[:], OP.is_le))
+        pop(1024, [K("D"), "selX"], [PB], [mm(P[:, 0:8], T.selX[:, 128 * p:128 * p + 128], X("D", p, None, 16), False, p == 15) for p in range(16)])
+        vop(8, [], [K("vL"), PB], cp(X("vL"), P[:, 0:8]))
+        vg(128, [K("vL"), K("su"), K("su2")], [K("sR")], cp(X("sR"), X("suI").indirect(X("vL"))))
+        sop(8, [], [K("vF"), PB], act(X("vF"), P[:, 0:8], AF.Copy))
+        if t < R - 1:
+            pop(384, [K("Fi"), K("tot"), K("Fp"), "ident", "triS", "id4k"], [PD], [
+                mm(D[:, 128:256], T.ident[:], X("Fi"), True, False), mm(D[:, 128:256], T.triS[:], X("tot"), False, False), mm(D[:, 128:256], T.id4k[:], X("Fp"), False, True)])
+            sop(128, [], [PD, K("Fc")], act(X("Fc"), D[:, 128:256], AF.Relu, bias=-4352.0))
+        pop(512, [K("vF"), "dupF0", "dupF1"], [PD], [mm(D[:, 256 + 8 * u:264 + 8 * u], T.dupF[:, 128 * u:128 * u + 128], X("vF"), True, True) for u in (0, 1)])
+        vop(16, [], [PD, K("vD")], cp(X("vD"), D[:, 256:272]))
+        for e in "SV":
+            for q, n in runs(CFG["renew"], e, 1):
+                a, b = 512 * q, 512 * (q + n)
+                if e == "S":
+                    sg(512 * n, [xt, K("sR")], blk("gF", q, n), act(X("gF", a, b), win("sR", 0, q, n), AF.Copy))
+                else:
+                    vg(512 * n, [xt, K("sR")], blk("gF", q, n), cp(X("gF", a, b), win("sR", 0, q, n)))
+        for q, n in CFG["scans"]:
+            a, b = 512 * q, 512 * (q + n)
+            vop(512 * n, blk("gF", q, n) + ["rX0", "rX1"], blk("E", q, n), scan(X("E", a, b), T.rX[:, 0:b - a], X("gF", a, b), 0.0, OP.min, OP.max), 0.5)
+            vop(512 * n, blk("gF", q, n) + ["rN0", "rN1"], blk("az", q, n), scan(X("az", a, b), T.rN[:, 0:b - a], X("gF", a, b), 64.0, OP.max, OP.min), 0.5)
+        pop(512, blk("E", 0, 4) + blk("az", 0, 4) + ["dupB"], [PA],
+            [mm(Q[:, 128 * u:128 * u + 128], T.dupB[:, 128 * u:128 * u + 128], X(nm, 15, None, 16), nm == "E", nm == "az") for u in (0, 1) for nm in ("E", "az")])
+        vop(256, [], [K("rI"), PA], ts(X("rI"), Q[:, 0:256], 0.5, -0.25, OP.mult, OP.add))
+        vop(256, [K("rI"), K("vD")], [xt], cp(X("Xw").indirect(X("vD")), X("rI")), SC)
+        if t == R - 1:
+            op("Y", 3.0, [xt], [], [(lambda u=u: g.sync.dma_start(T.yx[half(s), 1024 + 768 * u:1792 + 768 * u], XP(64 * u, "Xw", 1024 + 768 * u, 1792 + 768 * u))) for u in (0, 1)], "so", 16, True)
 
     for t in range(R):
-        sh = T.sh0 if t % 2 == 0 else T.sh1
-        sht = ["sh%d_%d" % (t % 2, k) for k in range(16)]
         if t:
             for k in range(16):
-                gop(256, ["dl%d" % t], [sht[k]], sel(sh[:, k::16], T.dls[:, 256 * t:256 * t + 256], [[0, 256]], OP.is_ge, 1, 0))
-        no = 32 * t
-        vop(32, cur_t, ["abU"], cp(T.abU[:], cur[:, co_:co_ + 32]))
-        vg(512, ["abU"] + co_t, ["df"], cp(T.df[:], T.coI[:].indirect(T.abU[:])))
-        for nm in ("H", "F"):
-            sg(512, ["abU", "co%s0" % nm, "co%s1" % nm], ["df" + nm], act(T["df" + nm][:], T["co" + nm][:, 0:2560].indirect(T.abU[:]), AF.Copy))
-
-        def second(step, h, q, lists, lo, Mb, mt, lt):
-            a, zt = 2048 * h + 512 * q, "z%d%d" % (h, q)
-            win = T.Xw[:, 0:2560].indirect(lists[:, lo + 32 * q:lo + 32 * q + 32])
-            if q in SPATH[step][h]:
-                gt, P = "gF%d%d" % (h, q), "P%d" % bank()
-                sg(512, x_t + [lt], [gt], act(T.gF[:, a:a + 512], win, AF.Copy))
-                pop(1024, ["ident", "nident", gt, mt], [P], [mm(T[P][:], T.nident[:], Mb[:, a:a + 512], True, False), mm(T[P][:], T.ident[:], T.gF[:, a:a + 512], False, True)])
-                sop(512, [], [P, "a" + zt], act(T.az[:, a:a + 512], T[P][:], AF.Abs))
-            else:
-                vg(512, x_t + [lt, mt], [zt], tt(T.z[:, a:a + 512], win, Mb[:, a:a + 512], OP.subtract))
-                sop(512, [zt], ["a" + zt], act(T.az[:, a:a + 512], T.z[:, a:a + 512], AF.Abs))
-
-        def moved(step, h, q, lists, lo, lt, Mb, mt):
-            a = 2048 * h + 512 * q
-            win = T.Xw[:, 0:2560].indirect(lists[:, lo + 32 * q:lo + 32 * q + 32])
-            if q in MPATH[step][h]:
-                gt, P = "gF%d%d" % (h, q), "P%d" % bank()
-                sg(512, x_t + [lt], [gt], act(T.gF[:, a:a + 512], win, AF.Copy))
-                pop(1024, ["ident", gt] + sht, [P], [mm(T[P][:], T.ident[:], sh[:, a:a + 512], True, False), mm(T[P][:], T.ident[:], T.gF[:, a:a + 512], False, True)])
-                vop(512, [], [P, mt], ts(Mb[:, a:a + 512], T[P][:], 0.0, 63.0, OP.max, OP.min))
-                return
-            vg(512, x_t + [lt] + sht, [mt], tt(Mb[:, a:a + 512], win, sh[:, a:a + 512], OP.add))
-            vop(512, [mt], [mt], ts(Mb[:, a:a + 512], Mb[:, a:a + 512], 0.0, 63.0, OP.max, OP.min), 0.5)
-
-        for h in hs:
-            X = lambda n, a=0, b=None, s=1, h=h: T[n][:, h * HALF[n] + a:h * HALF[n] + (HALF[n] if b is None else b):s]
-            K = lambda n, h=h: "%s_%d" % (n, h)
-            b, a0 = 128 * h, 2048 * h
-            for q in range(4):
-                moved(1, h, q, T.df, b, "df", T.M, "M%d%d" % (h, q))
-            for q in range(4):
-                second(1, h, q, T.df, b + 256, T.M, "M%d%d" % (h, q), "df")
-            azt = ["az%d%d" % (h, q) for q in range(4)]
-            for P, w, c0, d in (("P0", 384, 0, b), ("P1", 256, 384, b + 256)):
-                lh, lf = T.dfH[:, d:d + 128], T.dfF[:, d:d + 128]
-                pop(w + 768, ["ident", "identF", "nid32", "cK", "dfH", "dfF"], [P], [
-                    mm(T[P][:, 0:w], T.ident[:], T.cK[:, c0:c0 + w], True, False), mm(T[P][:, 0:128], lh, T.ident[:], False, False),
-                    mm(T[P][:, 128:256], lf, T.identF[:], False, False), mm(T[P][:, 128:256], lh, T.nid32[:], False, False)])
-            l = [T.az[:, a0 + k:a0 + 2048:16] for k in range(16)]
-            pop(1024, azt + ["g8p"], ["P0"], [mm(T.P0[:, k:384:16], l[k], T.g8p[:, 0:24], False, k == 15) for k in range(16)])
-            pop(1024, azt + ["g8p"], ["P1"], [mm(T.P1[:, k:256:16], l[k], T.g8p[:, 24:40], False, k == 15) for k in range(16)])
-            vop(384, ["segN"], [K("S") + "a", "P0"], scan(X("S", 0, 384), T.segN[:, 0:384], T.P0[:, 0:384], 1e9, OP.max, OP.min))
-            vg(384, [K("S") + "a", "LE", "dm"], [K("B")], tt(X("B", 0, 384), X("S", 0, 384).indirect(T.LE[:, 0:24]), T.dm[:, 0:384], OP.mult))
-            vop(256, ["segN"], [K("S") + "b", "P1"], scan(X("S", 384), T.segN[:, 0:256], T.P1[:, 0:256], 1e9, OP.max, OP.min))
-            vg(256, [K("S") + "b", "LE", "dm"], [K("B") + "b"], tt(X("B", 384), X("S", 384).indirect(T.LE[:, 0:16]), T.dm[:, 0:256], OP.mult))
-            c32, c41, c1 = T.g8s[:, 0:8], T.g8s[:, 8:16], T.g8s[:, 16:24]
-            blk = [X("B", 128 * i, 128 * i + 128) for i in range(5)]
-            pd, pf, pk = T.P2[:, 8 * h:8 * h + 8], T.P3[:, 8 * h:8 * h + 8], T.P3[:, 16 + 8 * h:24 + 8 * h]
-            pop(768, [K("B"), "g8s"], ["P2"], [mm(pd, blk[0], c32, True, False), mm(pd, blk[2], c41, False, False), mm(pd, blk[1], c1, False, True)])
-            pop(1024, [K("B"), K("B") + "b", "g8s"], ["P3"], [mm(pf, blk[3], c32, True, False), mm(pf, blk[2], c41, False, False), mm(pf, blk[4], c1, False, True), mm(pk, blk[2], c1, True, True)])
-            vop(8, [], [K("dL"), "P2"], cp(X("dL"), pd))
-        vop(16, ["thr"], ["al", "P3"], ts(T.al[:], T.P3[:, 16:32], T.thr[:, 0:1], None, OP.is_lt))
-        for q, P in ((0, "P2"), (1, "P3")):
-            tq = T.ta[:, 16 * q:16 * q + 16]
-            vop(16, cur_t, ["ta%d" % q, P], tt(tq, T[P][:, 0:16], cur[:, co_ + 16 * q:co_ + 16 * q + 16], OP.subtract))
-            vop(16, ["ta%d" % q, "al"], ["ta%d" % q], tt(tq, tq, T.al[:], OP.mult))
-        vop(32, ["ta0", "ta1"] + cur_t, ["abo%d" % t], tt(T.abo[:, no:no + 32], T.ta[:], cur[:, co_:co_ + 32], OP.add))
-        if t < R - 1:
-            i = send((rank + 1) % N, T.land[:, no:no + 32], T.abo[:, no:no + 32], "rab%d" % (t + 1), ["abo%d" % t])
-            op("R", 4.0, [], ["land%d" % (t + 1)], [], "rab%d" % (t + 1), 4, True, order=[i])
-            vop(16, ["al"], ["acc"], lambda: V.tensor_reduce(T.acc[:, 0:1], T.al[:], AxisListType.X, OP.add))
-            pop(256, ["acc", "onesF"], ["P3"], [mm(T.P3[:, 32:33], T.onesF[:], T.acc[:, 0:1], True, True)])
-            vop(1, [], ["acI", "P3"], ts(T.acJ[:, 0:1], T.P3[:, 32:33], -1.0, 2048.0, OP.mult, OP.add))
-            vop(1, ["acI"], ["acJ"], ts(T.acJ[:, 8:9], T.acJ[:, 0:1], 63, None, OP.bitwise_and))
-            vop(1, ["acJ", "th16"], ["thr"], ts(T.thr[:, 0:1], T.acJ[:, 8:9], 16.0, T.th16[:, 0:1], OP.mult, OP.add))
-        else:
-            for q, y in enumerate((T.ya, T.yb)):
-                u = no + 16 * q
-                op("Y", 2.0, ["abo%d" % t], [], [lambda y=y, u=u: g.sync.dma_start(y[:], T.abo[:, u:u + 16])], "so", 16, True)
-
-        for h in hs:
-            X = lambda n, a=0, b=None, s=1, h=h: T[n][:, h * HALF[n] + a:h * HALF[n] + (HALF[n] if b is None else b):s]
-            K = lambda n, h=h: "%s_%d" % (n, h)
-            a0 = 2048 * h
-            vg(128, [K("dL")] + su_t[:2], [K("sT")], cp(X("sT"), T.suI[:, 0:2560].indirect(X("dL"))))
-            for q in range(4):
-                moved(2, h, q, T.sT, 128 * h, K("sT"), T.E, "E%d%d" % (h, q))
-            et, azt = ["E%d%d" % (h, q) for q in range(4)], ["az%d%d" % (h, q) for q in range(4)]
-            for x in (0, 1):
-                pop(1024, et[2 * x:2 * x + 2] + ["WT"], ["P4"], [mm(T.P4[:, 64 * x:64 * x + 64], T.WT[:, 128 * j:128 * j + 128], T.E[:, a0 + 1024 * x + j:a0 + 1024 * x + 1024:16], j == 0, j == 15) for j in range(16)])
-            vop(128, [], [K("uI"), "P4"], cp(X("uI"), T.P4[:, 0:128]))
-            vop(128, [K("uI")], [K("uI")], ts(X("uI"), X("uI"), 4095, None, OP.bitwise_and))
-            vop(128, [K("uI")], [K("uA")], ts(X("uA"), X("uI"), -2048.0, None, OP.add))
-            vop(128, [K("uI")], [K("uB")], ts(X("uB"), X("uI"), 3232.0, None, OP.add))
-            vop(128, [K("uA"), K("uB")], [K("uA")], tt(X("uA"), X("uA"), X("uB"), OP.mult), 2)
-            vop(128, [K("uA")], [K("uI")], ts(X("uI"), X("uA"), 5, 1023, OP.arith_shift_right, OP.bitwise_and))
-            vop(128, [K("uI")], [K("nO")], cp(X("nO"), X("uI")))
-            vop(128, [K("uI"), "pFn"], [K("nP")], ts(X("nP"), X("uI"), T.pF[:, 6:7], None, OP.add))
-            for q in range(4):
-                second(2, h, q, T.nO, 128 * h, T.E, "E%d%d" % (h, q), K("nO"))
-            pop(512, [K("nP"), "identF"], ["P1"], [mm(T.P1[:, 256:384], X("nP"), T.identF[:], True, False)])
-            pop(1024, azt + ["g8p"], ["P1"], [mm(T.P1[:, 256 + j:384:16], T.az[:, a0 + j:a0 + 2048:16], T.g8p[:, 40:48], False, j == 15) for j in range(16)])
-            vop(128, ["segX"], [K("S") + "a", "P1"], scan(X("S", 0, 128), T.segX[:], T.P1[:, 256:384], 0.0, OP.min, OP.max))
-            vg(128, [K("S") + "a", "LE", "dm"], [K("B")], tt(X("B", 0, 128), X("S", 0, 128).indirect(T.LE[:, 0:8]), T.dm[:, 0:128], OP.mult))
-            pop(256, [K("B"), "g8"], ["P2"], [mm(T.P2[:, 16:24], X("B", 0, 128), T.g8[:], True, True)])
-            vop(8, [], [K("vI"), "P2"], cp(X("vI"), T.P2[:, 16:24]))
-            vop(8, [K("vI")], [K("nI")], ts(X("nI"), X("vI"), 1023, None, OP.bitwise_and))
-            vop(8, [K("vI")], [K("jI")], ts(X("jI"), X("vI"), 10, 15, OP.logical_shift_right, OP.bitwise_and))
-            vop(8, [K("jI"), "EB"], [K("jI")], tt(X("jI"), T.EB[:], X("jI"), OP.subtract))
-            vop(8, [K("jI")], [K("eO")], cp(X("eO"), X("jI")))
-            sg(128, et + [K("eO")], [K("eS")], act(X("eS"), T.E[:, a0:a0 + 2048].indirect(X("eO")), AF.Copy))
-            vop(8, [K("nI"), "idx"], [K("nt")], tt(X("nt"), T.idx[:], X("nI"), OP.subtract))
-            vop(8, [K("nt"), "al"], [K("nt")], tt(X("nt"), X("nt"), T.al[:, 8 * h:8 * h + 8], OP.mult))
-            vop(8, [K("nt"), K("nI")], [K("nS")], tt(X("nS"), X("nI"), X("nt"), OP.add))
-            sg(128, [K("S") + "a", "LE"], [K("nBs")], act(X("nBs"), X("S", 0, 128).indirect(T.LE[:, 0:8]), AF.Copy))
-            pop(512, [K("nBs"), "identF"], ["P2"], [mm(T.P2[:, 128:256], X("nBs"), T.identF[:], True, True)])
-            vop(128, [], [K("uA"), "P2"], cp(X("uA"), T.P2[:, 128:256]))
-            vop(128, [K("uA")], [K("uA")], ts(X("uA"), X("uA"), 1023, None, OP.bitwise_and))
-            eqt = ["EQ%d%d" % (h, i) for i in range(8)]
-            vg(128, [K("nS"), "LX", K("uA")], [eqt[7]], tt(X("EQ", 896), X("nS").indirect(T.LX[:]), X("uA"), OP.is_equal))
-            vop(128, [eqt[7], "ltm"], [eqt[7]], tt(X("EQ", 896), X("EQ", 896), T.ltm[:], OP.mult), 2)
-            fs = [mm(T.P3[:, 128:256], T.grp[:], X("EQ", 896), True, False)]
-            for c in range(7):
-                s = 16 * (c + 1)
-                e = X("EQ", 128 * c + s, 128 * c + 128)
-                vop(128 - s, [K("nS"), K("uA")], [eqt[c]], ts(e, X("uA", s), X("nS", c, c + 1), None, OP.is_equal))
-                fs.append(mm(T.P3[:, 128 + s:256], T.grp[:], e, False, c == 6))
-            pop(640, eqt + ["grp"], ["P3"], fs)
-            vop(128, ["dmI"], [K("B"), "P3"], tt(X("B", 0, 128), T.P3[:, 128:256], T.dmI[:], OP.mult))
-            vop(128, [K("B"), "seg1"], [K("S") + "b"], scan(X("S", 512), T.seg1[:, 0:128], X("B", 0, 128), 0.0, OP.mult, OP.add))
-            vop(8, [K("S") + "b", K("nS")], [K("nl")], tt(X("nl"), X("S", 527, 640, 16), X("nS"), OP.max))
-            vop(8, [K("nl"), "idx"], [K("nl")], tt(X("nl"), X("nl"), T.idx[:], OP.min))
-            for x in (0, 1):
-                vop(8, [K("nl")], [K("oD%d" % x)], cp(X("oD", x, 16, 2), X("nl")))
-            vop(8, [K("nl")], [K("oU")], cp(X("oU"), X("nl")))
-            sg(256, [K("oD0"), K("oD1"), "coF0", "coF1", "coF2"], [K("T1")], act(X("T1"), T.coF[:].indirect(X("oD")), AF.Copy))
-            vop(256, [K("T1")], [K("T2")], lambda X=X: V.transpose(X("T2"), X("T1")))
-            vg(128, [K("T2"), "LP"], [K("fL")], cp(X("fL"), X("T2").indirect(T.LP[:])))
-            for k in range(16):
-                off = X("fL", 8 * k, 8 * k + 8)
-                if k in FLAG_S[h]:
-                    sop(128, [K("fL"), "sts%d" % t], ["Fs%d" % h], act(T["Fs%d" % h][:].indirect(off), T.sts[:, 128 * t:128 * t + 128], AF.Silu), SC)
-                else:
-                    vop(128, [K("fL"), "stv%d" % t], ["Fv"], cp(T.Fv[:].indirect(off), T.stv[:, 128 * t:128 * t + 128]), SC)
-            sop(1536, ["Fs%d" % h], ["FsB%d" % h], act(T["FsB%d" % h][:], T["Fs%d" % h][:, 1024:2560], AF.Copy))
-        for h in (1, 0):
-            vop(128, ["eS_%d" % h, "oU_%d" % h], x_t, cp(T.Xw[:].indirect(T.oU[:, 8 * h:8 * h + 8]), T.eS[:, 128 * h:128 * h + 128]), SC)
-
-        F = lambda src, o, first, last: [mm(T.P4[:, 256:352], T.selX[:, 128 * r:128 * r + 128], src[:, o + r:o + 1536:16], first and r == 0, last and r == 15) for r in range(16)]
-        pop(1632, ["FsB0", "selX", "Fc", "idBig"], ["P4"], F(T.FsB0, 0, True, False) + [mm(T.P4[:, 256:352], T.idBig[:], T.Fc[:], False, False)])
-        for x in (0, 1):
-            gop(256, [], ["Vw%d" % x], iof(T["Vw%d" % x][:, 0:256], [[1, 256]], 2560))
-        pop(1536, ["FsB1", "selX"], ["P4"], F(T.FsB1, 0, False, False))
-        pop(1536, ["Fv", "selX"], ["P4"], F(T.Fv, 1024, False, True))
-        vop(96, [], ["Fp", "P4"], ts(T.Fp[:], T.P4[:, 256:352], 384.0 * 8 ** t, None, OP.is_ge))
-        vop(96, ["Fp", "one96"], ["Fi"], scan(T.Fi[:], T.one96[:], T.Fp[:], 0.0, OP.mult, OP.add), 0.5)
-        p7 = T.P7[:, 0:96]
-        pop(288, ["Fp", "ident", "c4k", "nid4k", "ntri"], ["P7"], [mm(p7, T.ident[:], T.c4k[:], True, False), mm(p7, T.nid4k[:], T.Fp[:], False, False), mm(p7, T.ntri[:], T.Fp[:], False, False)])
-        pop(96, ["Fi", "grp"], ["P7"], [mm(p7, T.grp[:], T.Fi[:], False, True)])
-        vop(96, ["Ld1"], ["s96", "P7"], tt(T.s96[:], p7, T.Ld1[:], OP.min))
-        vop(96, ["s96"], ["Lv"], ts(T.Lv[:], T.s96[:], -1.0, None, OP.add))
-        vop(96, [], ["t96", "P7"], ts(T.t96[:], p7, 256.0, None, OP.is_le))
-        vop(768, ["Lv", "iotaV"], ["Vw0"], cp(T.Vw0[:].indirect(T.Lv[:, 0:48]), T.iotaV[:, 0:768]), SC)
-        sop(768, ["Lv", "iotaV"], ["Vw1"], act(T.Vw1[:].indirect(T.Lv[:, 48:96]), T.iotaV[:, 768:1536], AF.Silu), SC)
-        vop(96, ["t96", "Fp"], ["Fc"], tt(T.Fc[:], T.Fp[:], T.t96[:], OP.subtract), 2)
-        vop(256, ["Vw0", "Vw1"], ["vS"], tt(T.vS[:], T.Vw0[:, 0:256], T.Vw1[:, 0:256], OP.min), 2)
-        vop(256, ["vS", "dm"], ["vX"], tt(T.vX[:], T.vS[:], T.dm[:, 0:256], OP.mult), 2)
-        vop(256, ["vX", "seg1"], ["vS"], scan(T.vS[:], T.seg1[:], T.vX[:], 0.0, OP.mult, OP.add))
-        vop(16, ["vS"], ["vL"], cp(T.vL[:], T.vS[:, 15::16]))
-        vg(256, ["vL"] + su_t, ["sR"], cp(T.sR[:], T.suI[:].indirect(T.vL[:])))
-        for q in range(8):
-            a, h = 512 * q, q // 4
-            gt, zt, at = "gF%d%d" % (h, q % 4), "z%d%d" % (h, q % 4), "az%d%d" % (h, q % 4)
-            win = T.Xw[:, 0:2560].indirect(T.sR[:, 32 * q:32 * q + 32])
-            if q in REN_S:
-                sg(512, x_t + ["sR"], [gt], act(T.gF[:, a:a + 512], win, AF.Copy))
-            else:
-                vg(512, x_t + ["sR"], [gt], cp(T.gF[:, a:a + 512], win))
-            vop(512, [gt, "rX"], [zt], scan(T.z[:, a:a + 512], T.rX[:], T.gF[:, a:a + 512], 0.0, OP.min, OP.max), 0.5)
-            vop(512, [gt, "rN"], [at], scan(T.az[:, a:a + 512], T.rN[:], T.gF[:, a:a + 512], 64.0, OP.max, OP.min), 0.5)
-            if q % 4 == 3:
-                b = 2048 * h
-                vop(128, [x + "%d%d" % (h, i) for i in range(4) for x in ("z", "az")], ["rs%d" % h],
-                    tt(T.rs[:, 128 * h:128 * h + 128], T.z[:, b + 15:b + 2048:16], T.az[:, b + 15:b + 2048:16], OP.add), 2)
-        vop(256, ["rs0", "rs1"], ["rI"], ts(T.rI[:], T.rs[:], 0.5, -0.25, OP.mult, OP.add))
-        vop(256, ["rI", "vL"], x_t, cp(T.Xw[:].indirect(T.vL[:]), T.rI[:]), SC)
-        cur, co_, cur_t = T.land, no, ["land%d" % (t + 1)]
-    for a in (0, 1280):
-        op("Y", 4.0, x_t, [], [lambda a=a: g.sync.dma_start(T.yx[:, a:a + 1280], T.Xw[:, a:a + 1280])], "so", 16, True)
+                gop(256, ["dl%d" % t], ["sh%d_%d" % (t % 2, k)], sel((T.sh1 if t % 2 else T.sh0)[:, k::16], T.dls[:, 256 * t:256 * t + 256], [[0, 256]], OP.is_ge, 1, 0))
+        for s in sets:
+            lanes(t, s)
 
     if "o" not in ORDER:
         ORDER["o"], ORDER["start"], ORDER["end"] = schedule(ops)
-        ORDER["ops"] = [(o["e"], o["c"]) for o in ops]
+        ORDER["ops"] = ops
     queue = {"V": V, "S": S, "PE": PE, "G": g, "Y": g.sync}
     count, known = {}, {q: {} for q in queue}
     for i in ORDER["o"]:
@@ -464,4 +542,4 @@ def rank_program(g, core, T, topo):
     for s in SEMAPHORES:
         if count.get(s, 0) > known["Y"].get(s, 0):
             g.sync.wait_ge(T.sem[s], count[s])
-    g.wait_ge(T.sem.ls, 4 * 6)
+    g.wait_ge(T.sem.ls, 4 * 9)

@@ -2,26 +2,27 @@ from concourse.mybir import AluOpType as OP, ActivationFunctionType as AF
 
 R = 4
 MID = 8096
+WINDOWS = "AVB"
 SCRATCH = {}
 for _n, _w, _t in [
-        ("sh0", 4096, "bfloat16"), ("sh1", 4096, "bfloat16"), ("dls", 1024, "bfloat16"),
+        ("dls", 1024, "bfloat16"),
         ("ident", 128, "bfloat16"), ("nident", 128, "bfloat16"), ("idC", 512, "bfloat16"), ("idBig", 128, "bfloat16"), ("id4k", 128, "bfloat16"),
         ("identF", 128, "float32"), ("id64F", 128, "float32"), ("antiF", 256, "float32"), ("grp", 128, "bfloat16"), ("onesF", 128, "float32"), ("onesB", 128, "bfloat16"),
         ("c32", 128, "bfloat16"), ("cK", 768, "bfloat16"), ("selX", 2048, "bfloat16"),
         ("dupB", 256, "bfloat16"), ("dupF", 256, "float32"), ("triI", 128, "bfloat16"), ("triS", 128, "bfloat16"),
-        ("g8", 8, "float32"), ("g8p", 48, "bfloat16"), ("gK", 48, "float32"), ("gB", 64, "float32"), ("gN", 24, "float32"), ("g4B", 8, "bfloat16"), ("g4F", 8, "float32"),
-        ("jm", 512, "float32"), ("dm", 512, "float32"), ("dmr", 128, "float32"), ("segN", 512, "float32"), ("segX", 256, "float32"), ("seg1", 128, "bfloat16"),
+        ("g8", 8, "float32"), ("g8p", 48, "bfloat16"), ("g8n", 48, "bfloat16"), ("gK", 48, "float32"), ("gB", 64, "float32"), ("gN", 24, "float32"), ("g4B", 8, "bfloat16"), ("g4F", 8, "float32"),
+        ("jm", 512, "float32"), ("dm", 256, "float32"), ("dmr", 128, "float32"), ("segN", 512, "float32"), ("segX", 256, "float32"), ("seg1", 128, "bfloat16"),
         ("rN", 1024, "bfloat16"), ("rX", 1024, "bfloat16"), ("mE", 576, "bfloat16"), ("iotaB", 256, "bfloat16"), ("w12", 16, "bfloat16"), ("c1k", 8, "bfloat16"),
         ("rk", 128, "float32"), ("idx", 16, "float32"), ("idxR", 128, "float32"), ("EB", 8, "float32"), ("pI", 8, "int32"), ("pT", 64, "int32"), ("pF", 16, "float32"),
         ("eI", 64, "int32"), ("LE", 32, "uint16"), ("LX", 8, "uint16"), ("LP", 8, "uint16"), ("LD", 8, "uint16"),
-        ("stv", 512, "bfloat16"), ("sts", 512, "float32"), ("thI", 8, "int32"), ("thF", 8, "float32"), ("gT", 256, "float32"),
+        ("thI", 8, "int32"), ("thF", 8, "float32"), ("gT", 256, "float32"),
         ("thr", 8, "float32"), ("th16", 8, "float32"), ("acc", 8, "float32"), ("acJ", 16, "int32"), ("junk", 8, "float32"),
         ("abI", 32, "int32"), ("land", 96, "float32"), ("abo", 128, "float32")]:
     SCRATCH[_n] = ("sbuf", [128, _w], _t)
 OWN = {}
 for _n, _w, _t in [
-        ("Xw", 2816, "bfloat16"), ("coF", 2688, "float32"), ("suI", 2816, "int32"), ("Fv0", 2688, "bfloat16"), ("Fv1", 2688, "bfloat16"), ("Fs", 2688, "float32"),
-        ("M", 2048, "bfloat16"), ("E", 2048, "bfloat16"), ("z", 1024, "bfloat16"), ("az", 2048, "bfloat16"), ("gF", 2048, "bfloat16"),
+        ("Xw", 2816, "bfloat16"), ("coF", 2688, "float32"), ("suI", 2816, "int32"),
+        *[("F" + c, 2688, "float32" if c in "AB" else "bfloat16") for c in WINDOWS], ("sh", 2048, "bfloat16"), ("stv", 128, "bfloat16"), ("sts", 128, "float32"), ("M", 2048, "bfloat16"), ("E", 2048, "bfloat16"), ("z", 1024, "bfloat16"), ("az", 2048, "bfloat16"), ("gF", 2048, "bfloat16"),
         ("WT", 2048, "bfloat16"), ("wt_", 8, "bfloat16"),
         ("abU", 16, "uint16"), ("df", 256, "uint16"), ("dfF", 256, "float32"), ("dfH", 256, "bfloat16"), ("S", 512, "float32"), ("B", 512, "float32"),
         ("dL", 8, "uint16"), ("dF", 16, "float32"), ("d64", 8, "float32"), ("al", 16, "float32"), ("alI", 16, "float32"), ("ta", 16, "float32"),
@@ -39,12 +40,14 @@ for _n, _w, _t in [
 for _b in range(8):
     SCRATCH["P%d" % _b] = ("psum", [128, 512], "float32")
 
-LOADS = ["ab", "dl", "co0", "co1", "x0", "x1", "su0", "su1", "wt", "th"]
+LOADS = ["ab", "dl", "co00", "co01", "co10", "co11", "x0", "x1", "su0", "su1", "wt", "th"]
 SEMAPHORES = (["sv", "ss", "sp", "sg", "ls", "so", "sb0", "sb1"] + ["ld_" + n for n in LOADS] + ["rdl%d" % t for t in (1, 2, 3)]
               + ["rab%d%d" % (t, s) for t in (1, 2, 3) for s in (0, 1)])
 
-CFG = {"first": {1: "VVVV", 2: "VVVV"}, "second": {1: "SSSS", 2: "SSSV"}, "renew": "SSSS", "flagS": 7, "conv": "S", "merge": 2, "scans": ((0, 2), (2, 1), (3, 1)),
-       "cum": True, "passes": 3, "lead": 8.0, "wake": 0.14, "pe": 0.8}
+CFG = {"first": {1: "SVVV", 2: "SVVV"}, "second": {1: "SSSS", 2: "SSSC"}, "renew": "SSSS", "flags": "ABABABABBBBVVVVV", "merge": 2, "scans": ((0, 2), (2, 1), (3, 1)),
+       "cum": True, "moves": 3000, "seed": 1, "leads": [6.0 + 0.5 * i for i in range(12)], "wake": 0.2, "pe": 0.6, "fix": 0.015, "far": 14.0}
+CFG["but"] = {}
+PLAN = CFG
 CY, GA, SC = 0.83e-3, 1.45, 3.3
 ORDER = {}
 
@@ -60,32 +63,66 @@ def schedule(ops):
             succ[d].append((i, lag))
 
     def place(order, back):
-        at, used = [0.0] * n, {}
+        at, begin, finish = [0.0] * n, {o["e"]: [] for o in ops}, {o["e"]: [] for o in ops}
         for i in order:
-            t = max([at[j] + hold[j] + lag - hold[i] for j, lag in succ[i]] + [cost[i] - hold[i]]) if back else max([at[d] + lag for d, lag in pred[i]] + [0.0])
-            u = used.setdefault(ops[i]["e"], [])
-            lo, hi = 0, len(u)
-            while lo < hi:
-                mid = (lo + hi) // 2
-                lo, hi = (mid + 1, hi) if u[mid][1] <= t else (lo, mid)
-            while lo < len(u) and u[lo][0] < t + hold[i] - 1e-9:
-                t, lo = max(t, u[lo][1]), lo + 1
-            u.insert(lo, (t, t + hold[i]))
+            h, t = hold[i], cost[i] - hold[i] if back else 0.0
+            for j, lag in after[i] if back else pred[i]:
+                if at[j] + lag > t:
+                    t = at[j] + lag
+            a, b = begin[ops[i]["e"]], finish[ops[i]["e"]]
+            k = m = len(a)
+            while k and b[k - 1] > t:
+                k -= 1
+            while k < m and a[k] < t + h - 1e-9:
+                t, k = max(t, b[k]), k + 1
+            a.insert(k, t)
+            b.insert(k, t + h)
             at[i] = t
         return at
 
-    pri = [0.0] * n
-    for i in range(n - 1, -1, -1):
-        pri[i] = max([pri[j] + lag for j, lag in succ[i]] + [cost[i] + (CFG["lead"] if ops[i]["w"][:1] == ["X_0"] else 0.0)])
-    order, best = sorted(range(n), key=lambda i: (-pri[i], i)), None
-    for _ in range(CFG["passes"]):
-        at = place(order, False)
-        end = max(at[i] + cost[i] for i in range(n))
-        if best is None or end < best[2]:
-            best = (sorted(range(n), key=lambda i: (at[i], i)), at, end)
+    def settle(key):
+        for i in range(n):
+            for d, _ in pred[i]:
+                if key[d] > key[i]:
+                    key[i] = key[d]
+        at = place(sorted(range(n), key=lambda i: (key[i], i)), False)
         bk = place(sorted(range(n), key=lambda i: (-at[i], -i)), True)
-        order = sorted(range(n), key=lambda i: (-bk[i] - hold[i], i))
-    return best
+        again = place(sorted(range(n), key=lambda i: (-bk[i] - hold[i], i)), False)
+        return min((max(x[i] + cost[i] for i in range(n)), x) for x in (at, again))
+
+    after = [[(j, hold[j] + lag - hold[i]) for j, lag in succ[i]] for i in range(n)]
+    tries = []
+    for lead in CFG["leads"]:
+        way = [0.0] * n
+        for i in range(n - 1, -1, -1):
+            way[i] = max([way[j] + lag for j, lag in succ[i]] + [cost[i] + (lead if ops[i]["w"][:1] == ["X_0"] else 0.0)])
+        tries.append(settle([-x for x in way]))
+    now = best = min(tries)
+    like = {}
+    for i, o in enumerate(ops):
+        if o["at"]:
+            name = (o["e"], o["at"][1], tuple(w[:2] if w[:2] == "ab" and w[2] != "U" else w for w in o["w"]))
+            like.setdefault(name + (sum(ops[j]["at"] == o["at"] for k in like if k[:3] == name for j in like[k]),), []).append(i)
+    names, state = list(like), [CFG["seed"]]
+
+    def draw(lo, hi):
+        state[0] = (state[0] * 6364136223846793005 + 1442695040888963407) % 2 ** 64
+        return lo + (hi - lo) * (state[0] >> 11) / 2 ** 53
+
+    for _ in range(CFG["moves"]):
+        key = list(now[1])
+        if draw(0, 1) < 0.5:
+            moves = [(names[int(draw(0, len(names)))], draw(-2, 2)) for _ in range(int(draw(1, 9)))]
+        else:
+            one, wide, by = names[int(draw(0, len(names)))], draw(0.5, 6), draw(-2, 2)
+            t, a = ops[like[one][0]]["at"][0], key[like[one][0]]
+            moves = [(k, by) for k in names if k[1] == one[1] and ops[like[k][0]]["at"][0] == t and a <= key[like[k][0]] <= a + wide]
+        for k, by in moves:
+            for i in like[k]:
+                key[i] += by
+        new = settle(key)
+        now, best = new if new[0] <= now[0] + 0.1 else now, min(best, new)
+    return sorted(range(n), key=lambda i: (best[1][i], i)), best[1], best[0], min(tries)[0]
 
 
 def runs(path, letter, most):
@@ -105,7 +142,7 @@ def rank_program(g, core, T, topo):
         return
     N = len(T.cores)
     V, S, PE = g.vector, g.scalar, g.tensor
-    ops, lastw, readers = [], {}, {}
+    ops, lastw, readers, where = [], {}, {}, []
 
     def op(e, c, r, w, fs, sem=None, val=None, isasync=False, order=()):
         i = len(ops)
@@ -120,12 +157,12 @@ def rank_program(g, core, T, topo):
             lastw[t] = i
             readers[t] = []
         deps.discard(i)
-        ops.append({"e": e, "c": c, "hard": sorted(deps), "deps": sorted(deps | soft), "f": fs, "sem": sem, "val": val, "async": isasync, "w": w})
+        ops.append({"e": e, "c": c, "hard": sorted(deps), "deps": sorted(deps | soft), "f": fs, "sem": sem, "val": val, "async": isasync, "w": w, "at": tuple(where)})
         return i
 
     esem = {"V": "sv", "S": "ss", "PE": "sp", "G": "sg"}
-    vop = lambda n, r, w, f, cy=1.0: op("V", 0.04 + max(n * cy, 64) * CY, r, w, [f])
-    sop = lambda n, r, w, f, cy=1.0: op("S", 0.055 + max(n * cy, 64) * CY, r, w, [f])
+    vop = lambda n, r, w, f, cy=1.0: op("V", (0.05 if cy in (GA, SC) else CFG["fix"]) + max(n * cy, 64) * CY, r, w, [f])
+    sop = lambda n, r, w, f, cy=1.0: op("S", (0.065 if cy in (GA, SC) else CFG["fix"]) + max(n * cy, 64) * CY, r, w, [f])
     vg = lambda n, r, w, f: vop(n, r, w, f, GA)
     sg = lambda n, r, w, f: sop(n, r, w, f, GA)
     pop = lambda cyc, r, w, fs: op("PE", cyc * CY * CFG["pe"], r, w, fs)
@@ -159,11 +196,12 @@ def rank_program(g, core, T, topo):
     half = lambda u: slice(64 * u, 64 * u + 64)
     X0, XP0, _ = own(0)
     X1, XP1, _ = own(1)
-    i = load("Y", "co0", 4.5, ["col0"], [(X1("suI", 0, 1280), T.co[:, 0:1280])])
-    i = load("Y", "co1", 7.0, ["col1"], [(X1("suI", 1280, 2560), T.co[:, 1280:2560])], order=[i])
-    i = load("Y", "x0", 8.0, ["Xa_0"], [(XP0(0, "Xw", 0, 2560), T.x0[0:64, :])], order=[i])
-    i = load("Y", "x1", 9.5, ["Xa_1"], [(XP1(64, "Xw", 0, 2560), T.x0[64:128, :])], order=[i])
-    su0 = load("Y", "su0", 14.0, ["su_0"], [(XP0(64 * u, "suI", 0, 2560), T.su[0:64, :]) for u in (0, 1)], order=[i])
+    before = []
+    for s in sets:
+        for h in (0, 1):
+            before = [load("Y", "co%d%d" % (s, h), 3.4 + 1.4 * h + 4.2 * s, ["col%d_%d" % (h, s)], [(XP1(64 * s, "suI", 1280 * h, 1280 * h + 1280), T.co[half(s), 1280 * h:1280 * h + 1280])], order=before)]
+        before = [load("Y", "x%d" % s, 6.2 + 5.5 * s, ["X_1" if s else "Xa_0"], [(own(s)[1](64 * u, "Xw", 0, 2560), T.x0[half(s), :]) for u in range(s + 1)], order=before)]
+    su0 = load("Y", "su0", 17.0, ["su_0"], [(XP0(64 * u, "suI", 0, 2560), T.su[0:64, :]) for u in (0, 1)], order=before)
     i = load("S", "ab", 2.5, ["ab0_0", "ab0_1"], [(T.abI[half(u), 16 * s + 8 * q:16 * s + 8 * q + 8], x[half(s), 8 * u:8 * u + 8]) for s in sets for q, x in enumerate((T.la, T.lb)) for u in (0, 1)])
     i = load("S", "dl", 2.5, ["dl0"], [(T.dls[half(u), 128 * s:128 * s + 128], T.dl[half(s), 128 * u:128 * u + 128]) for s in sets for u in (0, 1)], order=[i])
     i = load("S", "th", 3, ["thI"], [(T.thI[0:8, 0:1], T.th[:])], order=[i])
@@ -172,10 +210,10 @@ def rank_program(g, core, T, topo):
         X, XP, K = own(s)
         for h in (0, 1):
             a, b = 1280 * h, 1280 * h + 1280
-            vop(1280, ["col%d" % h], [K("coa%d" % h)], cp(XP(64 * s, "coF", a, b), XP1(64 * s, "suI", a, b)))
+            vop(1280, [K("col%d" % h)], [K("coa%d" % h)], cp(XP(64 * s, "coF", a, b), XP1(64 * s, "suI", a, b)))
             sop(1280, [K("coa%d" % h)], [K("cob%d" % h)], act(XP(64 - 64 * s, "coF", a, b), XP(64 * s, "coF", a, b), AF.Copy))
-        vop(2560, [K("Xa")], [K("X")], cp(XP(64 - 64 * s, "Xw", 0, 2560), XP(64 * s, "Xw", 0, 2560)), 0.5)
-    load("Y", "su1", 9.0, ["su_1", "col0", "col1"], [(XP1(64 * u, "suI", 0, 2560), T.su[64:128, :]) for u in (0, 1)], order=[su0])
+    vop(2560, ["Xa_0"], ["X_0"], cp(XP0(64, "Xw", 0, 2560), XP0(0, "Xw", 0, 2560)), 0.5)
+    load("Y", "su1", 10.0, ["su_1", "col0_0", "col1_0", "col0_1", "col1_1"], [(XP1(64 * u, "suI", 0, 2560), T.su[64:128, :]) for u in (0, 1)], order=[su0])
 
     pF = lambda c: T.pF[:, c:c + 1]
     pT = lambda c: T.pT[:, 4 * c:4 * c + 1]
@@ -186,16 +224,14 @@ def rank_program(g, core, T, topo):
     vop(1, ["pT0"], ["p16"], cp(pF(0), pT(0)))
     vop(1, ["pT0"], ["p15"], ts(pF(1), pT(0), -1.0, 15.0, OP.mult, OP.add))
     vop(1, ["pT0"], ["p256"], ts(pF(3), pT(0), 16.0, None, OP.mult))
-    vop(1, ["pT1"], ["p32"], ts(pF(4), pT(1), 2.0, None, OP.mult))
     vop(1, ["pT2"], ["p128"], ts(pF(5), pT(2), 2.0, None, OP.mult))
-    vop(512, ["jm", "p16"], ["dm"], ts(T.dm[:], T.jm[:], pF(0), None, OP.is_equal))
-    vop(128, ["jm", "p15"], ["dmr"], ts(T.dmr[:], T.jm[:, 0:128], pF(1), None, OP.is_equal))
+    vop(256, ["jm", "p16"], ["dm"], ts(T.dm[:], T.jm[:, 0:256], pF(0), None, OP.is_equal))
+    vop(128, ["jm", "p15"], ["dmr"], ts(T.dmr[:], T.jm[:, 0:128], pF(1), 4096.0, OP.is_equal, OP.mult))
     sop(512, ["jm"], ["segN"], act(T.segN[:], T.jm[:], AF.Identity, scale=-1e9, bias=5e8))
     sop(256, ["jm"], ["segX"], act(T.segX[:], T.jm[:, 0:256], AF.Identity, scale=1e9))
     sop(128, ["jm"], ["seg1"], act(T.seg1[:], T.jm[:, 0:128], AF.Sign))
-    for h in (0, 1):
-        sop(512, ["jm"], ["rN%d" % h], act(T.rN[:, 512 * h:512 * h + 512], T.jm[:], AF.Relu, scale=-64.0, bias=64.0))
-        sop(512, ["jm"], ["rX%d" % h], act(T.rX[:, 512 * h:512 * h + 512], T.jm[:], AF.Identity, scale=64.0))
+    gop(1024, [], ["rN"], iof(T.rN[:], [[0, 64], [-64, 16]], 64))
+    gop(1024, [], ["rX"], iof(T.rX[:], [[0, 64], [64, 16]], 0))
     gop(32, [], ["eI"], ioi(T.eI[:, 0:32], [[16, 32]], 15, 0))
     vop(32, ["eI"], ["LE"], cp(T.LE[:], T.eI[:, 0:32]))
     vop(128, [], ["onesB"], fill(T.onesB[:], 1.0))
@@ -208,7 +244,7 @@ def rank_program(g, core, T, topo):
     sop(128, ["anti0"], ["anti1"], act(T.antiF[:, 128:256], T.antiF[:, 0:128], AF.Identity, scale=-1.0))
     gop(8, ["onesF"], ["g8"], sel(T.g8[:], T.onesF[:, 0:8], [[-16, 8]], OP.is_ge, 0, 1))
     gop(8, ["g8"], ["g8"], sel(T.g8[:], T.g8[:], [[16, 8]], OP.is_ge, 15, -1))
-    for nm, cs in (("g8p", (2048.0, 32768.0, 2048.0, 16.0, 16384.0, 16384.0)), ("gK", (-4096.0, -266240.0, 1.0, 1.0)),
+    for nm, cs in (("g8p", (16.0, 2048.0, 32768.0, 2048.0, 16384.0, 16384.0)), ("gK", (-4096.0, -266240.0, 1.0, 1.0)),
                    ("gB", (32.0, 2048.0, 0.0, 32.0, 0.015625, 1.0, -32.0, -2048.0))):
         for i, c in enumerate(cs):
             sop(8, ["g8"], ["%s%d" % (nm, i)], act(T[nm][:, 8 * i:8 * i + 8], T.g8[:], AF.Identity, scale=c))
@@ -219,19 +255,20 @@ def rank_program(g, core, T, topo):
     sop(8, ["g8"], ["gN2"], act(T.gN[:, 16:24], T.g8[:], AF.Copy))
     sop(8, ["g4F0", "g4F1"], ["g4B"], act(T.g4B[:], T.g4F[:], AF.Copy))
     g8p_t, gK_t, gB_t = ["g8p%d" % i for i in range(6)], ["gK%d" % i for i in range(6)], ["gB%d" % i for i in range(8)]
+    sop(48, g8p_t, ["g8n"], act(T.g8n[:], T.g8p[:], AF.Identity, scale=-1.0))
+    g8p_t.append("g8n")
     vop(128, [], ["c32"], fill(T.c32[0:64, :], 0.03125))
-    for i, (a, v) in enumerate(((128, -160), (2048, 5120), (128, -160), (1, 0))):
+    for i, (a, v) in enumerate(((1, 0), (128, -160), (2048, 5120), (128, -160))):
         gop(128, [], ["cK%d" % i], iof(T.cK[0:32, 128 * i:128 * i + 128], [[0, 8], [a, 16]], v))
-    for i, v in enumerate((-128.0 * MID, 327680.0 - 2048.0 * MID, -128.0 * MID, -1.0 * MID)):
+    for i, v in enumerate((-1.0 * MID, -128.0 * MID, 327680.0 - 2048.0 * MID, -128.0 * MID)):
         vop(128, [], ["cK%d" % (4 + i)], fill(T.cK[32:64, 128 * i:128 * i + 128], v), 0.5)
     gop(256, [], ["cK8"], iof(T.cK[0:32, 512:768], [[0, 16], [-1024, 16]], 15360))
     cK_t = ["c32"] + ["cK%d" % i for i in range(8)] + ["idC%d" % a for a in (0, 128, 256, 384)] + ["identF", "id64F"]
-    th_t = ["Th%d_%d" % (G, s) for s in sets for G in range(8)]
-    gop(2048, [], th_t, iof(T.Th[:], [[-1, 16], [32, 8], [1, 16]], 0))
-    vop(2048, th_t + ["p32"], ["selX"], ts(T.selX[:], T.Th[:], pF(4), None, OP.is_equal), 0.5)
     gop(128, ["onesB"], ["grp"], sel(T.grp[:], T.onesB[:], [[-16, 8], [0, 16]], OP.is_ge, 0, 1))
     gop(128, ["grp"], ["grp"], sel(T.grp[:], T.grp[:], [[16, 8], [0, 16]], OP.is_ge, 15, -1))
-    sop(128, ["grp"], ["grp"], act(T.grp[:], T.grp[:], AF.Identity, scale=4096.0))
+    sel_t = ["selX%d" % j for j in range(16)]
+    for j in range(16):
+        gop(128, ["grp"], [sel_t[j]], sel(T.selX[:, 128 * j:128 * j + 128], T.grp[:], [[0, 8], [1, 16]], OP.is_equal, -j, 0))
     for u in (0, 1):
         gop(128, ["onesF"], ["dupF%d" % u], sel(T.dupF[:, 128 * u:128 * u + 128], T.onesF[:], [[0, 2], [-1, 64]], OP.is_equal, 64 * u - 64, 1))
     sop(256, ["dupF0", "dupF1"], ["dupB"], act(T.dupB[:], T.dupF[:], AF.Copy))
@@ -270,42 +307,46 @@ def rank_program(g, core, T, topo):
         X, XP, K = own(s)
         gop(128, ["onesF"], [K("gT")], sel(T.gT[0:8, 128 * s:128 * s + 128], T.onesF[0:8, :], [[0, 2], [1, 4], [0, 16]], OP.is_equal, 4 * s, -1))
         vop(1, ["wt"], [K("wtF")], cp(pF(10 + s), X("wt_", 0, 1)))
-        vop(2048, th_t + ["p32", K("wtF")], [K("WT")], ts(X("WT"), T.Th[:], pF(4), pF(10 + s), OP.is_equal, OP.mult), 0.5)
+        for h in (0, 1):
+            sop(1024, sel_t[8 * h:8 * h + 8] + [K("wtF")], [K("WT%d" % h)], act(X("WT", 1024 * h, 1024 * h + 1024), T.selX[:, 1024 * h:1024 * h + 1024], AF.Identity, scale=pF(10 + s)))
         gop(128, [], [K("co2")], iof(X("coF", 2560), [[1, 128]], 2560))
         gop(256, [], [K("su2")], ioi(X("suI", 2560), [[0, 256]], 0, 0))
         gop(128, [], [K("Fc")], iof(X("Fc"), [[0, 128]], 0))
-        gop(1536, [], [K("Fs")], iof(X("Fs", 1024, 2560), [[0, 1536]], 0))
-        vop(1536, [], [K("Fv0")], fill(X("Fv0", 1024, 2560), 0.0), 0.5)
-        gop(1536, [], [K("Fv1")], iof(X("Fv1", 1024, 2560), [[0, 1536]], 0))
+        for c in WINDOWS:
+            gop(1536, [], [K("F" + c)], iof(X("F" + c, 1024, 2560), [[0, 1536]], 0))
         vop(8, ["p16", "p128", "onesF"], [K("Rw2")], ts(X("Rw", 128), T.onesF[:, 0:8], pF(0), 8.0, OP.add, OP.mult))
         sop(8, [K("Rw2"), "p128"], [K("Rw2")], act(X("Rw", 128), X("Rw", 128), AF.Identity, bias=pF(5)))
     pop(512, ["gT_0", "gT_1", "thF"], ["P3"], [mm(T.P3[:, s:s + 1], T.gT[0:8, 128 * s:128 * s + 128], T.thF[0:8, 0:1], True, True) for s in sets])
     vop(2, [], ["th16", "P3"], ts(T.th16[:, 0:2], T.P3[:, 0:2], 16.0, -1.0 * MID, OP.mult, OP.add))
     vop(2, ["th16"], ["thr"], cp(T.thr[:, 0:2], T.th16[:, 0:2]))
-    for t in range(R):
-        gop(128, [], ["stv%d" % t], iof(T.stv[:, 128 * t:128 * t + 128], [[0, 128]], 32 * 8 ** t))
-        gop(128, [], ["sts%d" % t], iof(T.sts[:, 128 * t:128 * t + 128], [[0, 128]], 32 * 8 ** t))
 
-    def send(dst_rank, out, in_, sem, r):
+    def send(dst_rank, out, in_, sem, r, w, c=0.8):
         dst = T.cores[dst_rank]
         rid, pid, _ = topo.addr(dst)
         m = sum(1 << e for e in topo.engines(core, dst)[:4])
-        return op("G", 0.6, r, [], [lambda: g.remote_dma(out, in_, T.sem[sem], T.sem.ls, pid, rid, m)], "none", 0)
+        i = op("G", c, r + ["sent"] * (c < 1), ["sent"] * (c > 1), [lambda: g.remote_dma(out, in_, T.sem[sem], T.sem.ls, pid, rid, m)], "none", 0)
+        op("R", CFG["far"], [], [w], [], sem, 4, True, order=[i])
 
     for t in (1, 2, 3):
-        i = send((rank + t) % N, T.dls[:, 256 * t:256 * t + 256], T.dls[:, 0:256], "rdl%d" % t, ["dl0"])
-        op("R", 4.0, [], ["dl%d" % t], [], "rdl%d" % t, 4, True, order=[i])
-    for k in range(16):
-        if k % 3:
-            vop(256, ["dl0"], ["sh0_%d" % k], cp(T.sh0[:, k::16], T.dls[:, 0:256]), 0.5)
-        else:
-            sop(256, ["dl0"], ["sh0_%d" % k], act(T.sh0[:, k::16], T.dls[:, 0:256], AF.Copy))
+        send((rank + t) % N, T.dls[:, 256 * t:256 * t + 256], T.dls[:, 0:256], "rdl%d" % t, ["dl0"], "dl%d" % t, 0.8 if t > 1 else 6.0)
 
     def lanes(t, s):
         X, XP, K = own(s)
+        where[:] = [t, s]
+        CFG = dict(PLAN, **PLAN["but"].get((t, s), {}))
         PK, PA, PB, PD = ("P%d" % (4 * s + i) for i in range(4))
-        sht = ["sh%d_%d" % (t % 2, k) for k in range(16)]
-        sh = lambda a, n: (T.sh0 if t % 2 == 0 else T.sh1)[:, 2048 * s + a:2048 * s + a + n]
+        sht = [K("sh%d" % k) for k in range(16)]
+        sh = lambda a, n: X("sh", a, a + n)
+        dl = T.dls[:, 256 * t + 128 * s:256 * t + 128 * s + 128]
+        for k in range(16):
+            if t:
+                gop(128, ["dl%d" % t], [sht[k]], sel(X("sh", k, None, 16), dl, [[0, 128]], OP.is_ge, 1, 0))
+            elif k % 4:
+                vop(128, ["dl0"], [sht[k]], cp(X("sh", k, None, 16), dl), 0.5)
+            else:
+                sop(128, ["dl0"], [sht[k]], act(X("sh", k, None, 16), dl, AF.Copy))
+        for nm in ("stv", "sts"):
+            gop(128, [], [K(nm)], iof(X(nm), [[0, 128]], 32 * 8 ** t))
         cur = T.abI[:, 16 * s:16 * s + 16] if t == 0 else T.land[:, 32 * t - 32 + 16 * s:32 * t - 16 + 16 * s]
         nxt = lambda a=0, b=16, p=slice(0, 128): T.abo[p, 32 * t + 16 * s + a:32 * t + 16 * s + b]
         win = lambda lst, lo, q, n: X("Xw", 0, 2560).indirect(X(lst, lo + 32 * q, lo + 32 * (q + n)))
@@ -323,26 +364,44 @@ def rank_program(g, core, T, topo):
                 a, m = 512 * q, X(Mb, 512 * q, 512 * (q + n))
                 vg(512 * n, [xt, K(lst)] + sht, blk(Mb, q, n), tt(m, win(lst, 0, q, n), sh(a, 512 * n), OP.add))
                 vop(512 * n, blk(Mb, q, n), blk(Mb, q, n), ts(m, m, 0.0, 63.0, OP.max, OP.min), 0.5)
-            for q, n in runs(path, "S", 1):
-                a, P = 512 * q, bank()
+            for q in range(4):
+                if path[q] == "V":
+                    continue
+                a, P, m = 512 * q, bank(), X(Mb, 512 * q, 512 * q + 512)
                 sg(512, [xt, K(lst)], blk("gF", q), act(X("gF", a, a + 512), win(lst, 0, q, 1), AF.Copy))
                 pop(1024, ["ident"] + blk("gF", q) + sht, [P], [mm(T[P][:], T.ident[:], sh(a, 512), True, False), mm(T[P][:], T.ident[:], X("gF", a, a + 512), False, True)])
-                vop(512, [], [P] + blk(Mb, q), ts(X(Mb, a, a + 512), T[P][:], 0.0, 63.0, OP.max, OP.min))
+                if path[q] == "S":
+                    vop(512, [], [P] + blk(Mb, q), ts(m, T[P][:], 0.0, 63.0, OP.max, OP.min))
+                else:
+                    sop(512, [], [P] + blk(Mb, q), act(m, T[P][:], AF.Relu))
+                    vop(512, blk(Mb, q), blk(Mb, q), ts(m, m, 63.0, None, OP.min), 0.5)
 
         def second(step, lst, lo, Mb):
-            path = CFG["second"][step]
+            path, lt = CFG["second"][step], lambda q: K(lst if step == 1 else "%s%d" % (lst, q))
             for q, n in runs(path, "S", 1):
                 a, P = 512 * q, bank()
-                sg(512, [xt, K(lst)], blk("gF", q), act(X("gF", a, a + 512), win(lst, lo, q, 1), AF.Copy))
+                sg(512, [xt, lt(q)], blk("gF", q), act(X("gF", a, a + 512), win(lst, lo, q, 1), AF.Copy))
                 one = (mm(T[P][:], T.ident[:], X("gF", a, a + 512), step == 1, step == 2), ["ident"] + blk("gF", q))
                 two = (mm(T[P][:], T.nident[:], X(Mb, a, a + 512), step == 2, step == 1), ["nident"] + blk(Mb, q))
-                for f, r in (one, two) if step == 1 else (two, one):
-                    pop(512, r, [P], [f])
+                both = (one, two) if step == 1 else (two, one)
+                pop(1024, one[1] + two[1], [P], [f for f, _ in both])
                 sop(512, [], [P] + blk("az", q), act(X("az", a, a + 512), T[P][:], AF.Abs))
-            for x, (q, n) in enumerate(runs(path, "V", 1)):
-                a, z = 512 * q, X("z", 512 * (x % 2), 512 * (x % 2) + 512)
-                vg(512, [xt, K(lst)] + blk(Mb, q), blk("z", x % 2), tt(z, win(lst, lo, q, 1), X(Mb, a, a + 512), OP.subtract))
-                sop(512, blk("z", x % 2), blk("az", q), act(X("az", a, a + 512), z, AF.Abs))
+            for q in (2, 3):
+                if path[q] == "S":
+                    continue
+                a, z = 512 * q, X("z", 512 * q - 1024, 512 * q - 512)
+                vg(512, [xt, lt(q)] + blk(Mb, q), blk("z", q), tt(z, win(lst, lo, q, 1), X(Mb, a, a + 512), OP.subtract))
+                if path[q] == "V":
+                    sop(512, blk("z", q), blk("az", q), act(X("az", a, a + 512), z, AF.Abs))
+                else:
+                    vop(512, blk("z", q), blk("az", q), ts(X("az", a, a + 512), z, 0.0, 2.0, OP.max, OP.mult), 0.5)
+
+        def sums(step, bk, a, b, w):
+            path, n = CFG["second"][step], (b - a) // 16
+            for q in (2, 3):
+                if path[q] == "C":
+                    pop(512, blk("z", q) + g8p_t, [bk], [mm(T[bk][32 * q:32 * q + 32, a + k:b:16], X("z", 512 * q - 1024 + k, 512 * q - 512, 16), T.g8n[:, w:w + n], False, False) for k in range(16)])
+            pop(1024, blk("az", 0, 4) + g8p_t, [bk], [mm(T[bk][:, a + k:b:16], X("az", k, None, 16), T.g8p[:, w:w + n], False, k == 15) for k in range(16)])
 
         vop(16, [K("ab%d" % t)], [K("abU")], cp(X("abU"), cur))
         vg(256, [K("abU")] + co_t, [K("df")], cp(X("df"), X("coF", 0, 2560).indirect(X("abU"))))
@@ -350,17 +409,19 @@ def rank_program(g, core, T, topo):
         sop(256, [K("dfF")], [K("dfH")], act(X("dfH"), X("dfF"), AF.Identity, scale=0.03125, bias=159.515625))
         P = T[PK]
         pop(2048, cK_t + [K("dfH"), K("dfF")], [PK], [
-            mm(P[:], T.c32[0:64, :], T.cK[0:64, 0:512], True, False), mm(P[:, 128:256], X("dfF", 0, 128), T.id64F[:], False, False),
-            mm(P[:, 0:256], X("dfH", 0, 128), T.idC[:, 0:256], False, False), mm(P[:, 128:256], X("dfF", 128), T.identF[:], False, False),
-            mm(P[:, 128:384], X("dfH", 128), T.idC[:, 256:512], False, False)])
+            mm(P[:], T.c32[0:64, :], T.cK[0:64, 0:512], True, False), mm(P[:, 256:384], X("dfF", 0, 128), T.id64F[:], False, False),
+            mm(P[:, 128:384], X("dfH", 0, 128), T.idC[:, 0:256], False, False), mm(P[:, 256:384], X("dfF", 128), T.identF[:], False, False),
+            mm(P[:, 256:512], X("dfH", 128), T.idC[:, 256:512], False, False)])
         first(1, "df", "M")
         second(1, "df", 128, "M")
-        pop(1024, blk("az", 0, 4) + g8p_t, [PK], [mm(P[:, k::16], X("az", k, None, 16), T.g8p[:, 0:32], False, k == 15) for k in range(16)])
+        sums(1, PK, 0, 512, 0)
         vop(512, ["segN"], [K("S"), PK], scan(X("S"), T.segN[:], P[:], 1e9, OP.max, OP.min))
-        vg(512, [K("S"), "LE", "dm"], [K("B"), K("Bn")], tt(X("B"), X("S").indirect(T.LE[:]), T.dm[:], OP.mult))
+        for h, nm in ((0, "B"), (1, "Bn")):
+            vg(256, [K("S"), "LE", "dm"], [K(nm)], tt(X("B", 256 * h, 256 * h + 256), X("S").indirect(T.LE[:, 16 * h:16 * h + 16]), T.dm[:, 0:256], OP.mult))
         P = T[PB]
-        pop(1280, [K("B"), K("Bn")] + gK_t + gB_t, [PB], [mm(P[:, 0:48], X("B", 384), T.gK[:], True, False)]
-            + [mm(P[:, 0:16], X("B", a, a + 128), T.gB[:, 16 * i:16 * i + 16], False, i == 3) for i, a in enumerate((0, 256, 128, 384))])
+        part = lambda a, i, last=False: mm(P[:, 0:16], X("B", a, a + 128), T.gB[:, 16 * i:16 * i + 16], False, last)
+        pop(512, [K("B")] + gK_t + gB_t, [PB], [mm(P[:, 0:48], X("B", 0, 128), T.gK[:], True, False), part(128, 0)])
+        pop(768, [K("B"), K("Bn")], [PB], [part(384, 1), part(256, 2), part(0, 3, True)])
         vop(8, [], [K("dL"), PB], cp(X("dL"), P[:, 0:8]))
         vop(16, ["thr"], [K("al"), PB], ts(X("al"), P[:, 16:32], T.thr[:, s:s + 1], None, OP.is_lt))
         vop(16, ["thr"], [K("alI"), PB], ts(X("alI"), P[:, 32:48], T.thr[:, s:s + 1], None, OP.is_lt))
@@ -372,8 +433,7 @@ def rank_program(g, core, T, topo):
         vop(16, [K("ta"), K("al")], [K("ta")], tt(X("ta"), X("ta"), X("al"), OP.mult))
         vop(16, [K("ta"), K("ab%d" % t)], [K("abo%d" % t)], tt(nxt(), X("ta"), cur, OP.add))
         if t < R - 1:
-            i = send((rank + 1) % N, T.land[:, 32 * t + 16 * s:32 * t + 16 * s + 16], nxt(), "rab%d%d" % (t + 1, s), [K("abo%d" % t)])
-            op("R", 4.0, [], [K("ab%d" % (t + 1))], [], "rab%d%d" % (t + 1, s), 4, True, order=[i])
+            send((rank + 1) % N, T.land[:, 32 * t + 16 * s:32 * t + 16 * s + 16], nxt(), "rab%d%d" % (t + 1, s), [K("abo%d" % t)], K("ab%d" % (t + 1)))
             sop(8, [K("al")], [K("acc"), "junk"], act(T.junk[:], X("al", 0, 8), AF.Copy, accum_out=T.acc[:, s:s + 1]))
         else:
             op("Y", 2.0, [K("abo%d" % t)], [], [(lambda y=y, q=q, u=u: g.sync.dma_start(y[half(s), 8 * u:8 * u + 8], nxt(8 * q, 8 * q + 8, half(u))))
@@ -393,17 +453,19 @@ def rank_program(g, core, T, topo):
         first(2, "sT", "E")
         P = T[PB]
         for x in (0, 1):
-            pop(1024, blk("E", 2 * x, 2) + [K("WT")], [PB], [mm(P[:, 64 + 64 * x:128 + 64 * x], X("WT", 128 * j, 128 * j + 128), X("E", 1024 * x + j, 1024 * x + 1024, 16), j == 0, j == 15) for j in range(16)])
-        vop(128, [], [K("uI"), PB], cp(X("uI"), P[:, 64:192]))
-        vop(128, [K("uI")], [K("uI")], ts(X("uI"), X("uI"), 4095, None, OP.bitwise_and))
-        vop(128, [K("uI")], [K("uB")], ts(X("uB"), X("uI"), 1184.0, None, OP.add))
-        vop(128, [K("uI"), K("uB")], [K("uA")], tt(X("uA"), X("uI"), X("uB"), OP.mult), 2)
-        vop(128, [K("uA")], [K("uI")], ts(X("uI"), X("uA"), 5, 1023, OP.arith_shift_right, OP.bitwise_and))
-        vop(128, [K("uI")], [K("nO")], cp(X("nO"), X("uI")))
-        vop(128, [K("uI")], [K("nP")], cp(X("nP"), X("uI")))
-        pop(768, [K("nP"), "identF", "c32", "cK8"], [PB], [mm(P[:, 256:512], T.c32[0:32, :], T.cK[0:32, 512:768], True, False), mm(P[:, 256:384], X("nP"), T.identF[:], False, False)])
+            H = lambda n, x=x: X(n, 64 * x, 64 * x + 64)
+            uI, uA, uB = (K("%s%d" % (n, x)) for n in ("uI", "uA", "uB"))
+            pop(1024, blk("E", 2 * x, 2) + blk("WT", 0, 2), [PB], [mm(P[:, 64:128], X("WT", 128 * j, 128 * j + 128), X("E", 1024 * x + j, 1024 * x + 1024, 16), j == 0, j == 15) for j in range(16)])
+            vop(64, [], [uI, PB], cp(H("uI"), P[:, 64:128]))
+            vop(64, [uI], [uI], ts(H("uI"), H("uI"), 4095, None, OP.bitwise_and))
+            vop(64, [uI], [uB], ts(H("uB"), H("uI"), 1184.0, None, OP.add))
+            vop(64, [uI, uB], [uA], tt(H("uA"), H("uI"), H("uB"), OP.mult), 2)
+            vop(64, [uA], [uI], ts(H("uI"), H("uA"), 5, 1023, OP.arith_shift_right, OP.bitwise_and))
+            vop(64, [uI], blk("nO", 2 * x, 2), cp(H("nO"), H("uI")))
+            vop(64, [uI], blk("nP", x), cp(H("nP"), H("uI")))
+        pop(768, blk("nP", 0, 2) + ["identF", "c32", "cK8"], [PB], [mm(P[:, 256:512], T.c32[0:32, :], T.cK[0:32, 512:768], True, False), mm(P[:, 256:384], X("nP"), T.identF[:], False, False)])
         second(2, "nO", 0, "E")
-        pop(1024, blk("az", 0, 4) + g8p_t, [PB], [mm(P[:, 256 + j:512:16], X("az", j, None, 16), T.g8p[:, 32:48], False, j == 15) for j in range(16)])
+        sums(2, PB, 256, 512, 32)
         vop(256, ["segX"], [K("S"), PB], scan(X("S", 0, 256), T.segX[:], P[:, 256:512], 0.0, OP.min, OP.max))
         vg(256, [K("S"), "LE", "dm"], [K("B")], tt(X("B", 0, 256), X("S", 0, 256).indirect(T.LE[:, 0:16]), T.dm[:, 0:256], OP.mult))
         sg(256, [K("S"), "LE"], [K("Bn")], act(X("B", 256), X("S", 0, 256).indirect(T.LE[:, 0:16]), AF.Copy))
@@ -429,11 +491,11 @@ def rank_program(g, core, T, topo):
         vop(8, [K("nt"), K("nS")], [K("nl")], tt(X("nl"), X("nt", 0, 8), X("nS", 0, None, 2), OP.max))
         for k in range(16):
             off = X("fL", 8 * k, 8 * k + 8)
-            if k < CFG["flagS"]:
-                sop(128, [K("fL"), "sts%d" % t], [K("Fs")], act(X("Fs").indirect(off), T.sts[:, 128 * t:128 * t + 128], AF.Silu), SC)
+            c = CFG["flags"][k]
+            if c in "AB":
+                sop(128, [K("fL"), K("sts")], [K("F" + c)], act(X("F" + c).indirect(off), X("sts"), AF.Silu), SC)
             else:
-                nm = "Fv%d" % (k % 2)
-                vop(128, [K("fL"), "stv%d" % t], [K(nm)], cp(X(nm).indirect(off), T.stv[:, 128 * t:128 * t + 128]), SC)
+                vop(128, [K("fL"), K("stv")], [K("F" + c)], cp(X("F" + c).indirect(off), X("stv")), SC)
 
         pop(768, [K("eS"), K("nl"), "dupB", "dupF0", "dupF1"], [PA],
             [mm(Q[:, 128 * u:128 * u + 128], T.dupB[:, 128 * u:128 * u + 128], X("eS"), True, True) for u in (0, 1)]
@@ -447,16 +509,8 @@ def rank_program(g, core, T, topo):
 
         F = lambda nm, o, w, last: [mm(P[:, 128 + m:256:16], X(nm, o + m, o + 1536, 12), w, False, last and m == 11) for m in range(12)]
         pop(128, [K("Fc"), "idBig"], [PB], [mm(P[:, 128:256], T.idBig[:], X("Fc"), True, False)])
-        pop(768, [K("Fv0"), "g4B"], [PB], F("Fv0", 1024, T.g4B[:], False))
-        if CFG["conv"] == "PE":
-            pop(3072, [K("Fs"), "g4F0", "g4F1"], [PB], F("Fs", 1024, T.g4F[:], False))
-        pop(768, [K("Fv1"), "g4B"], [PB], F("Fv1", 1024, T.g4B[:], CFG["conv"] == "PE"))
-        if CFG["conv"] != "PE":
-            if CFG["conv"] == "G":
-                gop(1536, [K("Fs")], blk("gF", 0, 3), sel(X("gF", 0, 1536), X("Fs", 1024, 2560), [[0, 1536]], OP.is_ge, 1, 0))
-            else:
-                sop(1536, [K("Fs")], blk("gF", 0, 3), act(X("gF", 0, 1536), X("Fs", 1024, 2560), AF.Copy))
-            pop(768, blk("gF", 0, 3) + ["g4B"], [PB], F("gF", 0, T.g4B[:], True))
+        for c in WINDOWS:
+            pop(3072 if c in "AB" else 768, [K("F" + c), "g4F0", "g4F1", "g4B"], [PB], F("F" + c, 1024, T.g4F[:] if c in "AB" else T.g4B[:], c == WINDOWS[-1]))
         vop(128, [], [K("Fp"), PB], ts(X("Fp"), P[:, 128:256], 448.0 * 8 ** t, None, OP.is_ge))
         vop(128, [K("Fp"), "seg1"], [K("Fi")], scan(X("Fi"), T.seg1[:], X("Fp"), 0.0, OP.mult, OP.add), 0.5)
         pop(64, [K("Fi"), "triI"], [PA], [mm(Q[:, 0:8], T.triI[:], X("Fi", 15, None, 16), True, True)])
@@ -474,7 +528,7 @@ def rank_program(g, core, T, topo):
         pop(256, [K("Fi"), K("tot"), "ident", "triS"], [PD], [mm(D[:, 0:128], X("Fi"), T.ident[:], True, False), mm(D[:, 0:128], X("tot"), T.triS[:], False, True)])
         sop(128, [], [PD, K("Rw")], act(X("Rw", 0, 128), D[:, 0:128], AF.Copy))
         vg(128, [K("Rw"), K("Rw2"), K("cL"), "rk"], [K("D")], tt(X("D"), X("Rw").indirect(X("cL")), T.rk[:], OP.is_le))
-        pop(1024, [K("D"), "selX"], [PB], [mm(P[:, 0:8], T.selX[:, 128 * p:128 * p + 128], X("D", p, None, 16), False, p == 15) for p in range(16)])
+        pop(1024, [K("D")] + sel_t, [PB], [mm(P[:, 0:8], T.selX[:, 128 * p:128 * p + 128], X("D", p, None, 16), False, p == 15) for p in range(16)])
         vop(8, [], [K("vL"), PB], cp(X("vL"), P[:, 0:8]))
         vg(128, [K("vL"), K("su"), K("su2")], [K("sR")], cp(X("sR"), X("suI").indirect(X("vL"))))
         sop(8, [], [K("vF"), PB], act(X("vF"), P[:, 0:8], AF.Copy))
@@ -493,8 +547,8 @@ def rank_program(g, core, T, topo):
                     vg(512 * n, [xt, K("sR")], blk("gF", q, n), cp(X("gF", a, b), win("sR", 0, q, n)))
         for q, n in CFG["scans"]:
             a, b = 512 * q, 512 * (q + n)
-            vop(512 * n, blk("gF", q, n) + ["rX0", "rX1"], blk("E", q, n), scan(X("E", a, b), T.rX[:, 0:b - a], X("gF", a, b), 0.0, OP.min, OP.max), 0.5)
-            vop(512 * n, blk("gF", q, n) + ["rN0", "rN1"], blk("az", q, n), scan(X("az", a, b), T.rN[:, 0:b - a], X("gF", a, b), 64.0, OP.max, OP.min), 0.5)
+            vop(512 * n, blk("gF", q, n) + ["rX"], blk("E", q, n), scan(X("E", a, b), T.rX[:, 0:b - a], X("gF", a, b), 0.0, OP.min, OP.max), 0.5)
+            vop(512 * n, blk("gF", q, n) + ["rN"], blk("az", q, n), scan(X("az", a, b), T.rN[:, 0:b - a], X("gF", a, b), 64.0, OP.max, OP.min), 0.5)
         pop(512, blk("E", 0, 4) + blk("az", 0, 4) + ["dupB"], [PA],
             [mm(Q[:, 128 * u:128 * u + 128], T.dupB[:, 128 * u:128 * u + 128], X(nm, 15, None, 16), nm == "E", nm == "az") for u in (0, 1) for nm in ("E", "az")])
         vop(256, [], [K("rI"), PA], ts(X("rI"), Q[:, 0:256], 0.5, -0.25, OP.mult, OP.add))
@@ -503,14 +557,11 @@ def rank_program(g, core, T, topo):
             op("Y", 3.0, [xt], [], [(lambda u=u: g.sync.dma_start(T.yx[half(s), 1024 + 768 * u:1792 + 768 * u], XP(64 * u, "Xw", 1024 + 768 * u, 1792 + 768 * u))) for u in (0, 1)], "so", 16, True)
 
     for t in range(R):
-        if t:
-            for k in range(16):
-                gop(256, ["dl%d" % t], ["sh%d_%d" % (t % 2, k)], sel((T.sh1 if t % 2 else T.sh0)[:, k::16], T.dls[:, 256 * t:256 * t + 256], [[0, 256]], OP.is_ge, 1, 0))
         for s in sets:
             lanes(t, s)
 
     if "o" not in ORDER:
-        ORDER["o"], ORDER["start"], ORDER["end"] = schedule(ops)
+        ORDER["o"], ORDER["start"], ORDER["end"], ORDER["lead"] = schedule(ops)
         ORDER["ops"] = ops
     queue = {"V": V, "S": S, "PE": PE, "G": g, "Y": g.sync}
     count, known = {}, {q: {} for q in queue}

@@ -9,12 +9,12 @@ for _n, _w, _t in [
         ("ident", 128, "bfloat16"), ("nident", 128, "bfloat16"), ("idC", 512, "bfloat16"), ("idBig", 128, "bfloat16"), ("id4k", 128, "bfloat16"),
         ("identF", 128, "float32"), ("id64F", 128, "float32"), ("antiF", 256, "float32"), ("grp", 128, "bfloat16"), ("onesF", 128, "float32"), ("onesB", 128, "bfloat16"),
         ("c32", 128, "bfloat16"), ("cK", 768, "bfloat16"), ("selX", 2048, "bfloat16"),
-        ("dupB", 256, "bfloat16"), ("dupF", 256, "float32"), ("triI", 128, "bfloat16"), ("triS", 128, "bfloat16"),
+        ("dupB", 256, "bfloat16"), ("triI", 128, "bfloat16"), ("triS", 128, "bfloat16"),
         ("g8", 8, "float32"), ("g8p", 48, "bfloat16"), ("g8n", 48, "bfloat16"), ("gK", 48, "float32"), ("gB", 64, "float32"), ("gN", 24, "float32"), ("g4B", 8, "bfloat16"), ("g4F", 8, "float32"),
-        ("jm", 512, "float32"), ("dm", 256, "float32"), ("dmr", 128, "float32"), ("segN", 512, "float32"), ("segX", 256, "float32"), ("seg1", 128, "bfloat16"),
+        ("jm", 256, "float32"), ("dm", 256, "float32"), ("dmr", 128, "float32"), ("segN", 256, "float32"), ("segX", 256, "float32"), ("seg1", 128, "bfloat16"),
         ("rN", 1024, "bfloat16"), ("rX", 1024, "bfloat16"), ("mE", 576, "bfloat16"), ("iotaB", 256, "bfloat16"), ("w12", 16, "bfloat16"), ("c1k", 8, "bfloat16"),
         ("rk", 128, "float32"), ("idx", 16, "float32"), ("idxR", 128, "float32"), ("EB", 8, "float32"), ("pI", 8, "int32"), ("pT", 64, "int32"), ("pF", 16, "float32"),
-        ("eI", 64, "int32"), ("LE", 32, "uint16"), ("LX", 8, "uint16"), ("LP", 8, "uint16"), ("LD", 8, "uint16"),
+        ("eI", 64, "int32"), ("LE", 16, "uint16"), ("LX", 8, "uint16"), ("LP", 8, "uint16"), ("LD", 8, "uint16"),
         ("thI", 8, "int32"), ("thF", 8, "float32"), ("gT", 256, "float32"),
         ("thr", 8, "float32"), ("th16", 8, "float32"), ("acc", 8, "float32"), ("acJ", 16, "int32"), ("junk", 8, "float32"),
         ("abI", 32, "int32"), ("land", 96, "float32"), ("abo", 128, "float32")]:
@@ -32,7 +32,7 @@ for _n, _w, _t in [
         ("oD", 16, "uint16"), ("oU", 16, "uint16"), ("T1", 256, "float32"), ("T2", 256, "float32"), ("fL", 128, "uint16"),
         ("eS", 128, "bfloat16"), ("eD", 256, "bfloat16"), ("Fp", 128, "bfloat16"), ("Fc", 128, "bfloat16"), ("Fi", 128, "bfloat16"), ("tot", 128, "bfloat16"),
         ("cum", 8, "bfloat16"), ("Th", 1024, "bfloat16"), ("cL", 8, "uint16"), ("Rw", 136, "float32"), ("D", 128, "bfloat16"),
-        ("vL", 8, "uint16"), ("vF", 8, "float32"), ("vD", 16, "uint16"), ("sR", 128, "uint16"), ("rI", 256, "int32")]:
+        ("vL", 8, "uint16"), ("oN", 8, "uint16"), ("nK", 16, "float32"), ("nM", 8, "float32"), ("vD", 16, "uint16"), ("sR", 128, "uint16"), ("rI", 256, "int32")]:
     _b = _n if _w > 256 or _n == "wt_" else "small_" + _t
     _at, _w16 = SCRATCH.get(_b, (0, [0, 0]))[1][1], -(-_w // 16) * 16
     SCRATCH[_b] = ("sbuf", [128, _at + 2 * _w16], _t)
@@ -40,12 +40,12 @@ for _n, _w, _t in [
 for _b in range(8):
     SCRATCH["P%d" % _b] = ("psum", [128, 512], "float32")
 
-LOADS = ["ab", "dl", "co00", "co01", "co10", "co11", "x0", "x1", "su0", "su1", "wt", "th"]
-SEMAPHORES = (["sv", "ss", "sp", "sg", "ls", "so", "sb0", "sb1"] + ["ld_" + n for n in LOADS] + ["rdl%d" % t for t in (1, 2, 3)]
+LOADS = ["ab", "dl", "co00", "co01", "co10", "co11", "cob00", "cob01", "cob10", "cob11", "x0", "x1", "su0", "su1", "wt", "th"]
+SEMAPHORES = (["sv", "ss", "sp", "sg", "ls", "so", "sb0", "sb1"] + ["d%s%d" % (n, s) for n in ("oU", "eD", "vD") for s in (0, 1)] + ["ld_" + n for n in LOADS] + ["rdl%d" % t for t in (1, 2, 3)]
               + ["rab%d%d" % (t, s) for t in (1, 2, 3) for s in (0, 1)])
 
-CFG = {"first": {1: "SVVV", 2: "SVVV"}, "second": {1: "SSSS", 2: "SSSC"}, "renew": "SSSS", "flags": "ABABABABBBBVVVVV", "merge": 2, "scans": ((0, 2), (2, 1), (3, 1)),
-       "cum": True, "moves": 3000, "seed": 1, "leads": [6.0 + 0.5 * i for i in range(12)], "wake": 0.2, "pe": 0.6, "fix": 0.015, "far": 14.0}
+CFG = {"first": {1: "SVVV", 2: "SVVV"}, "second": {1: "SSSS", 2: "SSSC"}, "renew": "SSSS", "flags": "ABABABABBBBVVVVV", "turned": "", "merge": 2, "scans": ((0, 2), (2, 1), (3, 1)),
+       "cum": True, "moves": 3500, "seed": 1, "slack": 0.15, "leads": [6.0 + 0.5 * i for i in range(12)], "wake": 0.2, "pe": 0.6, "fix": 0.015, "far": 14.0, "near": 2.8, "eq": "V", "wt": "VVSS", "sums": {1: ((0, 4),), 2: ((0, 4),)}, "ren": ((0, 768), (768, 640), (1408, 384), (1792, 256)), "hash": "AB", "cob": "SSSS"}
 CFG["but"] = {}
 PLAN = CFG
 CY, GA, SC = 0.83e-3, 1.45, 3.3
@@ -109,19 +109,45 @@ def schedule(ops):
         state[0] = (state[0] * 6364136223846793005 + 1442695040888963407) % 2 ** 64
         return lo + (hi - lo) * (state[0] >> 11) / 2 ** 53
 
-    for _ in range(CFG["moves"]):
-        key = list(now[1])
-        if draw(0, 1) < 0.5:
+    kin = {i: k for k in names for i in like[k]}
+
+    def queued(end, at):
+        ends = {(ops[i]["e"], round(at[i] + hold[i], 6)): i for i in range(n)}
+        i, out = max(range(n), key=lambda j: at[j] + cost[j]), []
+        while i is not None:
+            d = next((d for d, lag in pred[i] if at[d] + lag > at[i] - 1e-6), None)
+            if d is None:
+                d = ends.get((ops[i]["e"], round(at[i], 6)))
+                if d in kin and i in kin:
+                    out.append((i, d))
+            i = d
+        return out
+
+    line = queued(*now)
+    for m in range(CFG["moves"]):
+        key, x = list(now[1]), draw(0, 1)
+        if x < 0.3 or not line:
             moves = [(names[int(draw(0, len(names)))], draw(-2, 2)) for _ in range(int(draw(1, 9)))]
         else:
-            one, wide, by = names[int(draw(0, len(names)))], draw(0.5, 6), draw(-2, 2)
-            t, a = ops[like[one][0]]["at"][0], key[like[one][0]]
-            moves = [(k, by) for k in names if k[1] == one[1] and ops[like[k][0]]["at"][0] == t and a <= key[like[k][0]] <= a + wide]
+            if x < 0.5:
+                i, wide, by = like[names[int(draw(0, len(names)))]][0], draw(0.5, 6), draw(-2, 2)
+                a = key[i]
+            else:
+                i, d = line[int(draw(0, len(line)))]
+                if x < 0.75:
+                    wide, by = draw(0, 3), key[d] - key[i] - draw(0.01, 1)
+                    a = key[i] - wide
+                else:
+                    wide, by, i = draw(0, 3), key[i] - key[d] + draw(0.01, 1), d
+                    a = key[i]
+            moves = [(kin[j], by) for j in kin if ops[j]["at"][1] == ops[i]["at"][1] and a <= key[j] <= a + wide]
         for k, by in moves:
             for i in like[k]:
                 key[i] += by
         new = settle(key)
-        now, best = new if new[0] <= now[0] + 0.1 else now, min(best, new)
+        if new[0] <= now[0] + CFG["slack"] * (1 - m / CFG["moves"]):
+            now, line = new, queued(*new)
+        best = min(best, new)
     return sorted(range(n), key=lambda i: (best[1][i], i)), best[1], best[0], min(tries)[0]
 
 
@@ -196,29 +222,31 @@ def rank_program(g, core, T, topo):
     half = lambda u: slice(64 * u, 64 * u + 64)
     X0, XP0, _ = own(0)
     X1, XP1, _ = own(1)
-    before = []
+    load("S", "ab", 3.0, ["ab0_0", "ab0_1"], [(T.abI[half(u), 16 * s + 8 * q:16 * s + 8 * q + 8], x[half(s), 8 * u:8 * u + 8]) for s in sets for q, x in enumerate((T.la, T.lb)) for u in (0, 1)])
+    i = load("Y", "dl", 2.6, ["dl0"], [(T.dls[half(u), 128 * s:128 * s + 128], T.dl[half(s), 128 * u:128 * u + 128]) for s in sets for u in (0, 1)])
+    i = load("Y", "th", 2.6, ["thI"], [(T.thI[0:8, 0:1], T.th[:])], order=[i])
+    before = [load("Y", "wt", 2.6, ["wt"], [(own(s)[1](64 * u, "wt_", 0, 1), T.wt[half(s)]) for s in sets for u in (0, 1)], order=[i])]
     for s in sets:
         for h in (0, 1):
-            before = [load("Y", "co%d%d" % (s, h), 3.4 + 1.4 * h + 4.2 * s, ["col%d_%d" % (h, s)], [(XP1(64 * s, "suI", 1280 * h, 1280 * h + 1280), T.co[half(s), 1280 * h:1280 * h + 1280])], order=before)]
-        before = [load("Y", "x%d" % s, 6.2 + 5.5 * s, ["X_1" if s else "Xa_0"], [(own(s)[1](64 * u, "Xw", 0, 2560), T.x0[half(s), :]) for u in range(s + 1)], order=before)]
-    su0 = load("Y", "su0", 17.0, ["su_0"], [(XP0(64 * u, "suI", 0, 2560), T.su[0:64, :]) for u in (0, 1)], order=before)
-    i = load("S", "ab", 2.5, ["ab0_0", "ab0_1"], [(T.abI[half(u), 16 * s + 8 * q:16 * s + 8 * q + 8], x[half(s), 8 * u:8 * u + 8]) for s in sets for q, x in enumerate((T.la, T.lb)) for u in (0, 1)])
-    i = load("S", "dl", 2.5, ["dl0"], [(T.dls[half(u), 128 * s:128 * s + 128], T.dl[half(s), 128 * u:128 * u + 128]) for s in sets for u in (0, 1)], order=[i])
-    i = load("S", "th", 3, ["thI"], [(T.thI[0:8, 0:1], T.th[:])], order=[i])
-    load("S", "wt", 3, ["wt"], [(own(s)[1](64 * u, "wt_", 0, 1), T.wt[half(s)]) for s in sets for u in (0, 1)], order=[i])
+            before = [load("Y", "co%d%d" % (s, h), 3.6 + 1.4 * h + 4.2 * s, ["col%d_%d" % (h, s)], [(XP1(64 * s, "suI", 1280 * h, 1280 * h + 1280), T.co[half(s), 1280 * h:1280 * h + 1280])], order=before)]
+        before = [load("Y", "x%d" % s, 6.4 + 5.5 * s, ["X_1" if s else "Xa_0"], [(own(s)[1](64 * u, "Xw", 0, 2560), T.x0[half(s), :]) for u in range(s + 1)], order=before)]
+    su0 = load("Y", "su0", 17.2, ["su_0"], [(XP0(64 * u, "suI", 0, 2560), T.su[0:64, :]) for u in (0, 1)], order=before)
     for s in sets:
         X, XP, K = own(s)
         for h in (0, 1):
             a, b = 1280 * h, 1280 * h + 1280
             vop(1280, [K("col%d" % h)], [K("coa%d" % h)], cp(XP(64 * s, "coF", a, b), XP1(64 * s, "suI", a, b)))
-            sop(1280, [K("coa%d" % h)], [K("cob%d" % h)], act(XP(64 - 64 * s, "coF", a, b), XP(64 * s, "coF", a, b), AF.Copy))
+            if CFG["cob"][2 * s + h] == "S":
+                sop(1280, [K("coa%d" % h)], [K("cob%d" % h)], act(XP(64 - 64 * s, "coF", a, b), XP(64 * s, "coF", a, b), AF.Copy))
+            else:
+                load("S", "cob%d%d" % (s, h), 4.5, [K("cob%d" % h)], [(XP(64 - 64 * s, "coF", a, b), XP(64 * s, "coF", a, b))], r=[K("coa%d" % h)])
     vop(2560, ["Xa_0"], ["X_0"], cp(XP0(64, "Xw", 0, 2560), XP0(0, "Xw", 0, 2560)), 0.5)
     load("Y", "su1", 10.0, ["su_1", "col0_0", "col1_0", "col0_1", "col1_1"], [(XP1(64 * u, "suI", 0, 2560), T.su[64:128, :]) for u in (0, 1)], order=[su0])
 
     pF = lambda c: T.pF[:, c:c + 1]
     pT = lambda c: T.pT[:, 4 * c:4 * c + 1]
     gop(1, [], ["pI"], ioi(T.pI[:, 0:1], [[0, 1]], 0, 1))
-    gop(512, [], ["jm"], iof(T.jm[:], [[0, 32], [1, 16]], 0))
+    gop(256, [], ["jm"], iof(T.jm[:], [[0, 16], [1, 16]], 0))
     for c, (a, b) in enumerate(((0, 15), (0, 112), (0, 64), (0, 7), (0, 16), (3, 1))):
         vop(1, ["pI"], ["pT%d" % c], ts(pT(c), T.pI[:, 0:1], a, b, OP.logical_shift_right, OP.bitwise_and))
     vop(1, ["pT0"], ["p16"], cp(pF(0), pT(0)))
@@ -227,13 +255,13 @@ def rank_program(g, core, T, topo):
     vop(1, ["pT2"], ["p128"], ts(pF(5), pT(2), 2.0, None, OP.mult))
     vop(256, ["jm", "p16"], ["dm"], ts(T.dm[:], T.jm[:, 0:256], pF(0), None, OP.is_equal))
     vop(128, ["jm", "p15"], ["dmr"], ts(T.dmr[:], T.jm[:, 0:128], pF(1), 4096.0, OP.is_equal, OP.mult))
-    sop(512, ["jm"], ["segN"], act(T.segN[:], T.jm[:], AF.Identity, scale=-1e9, bias=5e8))
+    sop(256, ["jm"], ["segN"], act(T.segN[:], T.jm[:], AF.Identity, scale=-1e9, bias=5e8))
     sop(256, ["jm"], ["segX"], act(T.segX[:], T.jm[:, 0:256], AF.Identity, scale=1e9))
     sop(128, ["jm"], ["seg1"], act(T.seg1[:], T.jm[:, 0:128], AF.Sign))
     gop(1024, [], ["rN"], iof(T.rN[:], [[0, 64], [-64, 16]], 64))
     gop(1024, [], ["rX"], iof(T.rX[:], [[0, 64], [64, 16]], 0))
-    gop(32, [], ["eI"], ioi(T.eI[:, 0:32], [[16, 32]], 15, 0))
-    vop(32, ["eI"], ["LE"], cp(T.LE[:], T.eI[:, 0:32]))
+    gop(16, [], ["eI"], ioi(T.eI[:, 0:16], [[16, 16]], 15, 0))
+    vop(16, ["eI"], ["LE"], cp(T.LE[:], T.eI[:, 0:16]))
     vop(128, [], ["onesB"], fill(T.onesB[:], 1.0))
     vop(128, [], ["onesF"], fill(T.onesF[:], 1.0))
     gop(128, ["onesF"], ["identF"], sel(T.identF[:], T.onesF[:], [[-1, 128]], OP.is_equal, 0, 1))
@@ -270,8 +298,7 @@ def rank_program(g, core, T, topo):
     for j in range(16):
         gop(128, ["grp"], [sel_t[j]], sel(T.selX[:, 128 * j:128 * j + 128], T.grp[:], [[0, 8], [1, 16]], OP.is_equal, -j, 0))
     for u in (0, 1):
-        gop(128, ["onesF"], ["dupF%d" % u], sel(T.dupF[:, 128 * u:128 * u + 128], T.onesF[:], [[0, 2], [-1, 64]], OP.is_equal, 64 * u - 64, 1))
-    sop(256, ["dupF0", "dupF1"], ["dupB"], act(T.dupB[:], T.dupF[:], AF.Copy))
+        gop(128, ["onesB"], ["dup%d" % u], sel(T.dupB[:, 128 * u:128 * u + 128], T.onesB[:], [[0, 2], [-1, 64]], OP.is_equal, 64 * u - 64, 1))
     gop(128, ["onesB"], ["triI"], sel(T.triI[:], T.onesB[:], [[1, 128]], OP.is_ge, 0, -1))
     gop(128, ["onesB"], ["triS"], sel(T.triS[:], T.onesB[:], [[1, 128]], OP.is_gt, 0, -1))
     gop(256, [], ["iotaB"], iof(T.iotaB[:], [[1, 256]], 0))
@@ -294,8 +321,8 @@ def rank_program(g, core, T, topo):
     vop(1, ["pT5", "pF7"], ["pF8"], tt(pF(8), pT(5), pF(7), OP.add))
     gop(8, [], ["eI3"], ioi(T.eI[:, 40:48], [[2, 8]], 0, 0))
     vop(8, ["eI3", "pF8"], ["LP"], ts(T.LP[:], T.eI[:, 40:48], pF(8), None, OP.add))
-    vop(576, [], ["mE"], fill(T.mE[:], 1.0), 0.5)
-    vop(16, ["jm", "p15", "mE"], ["mE0"], ts(T.mE[:, 0:16], T.jm[:, 0:16], pF(1), None, OP.is_gt))
+    vop(576, [], ["mE"], fill(T.mE[:], 0.0 if CFG["eq"] == "S" else 1.0), 0.5)
+    vop(16, ["jm", "p15", "mE"], ["mE0"], ts(T.mE[:, 0:16], T.jm[:, 0:16], pF(1), *((4096.0, OP.is_le) if CFG["eq"] == "S" else (1.0, OP.is_gt)), OP.mult))
     for c in range(1, 8):
         sop(16, ["mE0", "mE"], ["mE%d" % c], act(T.mE[:, 8 * c * (c + 1):8 * c * (c + 1) + 16], T.mE[:, 0:16], AF.Copy))
     mE_t = ["mE%d" % c for c in range(8)]
@@ -308,7 +335,11 @@ def rank_program(g, core, T, topo):
         gop(128, ["onesF"], [K("gT")], sel(T.gT[0:8, 128 * s:128 * s + 128], T.onesF[0:8, :], [[0, 2], [1, 4], [0, 16]], OP.is_equal, 4 * s, -1))
         vop(1, ["wt"], [K("wtF")], cp(pF(10 + s), X("wt_", 0, 1)))
         for h in (0, 1):
-            sop(1024, sel_t[8 * h:8 * h + 8] + [K("wtF")], [K("WT%d" % h)], act(X("WT", 1024 * h, 1024 * h + 1024), T.selX[:, 1024 * h:1024 * h + 1024], AF.Identity, scale=pF(10 + s)))
+            r, w, to, fr = sel_t[8 * h:8 * h + 8] + [K("wtF")], [K("WT%d" % h)], X("WT", 1024 * h, 1024 * h + 1024), T.selX[:, 1024 * h:1024 * h + 1024]
+            if CFG["wt"][2 * s + h] == "S":
+                sop(1024, r, w, act(to, fr, AF.Identity, scale=pF(10 + s)))
+            else:
+                vop(1024, r, w, ts(to, fr, X("wt_", 0, 1), None, OP.mult), 0.5)
         gop(128, [], [K("co2")], iof(X("coF", 2560), [[1, 128]], 2560))
         gop(256, [], [K("su2")], ioi(X("suI", 2560), [[0, 256]], 0, 0))
         gop(128, [], [K("Fc")], iof(X("Fc"), [[0, 128]], 0))
@@ -368,8 +399,8 @@ def rank_program(g, core, T, topo):
                 if path[q] == "V":
                     continue
                 a, P, m = 512 * q, bank(), X(Mb, 512 * q, 512 * q + 512)
-                sg(512, [xt, K(lst)], blk("gF", q), act(X("gF", a, a + 512), win(lst, 0, q, 1), AF.Copy))
-                pop(1024, ["ident"] + blk("gF", q) + sht, [P], [mm(T[P][:], T.ident[:], sh(a, 512), True, False), mm(T[P][:], T.ident[:], X("gF", a, a + 512), False, True)])
+                sg(512, [xt, K(lst)], blk("az", q), act(X("az", a, a + 512), win(lst, 0, q, 1), AF.Copy))
+                pop(1024, ["ident"] + blk("az", q) + sht, [P], [mm(T[P][:], T.ident[:], sh(a, 512), True, False), mm(T[P][:], T.ident[:], X("az", a, a + 512), False, True)])
                 if path[q] == "S":
                     vop(512, [], [P] + blk(Mb, q), ts(m, T[P][:], 0.0, 63.0, OP.max, OP.min))
                 else:
@@ -401,11 +432,14 @@ def rank_program(g, core, T, topo):
             for q in (2, 3):
                 if path[q] == "C":
                     pop(512, blk("z", q) + g8p_t, [bk], [mm(T[bk][32 * q:32 * q + 32, a + k:b:16], X("z", 512 * q - 1024 + k, 512 * q - 512, 16), T.g8n[:, w:w + n], False, False) for k in range(16)])
-            pop(1024, blk("az", 0, 4) + g8p_t, [bk], [mm(T[bk][:, a + k:b:16], X("az", k, None, 16), T.g8p[:, w:w + n], False, k == 15) for k in range(16)])
+            parts = CFG["sums"][step]
+            for q, c in parts:
+                pop(1024 if c > 1 else 512, blk("az", q, c) + g8p_t, [bk],
+                    [mm(T[bk][32 * q:32 * (q + c), a + k:b:16], X("az", 512 * q + k, 512 * (q + c), 16), T.g8p[:, w:w + n], False, k == 15 and q == parts[-1][0]) for k in range(16)])
 
         vop(16, [K("ab%d" % t)], [K("abU")], cp(X("abU"), cur))
-        vg(256, [K("abU")] + co_t, [K("df")], cp(X("df"), X("coF", 0, 2560).indirect(X("abU"))))
         sg(256, [K("abU")] + co_t, [K("dfF")], act(X("dfF"), X("coF", 0, 2560).indirect(X("abU")), AF.Copy))
+        vop(256, [K("dfF")], [K("df")], cp(X("df"), X("dfF")))
         sop(256, [K("dfF")], [K("dfH")], act(X("dfH"), X("dfF"), AF.Identity, scale=0.03125, bias=159.515625))
         P = T[PK]
         pop(2048, cK_t + [K("dfH"), K("dfF")], [PK], [
@@ -415,9 +449,10 @@ def rank_program(g, core, T, topo):
         first(1, "df", "M")
         second(1, "df", 128, "M")
         sums(1, PK, 0, 512, 0)
-        vop(512, ["segN"], [K("S"), PK], scan(X("S"), T.segN[:], P[:], 1e9, OP.max, OP.min))
-        for h, nm in ((0, "B"), (1, "Bn")):
-            vg(256, [K("S"), "LE", "dm"], [K(nm)], tt(X("B", 256 * h, 256 * h + 256), X("S").indirect(T.LE[:, 16 * h:16 * h + 16]), T.dm[:, 0:256], OP.mult))
+        for h, nm in ((0, "S"), (1, "Sn")):
+            vop(256, ["segN"], [K(nm), PK], scan(X("S", 256 * h, 256 * h + 256), T.segN[:], P[:, 256 * h:256 * h + 256], 1e9, OP.max, OP.min))
+        for h, nm in ((0, ""), (1, "n")):
+            vg(256, [K("S" + nm), "LE", "dm"], [K("B" + nm)], tt(X("B", 256 * h, 256 * h + 256), X("S", 256 * h, 256 * h + 256).indirect(T.LE[:]), T.dm[:], OP.mult))
         P = T[PB]
         part = lambda a, i, last=False: mm(P[:, 0:16], X("B", a, a + 128), T.gB[:, 16 * i:16 * i + 16], False, last)
         pop(512, [K("B")] + gK_t + gB_t, [PB], [mm(P[:, 0:48], X("B", 0, 128), T.gK[:], True, False), part(128, 0)])
@@ -455,8 +490,9 @@ def rank_program(g, core, T, topo):
         for x in (0, 1):
             H = lambda n, x=x: X(n, 64 * x, 64 * x + 64)
             uI, uA, uB = (K("%s%d" % (n, x)) for n in ("uI", "uA", "uB"))
-            pop(1024, blk("E", 2 * x, 2) + blk("WT", 0, 2), [PB], [mm(P[:, 64:128], X("WT", 128 * j, 128 * j + 128), X("E", 1024 * x + j, 1024 * x + 1024, 16), j == 0, j == 15) for j in range(16)])
-            vop(64, [], [uI, PB], cp(H("uI"), P[:, 64:128]))
+            bk = {"A": PA, "B": PB, "D": PD}[CFG["hash"][x]]
+            pop(1024, blk("E", 2 * x, 2) + blk("WT", 0, 2), [bk], [mm(T[bk][:, 64:128], X("WT", 128 * j, 128 * j + 128), X("E", 1024 * x + j, 1024 * x + 1024, 16), j == 0, j == 15) for j in range(16)])
+            vop(64, [], [uI, bk], cp(H("uI"), T[bk][:, 64:128]))
             vop(64, [uI], [uI], ts(H("uI"), H("uI"), 4095, None, OP.bitwise_and))
             vop(64, [uI], [uB], ts(H("uB"), H("uI"), 1184.0, None, OP.add))
             vop(64, [uI, uB], [uA], tt(H("uA"), H("uI"), H("uB"), OP.mult), 2)
@@ -479,16 +515,25 @@ def rank_program(g, core, T, topo):
         vop(8, [K("jI")], [K("eO")], cp(X("eO"), X("jI")))
         sg(128, blk("E", 0, 4) + [K("eO")], [K("eS")], act(X("eS"), X("E").indirect(X("eO")), AF.Copy))
         vop(16, [K("nS")], [K("oD")], cp(X("oD"), X("nS")))
-        sg(256, [K("oD"), K("co2")] + co_t, [K("T1")], act(X("T1"), X("coF").indirect(X("oD")), AF.Copy))
+        far = CFG["eq"] == "S"
+        sg(256, [K("oD"), K("co2")] + co_t, [K("T1")], act(X("T1"), X("coF").indirect(X("oD")), AF.Identity, scale=-1.0 if far else 1.0))
         vop(256, [K("T1")], [K("T2")], lambda: V.transpose(X("T2"), X("T1")))
+        if far:
+            vop(16, [K("nS")], [K("nK")], ts(X("nK"), X("nS"), 4096.0, None, OP.mult))
+            sop(8, [K("nS")], [K("nM")], act(X("nM"), X("nS", 0, None, 2), AF.Identity, scale=-1.0))
         for c in range(8):
             a, n = 8 * c * (c + 1), 16 * (c + 1)
-            vop(n, [K("nS")], [PK, K("EQ%d" % c)], ts(X("EQ", a, a + n), Pk[:, 128 - n:128], X("nS", 2 * c, 2 * c + 1), None, OP.is_equal))
-        vop(576, blk("EQ", 0, 8) + mE_t, [K("EK")], scan(X("EK"), X("EQ"), T.mE[:], 0.0, OP.max, OP.min), 0.5)
-        vg(128, [K("EK"), "LD", "idxR"], [K("nt")], tt(X("nt"), X("EK").indirect(T.LD[:]), T.idxR[:], OP.mult))
-        vg(128, [K("T2"), "LP", K("nt")], [K("fm")], tt(X("fm"), X("T2").indirect(T.LP[:]), X("nt"), OP.max))
-        vop(128, [K("fm")], [K("fL")], cp(X("fL"), X("fm")))
-        vop(8, [K("nt"), K("nS")], [K("nl")], tt(X("nl"), X("nt", 0, 8), X("nS", 0, None, 2), OP.max))
+            if far:
+                sop(n, [K("nK")], [PK, K("EQ%d" % c)], act(X("EQ", a, a + n), Pk[:, 128 - n:128], AF.Abs, scale=-4096.0, bias=X("nK", 2 * c, 2 * c + 1)))
+            else:
+                vop(n, [], [K("EQ%d" % c), PK, PA], ts(X("EQ", a, a + n), Pk[:, 128 - n:128], Q[:, 2 * c:2 * c + 1], None, OP.is_equal))
+        for h, (c0, c1) in enumerate(((0, 6), (6, 8))):
+            a, b = 8 * c0 * (c0 + 1), 8 * c1 * (c1 + 1)
+            vop(b - a, blk("EQ", c0, c1 - c0) + mE_t, blk("EK", h), scan(X("EK", a, b), X("EQ", a, b), T.mE[:, a:b], 0.0, *((OP.min, OP.max) if far else (OP.max, OP.min))), 0.5)
+        vg(128, blk("EK", 0, 2) + ["LD", "idxR"], [K("nt")], tt(X("nt"), X("EK").indirect(T.LD[:]), T.idxR[:], OP.subtract if far else OP.mult))
+        vg(128, [K("T2"), "LP", K("nt")], [K("fm")], tt(X("fm"), X("T2").indirect(T.LP[:]), X("nt"), OP.min if far else OP.max))
+        vop(128, [K("fm")], [K("fL")], ts(X("fL"), X("fm"), -1.0 if far else 1.0, None, OP.mult))
+        vop(8, [K("nt"), K("nM" if far else "nS")], [K("nl")], tt(X("nl"), X("nt", 0, 8), X("nM") if far else X("nS", 0, None, 2), OP.min if far else OP.max))
         for k in range(16):
             off = X("fL", 8 * k, 8 * k + 8)
             c = CFG["flags"][k]
@@ -497,11 +542,13 @@ def rank_program(g, core, T, topo):
             else:
                 vop(128, [K("fL"), K("stv")], [K("F" + c)], cp(X("F" + c).indirect(off), X("stv")), SC)
 
-        pop(768, [K("eS"), K("nl"), "dupB", "dupF0", "dupF1"], [PA],
-            [mm(Q[:, 128 * u:128 * u + 128], T.dupB[:, 128 * u:128 * u + 128], X("eS"), True, True) for u in (0, 1)]
-            + [mm(Q[:, 256 + 8 * u:264 + 8 * u], T.dupF[:, 128 * u:128 * u + 128], X("nl"), True, True) for u in (0, 1)])
-        sop(256, [], [PA, K("eD")], act(X("eD"), Q[:, 0:256], AF.Copy))
-        vop(16, [], [PA, K("oU")], cp(X("oU"), Q[:, 256:272]))
+        def spread(to, fr, w):
+            op("Y", CFG["near"], [K(fr)], [K(to)], [(lambda u=u, v=v: g.sync.dma_start(XP(64 * v, to, w * u, w * u + w), XP(64 - 64 * u, fr))) for u in (0, 1) for v in (0, 1)],
+               "d%s%d" % (to, s), 16, True)
+
+        vop(8, [K("nl")], [K("oN")], ts(X("oN"), X("nl"), -1.0 if CFG["eq"] == "S" else 1.0, None, OP.mult))
+        spread("oU", "oN", 8)
+        spread("eD", "eS", 128)
         for u in (0, 1):
             vop(128, [K("eD"), K("oU")], [xt], cp(X("Xw").indirect(X("oU", 8 * u, 8 * u + 8)), X("eD", 128 * u, 128 * u + 128)), SC)
         if t == R - 1:
@@ -510,6 +557,10 @@ def rank_program(g, core, T, topo):
         F = lambda nm, o, w, last: [mm(P[:, 128 + m:256:16], X(nm, o + m, o + 1536, 12), w, False, last and m == 11) for m in range(12)]
         pop(128, [K("Fc"), "idBig"], [PB], [mm(P[:, 128:256], T.idBig[:], X("Fc"), True, False)])
         for c in WINDOWS:
+            if c in CFG["turned"]:
+                gop(1536, [K("F" + c)], blk("gF", 0, 3), sel(X("gF", 0, 1536), X("F" + c, 1024, 2560), [[0, 1536]], OP.is_ge, 1, 0))
+                pop(768, blk("gF", 0, 3) + ["g4B"], [PB], F("gF", 0, T.g4B[:], c == WINDOWS[-1]))
+                continue
             pop(3072 if c in "AB" else 768, [K("F" + c), "g4F0", "g4F1", "g4B"], [PB], F("F" + c, 1024, T.g4F[:] if c in "AB" else T.g4B[:], c == WINDOWS[-1]))
         vop(128, [], [K("Fp"), PB], ts(X("Fp"), P[:, 128:256], 448.0 * 8 ** t, None, OP.is_ge))
         vop(128, [K("Fp"), "seg1"], [K("Fi")], scan(X("Fi"), T.seg1[:], X("Fp"), 0.0, OP.mult, OP.add), 0.5)
@@ -531,25 +582,23 @@ def rank_program(g, core, T, topo):
         pop(1024, [K("D")] + sel_t, [PB], [mm(P[:, 0:8], T.selX[:, 128 * p:128 * p + 128], X("D", p, None, 16), False, p == 15) for p in range(16)])
         vop(8, [], [K("vL"), PB], cp(X("vL"), P[:, 0:8]))
         vg(128, [K("vL"), K("su"), K("su2")], [K("sR")], cp(X("sR"), X("suI").indirect(X("vL"))))
-        sop(8, [], [K("vF"), PB], act(X("vF"), P[:, 0:8], AF.Copy))
+        spread("vD", "vL", 8)
         if t < R - 1:
             pop(384, [K("Fi"), K("tot"), K("Fp"), "ident", "triS", "id4k"], [PD], [
                 mm(D[:, 128:256], T.ident[:], X("Fi"), True, False), mm(D[:, 128:256], T.triS[:], X("tot"), False, False), mm(D[:, 128:256], T.id4k[:], X("Fp"), False, True)])
             sop(128, [], [PD, K("Fc")], act(X("Fc"), D[:, 128:256], AF.Relu, bias=-4352.0))
-        pop(512, [K("vF"), "dupF0", "dupF1"], [PD], [mm(D[:, 256 + 8 * u:264 + 8 * u], T.dupF[:, 128 * u:128 * u + 128], X("vF"), True, True) for u in (0, 1)])
-        vop(16, [], [PD, K("vD")], cp(X("vD"), D[:, 256:272]))
-        for e in "SV":
-            for q, n in runs(CFG["renew"], e, 1):
-                a, b = 512 * q, 512 * (q + n)
-                if e == "S":
-                    sg(512 * n, [xt, K("sR")], blk("gF", q, n), act(X("gF", a, b), win("sR", 0, q, n), AF.Copy))
-                else:
-                    vg(512 * n, [xt, K("sR")], blk("gF", q, n), cp(X("gF", a, b), win("sR", 0, q, n)))
-        for q, n in CFG["scans"]:
-            a, b = 512 * q, 512 * (q + n)
-            vop(512 * n, blk("gF", q, n) + ["rX"], blk("E", q, n), scan(X("E", a, b), T.rX[:, 0:b - a], X("gF", a, b), 0.0, OP.min, OP.max), 0.5)
-            vop(512 * n, blk("gF", q, n) + ["rN"], blk("az", q, n), scan(X("az", a, b), T.rN[:, 0:b - a], X("gF", a, b), 64.0, OP.max, OP.min), 0.5)
-        pop(512, blk("E", 0, 4) + blk("az", 0, 4) + ["dupB"], [PA],
+        done = []
+        for e, (a, n) in zip(CFG["renew"], CFG["ren"]):
+            b, of = a + n, lambda nm: blk(nm, a // 512, (a + n - 1) // 512 - a // 512 + 1)
+            got, w = K("gR%d" % a), X("Xw", 0, 2560).indirect(X("sR", a // 16, b // 16))
+            if e == "S":
+                sg(n, [xt, K("sR")] + of("gF"), [got], act(X("gF", a, b), w, AF.Copy))
+            else:
+                vg(n, [xt, K("sR")] + of("gF"), [got], cp(X("gF", a, b), w))
+            vop(n, [got, "rX"] + of("E") + of("gF"), [K("mx%d" % a)], scan(X("E", a, b), T.rX[:, 0:n], X("gF", a, b), 0.0, OP.min, OP.max), 0.5)
+            vop(n, [got, "rN"] + of("az") + of("gF"), [K("mn%d" % a)], scan(X("az", a, b), T.rN[:, 0:n], X("gF", a, b), 64.0, OP.max, OP.min), 0.5)
+            done += [K("mx%d" % a), K("mn%d" % a)]
+        pop(512, done + blk("E", 0, 4) + blk("az", 0, 4) + ["dup0", "dup1"], [PA],
             [mm(Q[:, 128 * u:128 * u + 128], T.dupB[:, 128 * u:128 * u + 128], X(nm, 15, None, 16), nm == "E", nm == "az") for u in (0, 1) for nm in ("E", "az")])
         vop(256, [], [K("rI"), PA], ts(X("rI"), Q[:, 0:256], 0.5, -0.25, OP.mult, OP.add))
         vop(256, [K("rI"), K("vD")], [xt], cp(X("Xw").indirect(X("vD")), X("rI")), SC)

from concourse.mybir import AluOpType as OP, ActivationFunctionType as AF

R = 4
MID = 8096
WINDOWS = "AVB"
SCRATCH = {}
for _n, _w, _t in [
        ("dls", 1024, "bfloat16"),
        ("ident", 128, "bfloat16"), ("nident", 128, "bfloat16"), ("idC", 512, "bfloat16"), ("idBig", 128, "bfloat16"), ("id4k", 128, "bfloat16"),
        ("identF", 128, "float32"), ("id64F", 128, "float32"), ("antiF", 256, "float32"), ("grp", 128, "bfloat16"), ("onesF", 128, "float32"), ("onesB", 128, "bfloat16"),
        ("c32", 128, "bfloat16"), ("cK", 768, "bfloat16"), ("selX", 2048, "bfloat16"),
        ("dupB", 256, "bfloat16"), ("triI", 128, "bfloat16"), ("triS", 128, "bfloat16"),
        ("g8", 8, "float32"), ("g8p", 48, "bfloat16"), ("g8n", 48, "bfloat16"), ("gK", 48, "float32"), ("gB", 64, "float32"), ("gN", 24, "float32"), ("g4B", 8, "bfloat16"), ("g4F", 8, "float32"),
        ("jm", 256, "float32"), ("dm", 256, "float32"), ("dmr", 128, "float32"), ("segN", 256, "float32"), ("segX", 256, "float32"), ("seg1", 128, "bfloat16"),
        ("rN", 1024, "bfloat16"), ("rX", 1024, "bfloat16"), ("mE", 576, "bfloat16"), ("iotaB", 256, "bfloat16"), ("w12", 16, "bfloat16"), ("c1k", 8, "bfloat16"),
        ("rk", 128, "float32"), ("idx", 16, "float32"), ("idxR", 128, "float32"), ("EB", 8, "float32"), ("pI", 8, "int32"), ("pT", 64, "int32"), ("pF", 16, "float32"),
        ("eI", 64, "int32"), ("LE", 16, "uint16"), ("LX", 8, "uint16"), ("LP", 8, "uint16"), ("LD", 8, "uint16"),
        ("thI", 8, "int32"), ("thF", 8, "float32"), ("gT", 256, "float32"),
        ("thr", 8, "float32"), ("th16", 8, "float32"), ("acc", 8, "float32"), ("acJ", 16, "int32"), ("junk", 8, "float32"),
        ("abI", 32, "int32"), ("land", 96, "float32"), ("abo", 128, "float32")]:
    SCRATCH[_n] = ("sbuf", [128, _w], _t)
OWN = {}
for _n, _w, _t in [
        ("Xw", 2816, "bfloat16"), ("coF", 2688, "float32"), ("suI", 2816, "int32"),
        *[("F" + c, 2688, "float32" if c in "AB" else "bfloat16") for c in WINDOWS], ("sh", 2048, "bfloat16"), ("stv", 128, "bfloat16"), ("sts", 128, "float32"), ("M", 2048, "bfloat16"), ("E", 2048, "bfloat16"), ("z", 1024, "bfloat16"), ("az", 2048, "bfloat16"), ("gF", 2048, "bfloat16"),
        ("WT", 2048, "bfloat16"), ("wt_", 8, "bfloat16"),
        ("abU", 16, "uint16"), ("df", 256, "uint16"), ("dfF", 256, "float32"), ("dfH", 256, "bfloat16"), ("S", 512, "float32"), ("B", 512, "float32"),
        ("dL", 8, "uint16"), ("dF", 16, "float32"), ("d64", 8, "float32"), ("al", 16, "float32"), ("alI", 16, "float32"), ("ta", 16, "float32"),
        ("sT", 128, "uint16"), ("uI", 128, "int32"), ("uA", 128, "int32"), ("uB", 128, "int32"), ("nO", 128, "uint16"), ("nP", 128, "float32"),
        ("jI", 8, "int32"), ("eO", 8, "uint16"), ("nS", 16, "float32"), ("nt", 128, "float32"), ("fm", 128, "float32"), ("nl", 8, "float32"),
        ("sp", 128, "bfloat16"), ("EQ", 576, "bfloat16"), ("EK", 576, "bfloat16"),
        ("oD", 16, "uint16"), ("oU", 16, "uint16"), ("T1", 256, "float32"), ("T2", 256, "float32"), ("fL", 128, "uint16"),
        ("eS", 128, "bfloat16"), ("eD", 256, "bfloat16"), ("Fp", 128, "bfloat16"), ("Fc", 128, "bfloat16"), ("Fi", 128, "bfloat16"), ("tot", 128, "bfloat16"),
        ("cum", 8, "bfloat16"), ("Th", 1024, "bfloat16"), ("cL", 8, "uint16"), ("Rw", 136, "float32"), ("D", 128, "bfloat16"),
        ("vL", 8, "uint16"), ("oN", 8, "uint16"), ("nK", 16, "float32"), ("nM", 8, "float32"), ("vD", 16, "uint16"), ("sR", 128, "uint16"), ("rI", 256, "int32")]:
    _b = _n if _w > 256 or _n == "wt_" else "small_" + _t
    _at, _w16 = SCRATCH.get(_b, (0, [0, 0]))[1][1], -(-_w // 16) * 16
    SCRATCH[_b] = ("sbuf", [128, _at + 2 * _w16], _t)
    OWN[_n] = (_b, _at, _w16, _w)
for _b in range(8):
    SCRATCH["P%d" % _b] = ("psum", [128, 512], "float32")

LOADS = ["ab", "dl", "co00", "co01", "co10", "co11", "cob00", "cob01", "cob10", "cob11", "x0", "x1", "su0", "su1", "wt", "th"]
SEMAPHORES = (["sv", "ss", "sp", "sg", "ls", "so", "sb0", "sb1"] + ["d%s%d" % (n, s) for n in ("oU", "eD", "vD") for s in (0, 1)] + ["ld_" + n for n in LOADS] + ["rdl%d" % t for t in (1, 2, 3)]
              + ["rab%d%d" % (t, s) for t in (1, 2, 3) for s in (0, 1)])

CFG = {"first": {1: "SVVV", 2: "SVVV"}, "second": {1: "SSSS", 2: "SSSC"}, "renew": "SSSS", "flags": "ABABABABBBBVVVVV", "turned": "", "merge": 2, "scans": ((0, 2), (2, 1), (3, 1)),
       "cum": True, "moves": 3500, "seed": 1, "slack": 0.15, "leads": [6.0 + 0.5 * i for i in range(12)], "wake": 0.2, "pe": 0.6, "fix": 0.015, "far": 14.0, "near": 2.8, "eq": "V", "wt": "VVSS", "sums": {1: ((0, 4),), 2: ((0, 4),)}, "ren": ((0, 768), (768, 640), (1408, 384), (1792, 256)), "hash": "AB", "cob": "SSSS"}
CFG["but"] = {}
PLAN = CFG
CY, GA, SC = 0.83e-3, 1.45, 3.3
ORDER = {}


def schedule(ops):
    n = len(ops)
    cost = [o["c"] for o in ops]
    hold = [0.06 * max(len(o["f"]), 1) if o["async"] else o["c"] for o in ops]
    pred = [[(d, cost[d] + CFG["wake"] if d in o["hard"] else cost[d] if o["e"] == "R" else hold[d]) for d in o["deps"]] for o in ops]
    succ = [[] for _ in ops]
    for i in range(n):
        for d, lag in pred[i]:
            succ[d].append((i, lag))

    def place(order, back):
        at, begin, finish = [0.0] * n, {o["e"]: [] for o in ops}, {o["e"]: [] for o in ops}
        for i in order:
            h, t = hold[i], cost[i] - hold[i] if back else 0.0
            for j, lag in after[i] if back else pred[i]:
                if at[j] + lag > t:
                    t = at[j] + lag
            a, b = begin[ops[i]["e"]], finish[ops[i]["e"]]
            k = m = len(a)
            while k and b[k - 1] > t:
                k -= 1
            while k < m and a[k] < t + h - 1e-9:
                t, k = max(t, b[k]), k + 1
            a.insert(k, t)
            b.insert(k, t + h)
            at[i] = t
        return at

    def settle(key):
        for i in range(n):
            for d, _ in pred[i]:
                if key[d] > key[i]:
                    key[i] = key[d]
        at = place(sorted(range(n), key=lambda i: (key[i], i)), False)
        bk = place(sorted(range(n), key=lambda i: (-at[i], -i)), True)
        again = place(sorted(range(n), key=lambda i: (-bk[i] - hold[i], i)), False)
        return min((max(x[i] + cost[i] for i in range(n)), x) for x in (at, again))

    after = [[(j, hold[j] + lag - hold[i]) for j, lag in succ[i]] for i in range(n)]
    tries = []
    for lead in CFG["leads"]:
        way = [0.0] * n
        for i in range(n - 1, -1, -1):
            way[i] = max([way[j] + lag for j, lag in succ[i]] + [cost[i] + (lead if ops[i]["w"][:1] == ["X_0"] else 0.0)])
        tries.append(settle([-x for x in way]))
    now = best = min(tries)
    like = {}
    for i, o in enumerate(ops):
        if o["at"]:
            name = (o["e"], o["at"][1], tuple(w[:2] if w[:2] == "ab" and w[2] != "U" else w for w in o["w"]))
            like.setdefault(name + (sum(ops[j]["at"] == o["at"] for k in like if k[:3] == name for j in like[k]),), []).append(i)
    names, state = list(like), [CFG["seed"]]

    def draw(lo, hi):
        state[0] = (state[0] * 6364136223846793005 + 1442695040888963407) % 2 ** 64
        return lo + (hi - lo) * (state[0] >> 11) / 2 ** 53

    kin = {i: k for k in names for i in like[k]}

    def queued(end, at):
        ends = {(ops[i]["e"], round(at[i] + hold[i], 6)): i for i in range(n)}
        i, out = max(range(n), key=lambda j: at[j] + cost[j]), []
        while i is not None:
            d = next((d for d, lag in pred[i] if at[d] + lag > at[i] - 1e-6), None)
            if d is None:
                d = ends.get((ops[i]["e"], round(at[i], 6)))
                if d in kin and i in kin:
                    out.append((i, d))
            i = d
        return out

    line = queued(*now)
    for m in range(CFG["moves"]):
        key, x = list(now[1]), draw(0, 1)
        if x < 0.3 or not line:
            moves = [(names[int(draw(0, len(names)))], draw(-2, 2)) for _ in range(int(draw(1, 9)))]
        else:
            if x < 0.5:
                i, wide, by = like[names[int(draw(0, len(names)))]][0], draw(0.5, 6), draw(-2, 2)
                a = key[i]
            else:
                i, d = line[int(draw(0, len(line)))]
                if x < 0.75:
                    wide, by = draw(0, 3), key[d] - key[i] - draw(0.01, 1)
                    a = key[i] - wide
                else:
                    wide, by, i = draw(0, 3), key[i] - key[d] + draw(0.01, 1), d
                    a = key[i]
            moves = [(kin[j], by) for j in kin if ops[j]["at"][1] == ops[i]["at"][1] and a <= key[j] <= a + wide]
        for k, by in moves:
            for i in like[k]:
                key[i] += by
        new = settle(key)
        if new[0] <= now[0] + CFG["slack"] * (1 - m / CFG["moves"]):
            now, line = new, queued(*new)
        best = min(best, new)
    return sorted(range(n), key=lambda i: (best[1][i], i)), best[1], best[0], min(tries)[0]


def runs(path, letter, most):
    out = []
    for q, c in enumerate(path):
        if c == letter:
            if out and out[-1][0] + out[-1][1] == q and out[-1][1] < most:
                out[-1][1] += 1
            else:
                out.append([q, 1])
    return out


def rank_program(g, core, T, topo):
    rank = T.rank_of(core)
    if rank is None:
        return
    N = len(T.cores)
    V, S, PE = g.vector, g.scalar, g.tensor
    ops, lastw, readers, where = [], {}, {}, []

    def op(e, c, r, w, fs, sem=None, val=None, isasync=False, order=()):
        i = len(ops)
        deps, soft = {lastw[t] for t in r if t in lastw}, set(order)
        for t in w:
            if t in lastw:
                (soft if t[0] == "P" and ops[lastw[t]]["e"] == e else deps).add(lastw[t])
            deps.update(readers.get(t, ()))
        for t in r:
            readers.setdefault(t, []).append(i)
        for t in w:
            lastw[t] = i
            readers[t] = []
        deps.discard(i)
        ops.append({"e": e, "c": c, "hard": sorted(deps), "deps": sorted(deps | soft), "f": fs, "sem": sem, "val": val, "async": isasync, "w": w, "at": tuple(where)})
        return i

    esem = {"V": "sv", "S": "ss", "PE": "sp", "G": "sg"}
    vop = lambda n, r, w, f, cy=1.0: op("V", (0.05 if cy in (GA, SC) else CFG["fix"]) + max(n * cy, 64) * CY, r, w, [f])
    sop = lambda n, r, w, f, cy=1.0: op("S", (0.065 if cy in (GA, SC) else CFG["fix"]) + max(n * cy, 64) * CY, r, w, [f])
    vg = lambda n, r, w, f: vop(n, r, w, f, GA)
    sg = lambda n, r, w, f: sop(n, r, w, f, GA)
    pop = lambda cyc, r, w, fs: op("PE", cyc * CY * CFG["pe"], r, w, fs)
    gop = lambda n, r, w, f: op("G", 0.15 + 2 * n * CY, r, w, [f])

    def load(q, name, c, w, pairs, r=(), order=()):
        return op(q, c, r, w, [(lambda a=a, b=b: (g.sync if q == "Y" else S).dma_start(a, b)) for a, b in pairs], "ld_" + name, 16, True, order)

    def ts(out, a, s1, s2, o0, o1=None):
        return (lambda: V.tensor_scalar(out, a, s1, s2, o0)) if o1 is None else (lambda: V.tensor_scalar(out, a, s1, s2, o0, o1))

    tt = lambda out, a, b, o: (lambda: V.tensor_tensor(out, a, b, o))
    cp = lambda out, a: (lambda: V.tensor_copy(out, a))
    fill = lambda out, c: (lambda: V.memset(out, c))
    act = lambda out, a, f, **k: (lambda: S.activation(out, a, f, **k))
    mm = lambda out, l, r, a, b: (lambda: PE.matmul(out, l, r, a, b))
    scan = lambda out, a, b, i, o0, o1: (lambda: V.tensor_tensor_scan(out, a, b, i, o0, o1))
    iof = lambda out, pat, base: (lambda: g.iota(out, pat, base, 0, allow_small_or_imprecise_dtypes=True))
    ioi = lambda out, pat, base, cm: (lambda: g.iota(out, pat, base, cm))
    sel = lambda out, a, pat, o, base, cm: (lambda: g.affine_select(out, a, pat, o, 0.0, base, cm))
    sets = (0, 1)

    def own(s):
        def col(n, a, b, st):
            _, at, step, w = OWN[n]
            return slice(at + s * step + a, at + s * step + (w if b is None else b), st)
        return (lambda n, a=0, b=None, st=1: T[OWN[n][0]][:, col(n, a, b, st)],
                lambda p, n, a=0, b=None, st=1: T[OWN[n][0]][p:p + 64, col(n, a, b, st)],
                lambda n: "%s_%d" % (n, s))

    half = lambda u: slice(64 * u, 64 * u + 64)
    X0, XP0, _ = own(0)
    X1, XP1, _ = own(1)
    load("S", "ab", 3.0, ["ab0_0", "ab0_1"], [(T.abI[half(u), 16 * s + 8 * q:16 * s + 8 * q + 8], x[half(s), 8 * u:8 * u + 8]) for s in sets for q, x in enumerate((T.la, T.lb)) for u in (0, 1)])
    i = load("Y", "dl", 2.6, ["dl0"], [(T.dls[half(u), 128 * s:128 * s + 128], T.dl[half(s), 128 * u:128 * u + 128]) for s in sets for u in (0, 1)])
    i = load("Y", "th", 2.6, ["thI"], [(T.thI[0:8, 0:1], T.th[:])], order=[i])
    before = [load("Y", "wt", 2.6, ["wt"], [(own(s)[1](64 * u, "wt_", 0, 1), T.wt[half(s)]) for s in sets for u in (0, 1)], order=[i])]
    for s in sets:
        for h in (0, 1):
            before = [load("Y", "co%d%d" % (s, h), 3.6 + 1.4 * h + 4.2 * s, ["col%d_%d" % (h, s)], [(XP1(64 * s, "suI", 1280 * h, 1280 * h + 1280), T.co[half(s), 1280 * h:1280 * h + 1280])], order=before)]
        before = [load("Y", "x%d" % s, 6.4 + 5.5 * s, ["X_1" if s else "Xa_0"], [(own(s)[1](64 * u, "Xw", 0, 2560), T.x0[half(s), :]) for u in range(s + 1)], order=before)]
    su0 = load("Y", "su0", 17.2, ["su_0"], [(XP0(64 * u, "suI", 0, 2560), T.su[0:64, :]) for u in (0, 1)], order=before)
    for s in sets:
        X, XP, K = own(s)
        for h in (0, 1):
            a, b = 1280 * h, 1280 * h + 1280
            vop(1280, [K("col%d" % h)], [K("coa%d" % h)], cp(XP(64 * s, "coF", a, b), XP1(64 * s, "suI", a, b)))
            if CFG["cob"][2 * s + h] == "S":
                sop(1280, [K("coa%d" % h)], [K("cob%d" % h)], act(XP(64 - 64 * s, "coF", a, b), XP(64 * s, "coF", a, b), AF.Copy))
            else:
                load("S", "cob%d%d" % (s, h), 4.5, [K("cob%d" % h)], [(XP(64 - 64 * s, "coF", a, b), XP(64 * s, "coF", a, b))], r=[K("coa%d" % h)])
    vop(2560, ["Xa_0"], ["X_0"], cp(XP0(64, "Xw", 0, 2560), XP0(0, "Xw", 0, 2560)), 0.5)
    load("Y", "su1", 10.0, ["su_1", "col0_0", "col1_0", "col0_1", "col1_1"], [(XP1(64 * u, "suI", 0, 2560), T.su[64:128, :]) for u in (0, 1)], order=[su0])

    pF = lambda c: T.pF[:, c:c + 1]
    pT = lambda c: T.pT[:, 4 * c:4 * c + 1]
    gop(1, [], ["pI"], ioi(T.pI[:, 0:1], [[0, 1]], 0, 1))
    gop(256, [], ["jm"], iof(T.jm[:], [[0, 16], [1, 16]], 0))
    for c, (a, b) in enumerate(((0, 15), (0, 112), (0, 64), (0, 7), (0, 16), (3, 1))):
        vop(1, ["pI"], ["pT%d" % c], ts(pT(c), T.pI[:, 0:1], a, b, OP.logical_shift_right, OP.bitwise_and))
    vop(1, ["pT0"], ["p16"], cp(pF(0), pT(0)))
    vop(1, ["pT0"], ["p15"], ts(pF(1), pT(0), -1.0, 15.0, OP.mult, OP.add))
    vop(1, ["pT0"], ["p256"], ts(pF(3), pT(0), 16.0, None, OP.mult))
    vop(1, ["pT2"], ["p128"], ts(pF(5), pT(2), 2.0, None, OP.mult))
    vop(256, ["jm", "p16"], ["dm"], ts(T.dm[:], T.jm[:, 0:256], pF(0), None, OP.is_equal))
    vop(128, ["jm", "p15"], ["dmr"], ts(T.dmr[:], T.jm[:, 0:128], pF(1), 4096.0, OP.is_equal, OP.mult))
    sop(256, ["jm"], ["segN"], act(T.segN[:], T.jm[:], AF.Identity, scale=-1e9, bias=5e8))
    sop(256, ["jm"], ["segX"], act(T.segX[:], T.jm[:, 0:256], AF.Identity, scale=1e9))
    sop(128, ["jm"], ["seg1"], act(T.seg1[:], T.jm[:, 0:128], AF.Sign))
    gop(1024, [], ["rN"], iof(T.rN[:], [[0, 64], [-64, 16]], 64))
    gop(1024, [], ["rX"], iof(T.rX[:], [[0, 64], [64, 16]], 0))
    gop(16, [], ["eI"], ioi(T.eI[:, 0:16], [[16, 16]], 15, 0))
    vop(16, ["eI"], ["LE"], cp(T.LE[:], T.eI[:, 0:16]))
    vop(128, [], ["onesB"], fill(T.onesB[:], 1.0))
    vop(128, [], ["onesF"], fill(T.onesF[:], 1.0))
    gop(128, ["onesF"], ["identF"], sel(T.identF[:], T.onesF[:], [[-1, 128]], OP.is_equal, 0, 1))
    for nm, a, c in (("ident", 0, 1.0), ("nident", 0, -1.0), ("idC", 0, 1.0), ("idC", 128, -2048.0), ("idC", 256, -32.0), ("idC", 384, 1.0),
                     ("idBig", 0, 1048576.0), ("id4k", 0, 4096.0), ("id64F", 0, 64.0)):
        sop(128, ["identF"], ["%s%d" % (nm, a) if nm == "idC" else nm], act(T[nm][:, a:a + 128], T.identF[:], AF.Identity, scale=c))
    gop(128, ["onesF"], ["anti0"], sel(T.antiF[:, 0:128], T.onesF[:], [[1, 128]], OP.is_equal, -127, 1))
    sop(128, ["anti0"], ["anti1"], act(T.antiF[:, 128:256], T.antiF[:, 0:128], AF.Identity, scale=-1.0))
    gop(8, ["onesF"], ["g8"], sel(T.g8[:], T.onesF[:, 0:8], [[-16, 8]], OP.is_ge, 0, 1))
    gop(8, ["g8"], ["g8"], sel(T.g8[:], T.g8[:], [[16, 8]], OP.is_ge, 15, -1))
    for nm, cs in (("g8p", (16.0, 2048.0, 32768.0, 2048.0, 16384.0, 16384.0)), ("gK", (-4096.0, -266240.0, 1.0, 1.0)),
                   ("gB", (32.0, 2048.0, 0.0, 32.0, 0.015625, 1.0, -32.0, -2048.0))):
        for i, c in enumerate(cs):
            sop(8, ["g8"], ["%s%d" % (nm, i)], act(T[nm][:, 8 * i:8 * i + 8], T.g8[:], AF.Identity, scale=c))
    for x in (0, 1):
        sop(8, ["g8"], ["gK%d" % (4 + x)], act(T.gK[:, 32 + x:48:2], T.g8[:], AF.Copy))
        sop(8, ["g8"], ["gN%d" % x], act(T.gN[:, x:16:2], T.g8[:], AF.Identity, scale=-1.0))
        vop(4, ["g8"], ["g4F%d" % x], tt(T.g4F[:, 4 * x:4 * x + 4], T.g8[:, 0:4], T.g8[:, 4:8], OP.add))
    sop(8, ["g8"], ["gN2"], act(T.gN[:, 16:24], T.g8[:], AF.Copy))
    sop(8, ["g4F0", "g4F1"], ["g4B"], act(T.g4B[:], T.g4F[:], AF.Copy))
    g8p_t, gK_t, gB_t = ["g8p%d" % i for i in range(6)], ["gK%d" % i for i in range(6)], ["gB%d" % i for i in range(8)]
    sop(48, g8p_t, ["g8n"], act(T.g8n[:], T.g8p[:], AF.Identity, scale=-1.0))
    g8p_t.append("g8n")
    vop(128, [], ["c32"], fill(T.c32[0:64, :], 0.03125))
    for i, (a, v) in enumerate(((1, 0), (128, -160), (2048, 5120), (128, -160))):
        gop(128, [], ["cK%d" % i], iof(T.cK[0:32, 128 * i:128 * i + 128], [[0, 8], [a, 16]], v))
    for i, v in enumerate((-1.0 * MID, -128.0 * MID, 327680.0 - 2048.0 * MID, -128.0 * MID)):
        vop(128, [], ["cK%d" % (4 + i)], fill(T.cK[32:64, 128 * i:128 * i + 128], v), 0.5)
    gop(256, [], ["cK8"], iof(T.cK[0:32, 512:768], [[0, 16], [-1024, 16]], 15360))
    cK_t = ["c32"] + ["cK%d" % i for i in range(8)] + ["idC%d" % a for a in (0, 128, 256, 384)] + ["identF", "id64F"]
    gop(128, ["onesB"], ["grp"], sel(T.grp[:], T.onesB[:], [[-16, 8], [0, 16]], OP.is_ge, 0, 1))
    gop(128, ["grp"], ["grp"], sel(T.grp[:], T.grp[:], [[16, 8], [0, 16]], OP.is_ge, 15, -1))
    sel_t = ["selX%d" % j for j in range(16)]
    for j in range(16):
        gop(128, ["grp"], [sel_t[j]], sel(T.selX[:, 128 * j:128 * j + 128], T.grp[:], [[0, 8], [1, 16]], OP.is_equal, -j, 0))
    for u in (0, 1):
        gop(128, ["onesB"], ["dup%d" % u], sel(T.dupB[:, 128 * u:128 * u + 128], T.onesB[:], [[0, 2], [-1, 64]], OP.is_equal, 64 * u - 64, 1))
    gop(128, ["onesB"], ["triI"], sel(T.triI[:], T.onesB[:], [[1, 128]], OP.is_ge, 0, -1))
    gop(128, ["onesB"], ["triS"], sel(T.triS[:], T.onesB[:], [[1, 128]], OP.is_gt, 0, -1))
    gop(256, [], ["iotaB"], iof(T.iotaB[:], [[1, 256]], 0))
    gop(16, [], ["w12"], iof(T.w12[:], [[16, 16]], 0))
    gop(16, ["w12"], ["w12"], sel(T.w12[:], T.w12[:], [[0, 16]], OP.is_equal, -127, 1))
    sop(16, ["w12"], ["w12"], act(T.w12[:], T.w12[:], AF.Identity, bias=12.0))
    sop(8, ["onesF"], ["c1k"], act(T.c1k[:], T.onesF[:, 0:8], AF.Identity, scale=1024.0))
    gop(128, [], ["rk"], iof(T.rk[:], [[1, 8], [8, 16]], 0))
    sop(128, ["rk", "p128"], ["rk"], act(T.rk[:], T.rk[:], AF.Identity, bias=pF(5)))
    gop(16, [], ["idx"], iof(T.idx[:], [[16, 8], [0, 2]], 2560))
    sop(16, ["p16", "idx"], ["idx"], act(T.idx[:], T.idx[:], AF.Identity, bias=pF(0)))
    gop(128, [], ["idxR"], iof(T.idxR[:], [[0, 16], [16, 8]], 2560))
    sop(128, ["p16", "idxR"], ["idxR"], act(T.idxR[:], T.idxR[:], AF.Identity, bias=pF(0)))
    gop(8, [], ["EB"], iof(T.EB[:], [[256, 8]], 15))
    sop(8, ["p256", "EB"], ["EB"], act(T.EB[:], T.EB[:], AF.Identity, bias=pF(3)))
    gop(8, [], ["eI2"], ioi(T.eI[:, 32:40], [[-1, 8]], 7, 0))
    vop(8, ["eI2"], ["LX"], cp(T.LX[:], T.eI[:, 32:40]))
    vop(1, ["pT4"], ["pF6"], cp(pF(6), pT(4)))
    vop(1, ["pT3", "pF6"], ["pF7"], ts(pF(7), pT(3), 32.0, pF(6), OP.mult, OP.add))
    vop(1, ["pT5", "pF7"], ["pF8"], tt(pF(8), pT(5), pF(7), OP.add))
    gop(8, [], ["eI3"], ioi(T.eI[:, 40:48], [[2, 8]], 0, 0))
    vop(8, ["eI3", "pF8"], ["LP"], ts(T.LP[:], T.eI[:, 40:48], pF(8), None, OP.add))
    vop(576, [], ["mE"], fill(T.mE[:], 0.0 if CFG["eq"] == "S" else 1.0), 0.5)
    vop(16, ["jm", "p15", "mE"], ["mE0"], ts(T.mE[:, 0:16], T.jm[:, 0:16], pF(1), *((4096.0, OP.is_le) if CFG["eq"] == "S" else (1.0, OP.is_gt)), OP.mult))
    for c in range(1, 8):
        sop(16, ["mE0", "mE"], ["mE%d" % c], act(T.mE[:, 8 * c * (c + 1):8 * c * (c + 1) + 16], T.mE[:, 0:16], AF.Copy))
    mE_t = ["mE%d" % c for c in range(8)]
    vop(1, ["pT3"], ["pF9"], ts(pF(9), pT(3), 8.0, 24.0, OP.mult, OP.add))
    vop(1, ["pT3", "pF9"], ["pF2"], ts(pF(2), pT(3), pF(9), 15.0, OP.mult, OP.add))
    vop(8, ["pF2", "onesF"], ["LD"], ts(T.LD[:], T.onesF[:, 0:8], pF(2), None, OP.mult))
    vop(1, ["thI"], ["thF"], cp(T.thF[0:8, 0:1], T.thI[0:8, 0:1]))
    for s in sets:
        X, XP, K = own(s)
        gop(128, ["onesF"], [K("gT")], sel(T.gT[0:8, 128 * s:128 * s + 128], T.onesF[0:8, :], [[0, 2], [1, 4], [0, 16]], OP.is_equal, 4 * s, -1))
        vop(1, ["wt"], [K("wtF")], cp(pF(10 + s), X("wt_", 0, 1)))
        for h in (0, 1):
            r, w, to, fr = sel_t[8 * h:8 * h + 8] + [K("wtF")], [K("WT%d" % h)], X("WT", 1024 * h, 1024 * h + 1024), T.selX[:, 1024 * h:1024 * h + 1024]
            if CFG["wt"][2 * s + h] == "S":
                sop(1024, r, w, act(to, fr, AF.Identity, scale=pF(10 + s)))
            else:
                vop(1024, r, w, ts(to, fr, X("wt_", 0, 1), None, OP.mult), 0.5)
        gop(128, [], [K("co2")], iof(X("coF", 2560), [[1, 128]], 2560))
        gop(256, [], [K("su2")], ioi(X("suI", 2560), [[0, 256]], 0, 0))
        gop(128, [], [K("Fc")], iof(X("Fc"), [[0, 128]], 0))
        for c in WINDOWS:
            gop(1536, [], [K("F" + c)], iof(X("F" + c, 1024, 2560), [[0, 1536]], 0))
        vop(8, ["p16", "p128", "onesF"], [K("Rw2")], ts(X("Rw", 128), T.onesF[:, 0:8], pF(0), 8.0, OP.add, OP.mult))
        sop(8, [K("Rw2"), "p128"], [K("Rw2")], act(X("Rw", 128), X("Rw", 128), AF.Identity, bias=pF(5)))
    pop(512, ["gT_0", "gT_1", "thF"], ["P3"], [mm(T.P3[:, s:s + 1], T.gT[0:8, 128 * s:128 * s + 128], T.thF[0:8, 0:1], True, True) for s in sets])
    vop(2, [], ["th16", "P3"], ts(T.th16[:, 0:2], T.P3[:, 0:2], 16.0, -1.0 * MID, OP.mult, OP.add))
    vop(2, ["th16"], ["thr"], cp(T.thr[:, 0:2], T.th16[:, 0:2]))

    def send(dst_rank, out, in_, sem, r, w, c=0.8):
        dst = T.cores[dst_rank]
        rid, pid, _ = topo.addr(dst)
        m = sum(1 << e for e in topo.engines(core, dst)[:4])
        i = op("G", c, r + ["sent"] * (c < 1), ["sent"] * (c > 1), [lambda: g.remote_dma(out, in_, T.sem[sem], T.sem.ls, pid, rid, m)], "none", 0)
        op("R", CFG["far"], [], [w], [], sem, 4, True, order=[i])

    for t in (1, 2, 3):
        send((rank + t) % N, T.dls[:, 256 * t:256 * t + 256], T.dls[:, 0:256], "rdl%d" % t, ["dl0"], "dl%d" % t, 0.8 if t > 1 else 6.0)

    def lanes(t, s):
        X, XP, K = own(s)
        where[:] = [t, s]
        CFG = dict(PLAN, **PLAN["but"].get((t, s), {}))
        PK, PA, PB, PD = ("P%d" % (4 * s + i) for i in range(4))
        sht = [K("sh%d" % k) for k in range(16)]
        sh = lambda a, n: X("sh", a, a + n)
        dl = T.dls[:, 256 * t + 128 * s:256 * t + 128 * s + 128]
        for k in range(16):
            if t:
                gop(128, ["dl%d" % t], [sht[k]], sel(X("sh", k, None, 16), dl, [[0, 128]], OP.is_ge, 1, 0))
            elif k % 4:
                vop(128, ["dl0"], [sht[k]], cp(X("sh", k, None, 16), dl), 0.5)
            else:
                sop(128, ["dl0"], [sht[k]], act(X("sh", k, None, 16), dl, AF.Copy))
        for nm in ("stv", "sts"):
            gop(128, [], [K(nm)], iof(X(nm), [[0, 128]], 32 * 8 ** t))
        cur = T.abI[:, 16 * s:16 * s + 16] if t == 0 else T.land[:, 32 * t - 32 + 16 * s:32 * t - 16 + 16 * s]
        nxt = lambda a=0, b=16, p=slice(0, 128): T.abo[p, 32 * t + 16 * s + a:32 * t + 16 * s + b]
        win = lambda lst, lo, q, n: X("Xw", 0, 2560).indirect(X(lst, lo + 32 * q, lo + 32 * (q + n)))
        blk = lambda nm, q, n=1: [K("%s%d" % (nm, i)) for i in range(q, q + n)]
        xt, turn = K("X"), [0]
        co_t = blk("coa", 0, 2) + blk("cob", 0, 2)

        def bank():
            turn[0] += 1
            return PD if turn[0] % 2 else PA

        def first(step, lst, Mb):
            path = CFG["first"][step]
            for q, n in runs(path, "V", CFG["merge"]):
                a, m = 512 * q, X(Mb, 512 * q, 512 * (q + n))
                vg(512 * n, [xt, K(lst)] + sht, blk(Mb, q, n), tt(m, win(lst, 0, q, n), sh(a, 512 * n), OP.add))
                vop(512 * n, blk(Mb, q, n), blk(Mb, q, n), ts(m, m, 0.0, 63.0, OP.max, OP.min), 0.5)
            for q in range(4):
                if path[q] == "V":
                    continue
                a, P, m = 512 * q, bank(), X(Mb, 512 * q, 512 * q + 512)
                sg(512, [xt, K(lst)], blk("az", q), act(X("az", a, a + 512), win(lst, 0, q, 1), AF.Copy))
                pop(1024, ["ident"] + blk("az", q) + sht, [P], [mm(T[P][:], T.ident[:], sh(a, 512), True, False), mm(T[P][:], T.ident[:], X("az", a, a + 512), False, True)])
                if path[q] == "S":
                    vop(512, [], [P] + blk(Mb, q), ts(m, T[P][:], 0.0, 63.0, OP.max, OP.min))
                else:
                    sop(512, [], [P] + blk(Mb, q), act(m, T[P][:], AF.Relu))
                    vop(512, blk(Mb, q), blk(Mb, q), ts(m, m, 63.0, None, OP.min), 0.5)

        def second(step, lst, lo, Mb):
            path, lt = CFG["second"][step], lambda q: K(lst if step == 1 else "%s%d" % (lst, q))
            for q, n in runs(path, "S", 1):
                a, P = 512 * q, bank()
                sg(512, [xt, lt(q)], blk("gF", q), act(X("gF", a, a + 512), win(lst, lo, q, 1), AF.Copy))
                one = (mm(T[P][:], T.ident[:], X("gF", a, a + 512), step == 1, step == 2), ["ident"] + blk("gF", q))
                two = (mm(T[P][:], T.nident[:], X(Mb, a, a + 512), step == 2, step == 1), ["nident"] + blk(Mb, q))
                both = (one, two) if step == 1 else (two, one)
                pop(1024, one[1] + two[1], [P], [f for f, _ in both])
                sop(512, [], [P] + blk("az", q), act(X("az", a, a + 512), T[P][:], AF.Abs))
            for q in (2, 3):
                if path[q] == "S":
                    continue
                a, z = 512 * q, X("z", 512 * q - 1024, 512 * q - 512)
                vg(512, [xt, lt(q)] + blk(Mb, q), blk("z", q), tt(z, win(lst, lo, q, 1), X(Mb, a, a + 512), OP.subtract))
                if path[q] == "V":
                    sop(512, blk("z", q), blk("az", q), act(X("az", a, a + 512), z, AF.Abs))
                else:
                    vop(512, blk("z", q), blk("az", q), ts(X("az", a, a + 512), z, 0.0, 2.0, OP.max, OP.mult), 0.5)

        def sums(step, bk, a, b, w):
            path, n = CFG["second"][step], (b - a) // 16
            for q in (2, 3):
                if path[q] == "C":
                    pop(512, blk("z", q) + g8p_t, [bk], [mm(T[bk][32 * q:32 * q + 32, a + k:b:16], X("z", 512 * q - 1024 + k, 512 * q - 512, 16), T.g8n[:, w:w + n], False, False) for k in range(16)])
            parts = CFG["sums"][step]
            for q, c in parts:
                pop(1024 if c > 1 else 512, blk("az", q, c) + g8p_t, [bk],
                    [mm(T[bk][32 * q:32 * (q + c), a + k:b:16], X("az", 512 * q + k, 512 * (q + c), 16), T.g8p[:, w:w + n], False, k == 15 and q == parts[-1][0]) for k in range(16)])

        vop(16, [K("ab%d" % t)], [K("abU")], cp(X("abU"), cur))
        sg(256, [K("abU")] + co_t, [K("dfF")], act(X("dfF"), X("coF", 0, 2560).indirect(X("abU")), AF.Copy))
        vop(256, [K("dfF")], [K("df")], cp(X("df"), X("dfF")))
        sop(256, [K("dfF")], [K("dfH")], act(X("dfH"), X("dfF"), AF.Identity, scale=0.03125, bias=159.515625))
        P = T[PK]
        pop(2048, cK_t + [K("dfH"), K("dfF")], [PK], [
            mm(P[:], T.c32[0:64, :], T.cK[0:64, 0:512], True, False), mm(P[:, 256:384], X("dfF", 0, 128), T.id64F[:], False, False),
            mm(P[:, 128:384], X("dfH", 0, 128), T.idC[:, 0:256], False, False), mm(P[:, 256:384], X("dfF", 128), T.identF[:], False, False),
            mm(P[:, 256:512], X("dfH", 128), T.idC[:, 256:512], False, False)])
        first(1, "df", "M")
        second(1, "df", 128, "M")
        sums(1, PK, 0, 512, 0)
        for h, nm in ((0, "S"), (1, "Sn")):
            vop(256, ["segN"], [K(nm), PK], scan(X("S", 256 * h, 256 * h + 256), T.segN[:], P[:, 256 * h:256 * h + 256], 1e9, OP.max, OP.min))
        for h, nm in ((0, ""), (1, "n")):
            vg(256, [K("S" + nm), "LE", "dm"], [K("B" + nm)], tt(X("B", 256 * h, 256 * h + 256), X("S", 256 * h, 256 * h + 256).indirect(T.LE[:]), T.dm[:], OP.mult))
        P = T[PB]
        part = lambda a, i, last=False: mm(P[:, 0:16], X("B", a, a + 128), T.gB[:, 16 * i:16 * i + 16], False, last)
        pop(512, [K("B")] + gK_t + gB_t, [PB], [mm(P[:, 0:48], X("B", 0, 128), T.gK[:], True, False), part(128, 0)])
        pop(768, [K("B"), K("Bn")], [PB], [part(384, 1), part(256, 2), part(0, 3, True)])
        vop(8, [], [K("dL"), PB], cp(X("dL"), P[:, 0:8]))
        vop(16, ["thr"], [K("al"), PB], ts(X("al"), P[:, 16:32], T.thr[:, s:s + 1], None, OP.is_lt))
        vop(16, ["thr"], [K("alI"), PB], ts(X("alI"), P[:, 32:48], T.thr[:, s:s + 1], None, OP.is_lt))
        vop(16, [K("alI"), "idx"], [K("alI")], tt(X("alI"), X("alI"), T.idx[:], OP.mult))
        vop(8, [K("dL")], [K("dF")], cp(X("dF", 0, 8), X("dL")))
        sop(8, [K("dF")], [K("d64")], act(X("d64"), X("dF", 0, 8), AF.Identity, scale=-64.0))
        vop(8, [K("d64")], [K("fF"), PB], tt(X("dF", 8), P[:, 8:16], X("d64"), OP.add))
        vop(16, [K("dF"), K("fF"), K("ab%d" % t)], [K("ta")], tt(X("ta"), X("dF"), cur, OP.subtract))
        vop(16, [K("ta"), K("al")], [K("ta")], tt(X("ta"), X("ta"), X("al"), OP.mult))
        vop(16, [K("ta"), K("ab%d" % t)], [K("abo%d" % t)], tt(nxt(), X("ta"), cur, OP.add))
        if t < R - 1:
            send((rank + 1) % N, T.land[:, 32 * t + 16 * s:32 * t + 16 * s + 16], nxt(), "rab%d%d" % (t + 1, s), [K("abo%d" % t)], K("ab%d" % (t + 1)))
            sop(8, [K("al")], [K("acc"), "junk"], act(T.junk[:], X("al", 0, 8), AF.Copy, accum_out=T.acc[:, s:s + 1]))
        else:
            op("Y", 2.0, [K("abo%d" % t)], [], [(lambda y=y, q=q, u=u: g.sync.dma_start(y[half(s), 8 * u:8 * u + 8], nxt(8 * q, 8 * q + 8, half(u))))
                                                for q, y in enumerate((T.ya, T.yb)) for u in (0, 1)], "so", 16, True)
        if t < R - 1 and s == 1:
            Q = T[PD]
            pop(512, ["acc_0", "acc_1", "onesF"], [PD], [mm(Q[:, 0:1], T.onesF[:], T.acc[:, x:x + 1], x == 0, x == 1) for x in sets])
            vop(1, [], ["acI", PD], ts(T.acJ[:, 0:1], Q[:, 0:1], -16.0, 32768.0, OP.mult, OP.add))
            vop(1, ["acI"], ["acJ"], ts(T.acJ[:, 8:9], T.acJ[:, 0:1], 1008, None, OP.bitwise_and))
            vop(1, ["acJ"], ["acF"], cp(T.acc[:, 4:5], T.acJ[:, 8:9]))
            sop(2, ["acF", "th16"], ["thr"], act(T.thr[:, 0:2], T.th16[:, 0:2], AF.Identity, bias=T.acc[:, 4:5]))
        Pk = T[PK]
        vg(128, [K("al"), "LX", "dmr"], [K("sp")], tt(X("sp"), X("al").indirect(T.LX[:]), T.dmr[:], OP.mult))
        pop(128, [K("sp"), "grp"], [PK], [mm(Pk[:, 0:128], T.grp[:], X("sp"), True, False)])

        vg(128, [K("dL"), K("su")], [K("sT")], cp(X("sT"), X("suI", 0, 2560).indirect(X("dL"))))
        first(2, "sT", "E")
        P = T[PB]
        for x in (0, 1):
            H = lambda n, x=x: X(n, 64 * x, 64 * x + 64)
            uI, uA, uB = (K("%s%d" % (n, x)) for n in ("uI", "uA", "uB"))
            bk = {"A": PA, "B": PB, "D": PD}[CFG["hash"][x]]
            pop(1024, blk("E", 2 * x, 2) + blk("WT", 0, 2), [bk], [mm(T[bk][:, 64:128], X("WT", 128 * j, 128 * j + 128), X("E", 1024 * x + j, 1024 * x + 1024, 16), j == 0, j == 15) for j in range(16)])
            vop(64, [], [uI, bk], cp(H("uI"), T[bk][:, 64:128]))
            vop(64, [uI], [uI], ts(H("uI"), H("uI"), 4095, None, OP.bitwise_and))
            vop(64, [uI], [uB], ts(H("uB"), H("uI"), 1184.0, None, OP.add))
            vop(64, [uI, uB], [uA], tt(H("uA"), H("uI"), H("uB"), OP.mult), 2)
            vop(64, [uA], [uI], ts(H("uI"), H("uA"), 5, 1023, OP.arith_shift_right, OP.bitwise_and))
            vop(64, [uI], blk("nO", 2 * x, 2), cp(H("nO"), H("uI")))
            vop(64, [uI], blk("nP", x), cp(H("nP"), H("uI")))
        pop(768, blk("nP", 0, 2) + ["identF", "c32", "cK8"], [PB], [mm(P[:, 256:512], T.c32[0:32, :], T.cK[0:32, 512:768], True, False), mm(P[:, 256:384], X("nP"), T.identF[:], False, False)])
        second(2, "nO", 0, "E")
        sums(2, PB, 256, 512, 32)
        vop(256, ["segX"], [K("S"), PB], scan(X("S", 0, 256), T.segX[:], P[:, 256:512], 0.0, OP.min, OP.max))
        vg(256, [K("S"), "LE", "dm"], [K("B")], tt(X("B", 0, 256), X("S", 0, 256).indirect(T.LE[:, 0:16]), T.dm[:, 0:256], OP.mult))
        sg(256, [K("S"), "LE"], [K("Bn")], act(X("B", 256), X("S", 0, 256).indirect(T.LE[:, 0:16]), AF.Copy))
        Q = T[PA]
        pop(512, [K("B"), "gN0", "gN1", "gN2"] + gK_t, [PA], [mm(Q[:, 0:24], X("B", 128, 256), T.gN[:], True, False), mm(Q[:, 0:16], X("B", 0, 128), T.gK[:, 32:48], False, True)])
        pop(1024, [K("Bn"), "anti0", "anti1"], [PK], [mm(Pk[:, 0:128], X("B", 384), T.antiF[:, 128:256], False, False), mm(Pk[:, 0:128], X("B", 256, 384), T.antiF[:, 0:128], False, True)])
        vop(16, [K("alI")], [K("nS"), PA], tt(X("nS"), Q[:, 0:16], X("alI"), OP.max))
        vop(8, [], [K("jI"), PA], cp(X("jI"), Q[:, 16:24]))
        vop(8, [K("jI")], [K("jI")], ts(X("jI"), X("jI"), 10, 15, OP.logical_shift_right, OP.bitwise_and))
        vop(8, [K("jI"), "EB"], [K("jI")], tt(X("jI"), T.EB[:], X("jI"), OP.subtract))
        vop(8, [K("jI")], [K("eO")], cp(X("eO"), X("jI")))
        sg(128, blk("E", 0, 4) + [K("eO")], [K("eS")], act(X("eS"), X("E").indirect(X("eO")), AF.Copy))
        vop(16, [K("nS")], [K("oD")], cp(X("oD"), X("nS")))
        far = CFG["eq"] == "S"
        sg(256, [K("oD"), K("co2")] + co_t, [K("T1")], act(X("T1"), X("coF").indirect(X("oD")), AF.Identity, scale=-1.0 if far else 1.0))
        vop(256, [K("T1")], [K("T2")], lambda: V.transpose(X("T2"), X("T1")))
        if far:
            vop(16, [K("nS")], [K("nK")], ts(X("nK"), X("nS"), 4096.0, None, OP.mult))
            sop(8, [K("nS")], [K("nM")], act(X("nM"), X("nS", 0, None, 2), AF.Identity, scale=-1.0))
        for c in range(8):
            a, n = 8 * c * (c + 1), 16 * (c + 1)
            if far:
                sop(n, [K("nK")], [PK, K("EQ%d" % c)], act(X("EQ", a, a + n), Pk[:, 128 - n:128], AF.Abs, scale=-4096.0, bias=X("nK", 2 * c, 2 * c + 1)))
            else:
                vop(n, [], [K("EQ%d" % c), PK, PA], ts(X("EQ", a, a + n), Pk[:, 128 - n:128], Q[:, 2 * c:2 * c + 1], None, OP.is_equal))
        for h, (c0, c1) in enumerate(((0, 6), (6, 8))):
            a, b = 8 * c0 * (c0 + 1), 8 * c1 * (c1 + 1)
            vop(b - a, blk("EQ", c0, c1 - c0) + mE_t, blk("EK", h), scan(X("EK", a, b), X("EQ", a, b), T.mE[:, a:b], 0.0, *((OP.min, OP.max) if far else (OP.max, OP.min))), 0.5)
        vg(128, blk("EK", 0, 2) + ["LD", "idxR"], [K("nt")], tt(X("nt"), X("EK").indirect(T.LD[:]), T.idxR[:], OP.subtract if far else OP.mult))
        vg(128, [K("T2"), "LP", K("nt")], [K("fm")], tt(X("fm"), X("T2").indirect(T.LP[:]), X("nt"), OP.min if far else OP.max))
        vop(128, [K("fm")], [K("fL")], ts(X("fL"), X("fm"), -1.0 if far else 1.0, None, OP.mult))
        vop(8, [K("nt"), K("nM" if far else "nS")], [K("nl")], tt(X("nl"), X("nt", 0, 8), X("nM") if far else X("nS", 0, None, 2), OP.min if far else OP.max))
        for k in range(16):
            off = X("fL", 8 * k, 8 * k + 8)
            c = CFG["flags"][k]
            if c in "AB":
                sop(128, [K("fL"), K("sts")], [K("F" + c)], act(X("F" + c).indirect(off), X("sts"), AF.Silu), SC)
            else:
                vop(128, [K("fL"), K("stv")], [K("F" + c)], cp(X("F" + c).indirect(off), X("stv")), SC)

        def spread(to, fr, w):
            op("Y", CFG["near"], [K(fr)], [K(to)], [(lambda u=u, v=v: g.sync.dma_start(XP(64 * v, to, w * u, w * u + w), XP(64 - 64 * u, fr))) for u in (0, 1) for v in (0, 1)],
               "d%s%d" % (to, s), 16, True)

        vop(8, [K("nl")], [K("oN")], ts(X("oN"), X("nl"), -1.0 if CFG["eq"] == "S" else 1.0, None, OP.mult))
        spread("oU", "oN", 8)
        spread("eD", "eS", 128)
        for u in (0, 1):
            vop(128, [K("eD"), K("oU")], [xt], cp(X("Xw").indirect(X("oU", 8 * u, 8 * u + 8)), X("eD", 128 * u, 128 * u + 128)), SC)
        if t == R - 1:
            op("Y", 3.0, [xt], [], [(lambda u=u: g.sync.dma_start(T.yx[half(s), 512 * u:512 * u + 512], XP(64 * u, "Xw", 512 * u, 512 * u + 512))) for u in (0, 1)], "sb%d" % s, 16, True)

        F = lambda nm, o, w, last: [mm(P[:, 128 + m:256:16], X(nm, o + m, o + 1536, 12), w, False, last and m == 11) for m in range(12)]
        pop(128, [K("Fc"), "idBig"], [PB], [mm(P[:, 128:256], T.idBig[:], X("Fc"), True, False)])
        for c in WINDOWS:
            if c in CFG["turned"]:
                gop(1536, [K("F" + c)], blk("gF", 0, 3), sel(X("gF", 0, 1536), X("F" + c, 1024, 2560), [[0, 1536]], OP.is_ge, 1, 0))
                pop(768, blk("gF", 0, 3) + ["g4B"], [PB], F("gF", 0, T.g4B[:], c == WINDOWS[-1]))
                continue
            pop(3072 if c in "AB" else 768, [K("F" + c), "g4F0", "g4F1", "g4B"], [PB], F("F" + c, 1024, T.g4F[:] if c in "AB" else T.g4B[:], c == WINDOWS[-1]))
        vop(128, [], [K("Fp"), PB], ts(X("Fp"), P[:, 128:256], 448.0 * 8 ** t, None, OP.is_ge))
        vop(128, [K("Fp"), "seg1"], [K("Fi")], scan(X("Fi"), T.seg1[:], X("Fp"), 0.0, OP.mult, OP.add), 0.5)
        pop(64, [K("Fi"), "triI"], [PA], [mm(Q[:, 0:8], T.triI[:], X("Fi", 15, None, 16), True, True)])
        if CFG["cum"]:
            vop(8, [], [K("cum"), PA], cp(X("cum"), Q[:, 0:8]))
        for G in range(8):
            c = X("cum", G, G + 1) if CFG["cum"] else Q[:, G:G + 1]
            vop(128, [K("cum"), "iotaB"], [K("Th%d" % G)] + [PA] * (not CFG["cum"]), ts(X("Th", 128 * G, 128 * G + 128), T.iotaB[:, 128 * (G // 4):128 * (G // 4) + 128], c, None, OP.is_ge), 0.5)
        pop(512, blk("Th", 0, 8) + ["onesB"], [PA], [mm(Q[:, 8 + q:9 + q], X("Th", q, None, 8), T.onesB[:, 0:1], True, True) for q in range(8)])
        vop(8, [], [K("cL"), PA], cp(X("cL"), Q[:, 8:16]))
        pop(1088, blk("Th", 0, 8) + ["w12", "c1k", "ident"], [PB], [mm(P[:, 0:8], T.ident[:], T.c1k[:], True, False)]
            + [mm(P[half(u), q:q + 1], X("Th", 512 * u + q, 512 * u + 512, 8), T.w12[:, 8 * u + q:8 * u + q + 1], False, False) for u in (0, 1) for q in range(8)])
        sg(128, [K("Fi"), "LE"], [K("tot")], act(X("tot"), X("Fi").indirect(T.LE[:, 0:8]), AF.Copy))
        D = T[PD]
        pop(256, [K("Fi"), K("tot"), "ident", "triS"], [PD], [mm(D[:, 0:128], X("Fi"), T.ident[:], True, False), mm(D[:, 0:128], X("tot"), T.triS[:], False, True)])
        sop(128, [], [PD, K("Rw")], act(X("Rw", 0, 128), D[:, 0:128], AF.Copy))
        vg(128, [K("Rw"), K("Rw2"), K("cL"), "rk"], [K("D")], tt(X("D"), X("Rw").indirect(X("cL")), T.rk[:], OP.is_le))
        pop(1024, [K("D")] + sel_t, [PB], [mm(P[:, 0:8], T.selX[:, 128 * p:128 * p + 128], X("D", p, None, 16), False, p == 15) for p in range(16)])
        vop(8, [], [K("vL"), PB], cp(X("vL"), P[:, 0:8]))
        vg(128, [K("vL"), K("su"), K("su2")], [K("sR")], cp(X("sR"), X("suI").indirect(X("vL"))))
        spread("vD", "vL", 8)
        if t < R - 1:
            pop(384, [K("Fi"), K("tot"), K("Fp"), "ident", "triS", "id4k"], [PD], [
                mm(D[:, 128:256], T.ident[:], X("Fi"), True, False), mm(D[:, 128:256], T.triS[:], X("tot"), False, False), mm(D[:, 128:256], T.id4k[:], X("Fp"), False, True)])
            sop(128, [], [PD, K("Fc")], act(X("Fc"), D[:, 128:256], AF.Relu, bias=-4352.0))
        done = []
        for e, (a, n) in zip(CFG["renew"], CFG["ren"]):
            b, of = a + n, lambda nm: blk(nm, a // 512, (a + n - 1) // 512 - a // 512 + 1)
            got, w = K("gR%d" % a), X("Xw", 0, 2560).indirect(X("sR", a // 16, b // 16))
            if e == "S":
                sg(n, [xt, K("sR")] + of("gF"), [got], act(X("gF", a, b), w, AF.Copy))
            else:
                vg(n, [xt, K("sR")] + of("gF"), [got], cp(X("gF", a, b), w))
            vop(n, [got, "rX"] + of("E") + of("gF"), [K("mx%d" % a)], scan(X("E", a, b), T.rX[:, 0:n], X("gF", a, b), 0.0, OP.min, OP.max), 0.5)
            vop(n, [got, "rN"] + of("az") + of("gF"), [K("mn%d" % a)], scan(X("az", a, b), T.rN[:, 0:n], X("gF", a, b), 64.0, OP.max, OP.min), 0.5)
            done += [K("mx%d" % a), K("mn%d" % a)]
        pop(512, done + blk("E", 0, 4) + blk("az", 0, 4) + ["dup0", "dup1"], [PA],
            [mm(Q[:, 128 * u:128 * u + 128], T.dupB[:, 128 * u:128 * u + 128], X(nm, 15, None, 16), nm == "E", nm == "az") for u in (0, 1) for nm in ("E", "az")])
        vop(256, [], [K("rI"), PA], ts(X("rI"), Q[:, 0:256], 0.5, -0.25, OP.mult, OP.add))
        vop(256, [K("rI"), K("vD")], [xt], cp(X("Xw").indirect(X("vD")), X("rI")), SC)
        if t == R - 1:
            op("Y", 3.0, [xt], [], [(lambda u=u: g.sync.dma_start(T.yx[half(s), 1024 + 768 * u:1792 + 768 * u], XP(64 * u, "Xw", 1024 + 768 * u, 1792 + 768 * u))) for u in (0, 1)], "so", 16, True)

    for t in range(R):
        for s in sets:
            lanes(t, s)

    if "o" not in ORDER:
        ORDER["o"], ORDER["start"], ORDER["end"], ORDER["lead"] = schedule(ops)
        ORDER["ops"] = ops
    queue = {"V": V, "S": S, "PE": PE, "G": g, "Y": g.sync}
    count, known = {}, {q: {} for q in queue}
    for i in ORDER["o"]:
        o = ops[i]
        e, clk = o["e"], {}
        if e != "R":
            kn = known[e]
            for d in reversed(o["hard"]):
                x = ops[d]
                if x["sem"] != "none" and kn.get(x["s"], 0) < x["n"]:
                    queue[e].wait_ge(T.sem[x["s"]], x["n"])
                    for s, v in x["clk"].items():
                        kn[s] = max(kn.get(s, 0), v)
            clk = dict(kn)
        s = o["sem"] or esem[e]
        inc = 16 if o["sem"] else 1
        for f in o["f"]:
            ins = f()
            if s != "none":
                ins.then_inc(T.sem[s], inc)
                count[s] = count.get(s, 0) + inc
        if e == "R":
            count[s] = o["val"]
        if s != "none":
            o["s"], o["n"] = s, count[s]
            clk[s] = count[s]
        o["clk"] = clk
    for s in SEMAPHORES:
        if count.get(s, 0) > known["Y"].get(s, 0):
            g.sync.wait_ge(T.sem[s], count[s])
    g.wait_ge(T.sem.ls, 4 * 9)
